import numpy as np
import ml_dtypes


def mxq(x, axis, fmt="e4m3"):
    dtype, down = {"e4m3": (ml_dtypes.float8_e4m3fn, 7), "e5m2": (ml_dtypes.float8_e5m2, 14)}[fmt]
    v = np.moveaxis(np.asarray(x, np.float32).astype(ml_dtypes.bfloat16).astype(np.float64), axis, -1)
    blocks = v.reshape(v.shape[:-1] + (-1, 32))
    amax = np.abs(blocks).max(-1, keepdims=True)
    byte = np.maximum(np.where(amax > 0, np.frexp(amax)[1] - 1 + 127, 0) - down, 1)
    scale = np.exp2(byte - 127.0)
    codes = (blocks / scale).astype(np.float32).astype(dtype).astype(np.float64)
    return np.moveaxis((codes * scale).reshape(v.shape), -1, axis)


WIDE = False


def mx_kscale(k):
    if not WIDE:
        return np.ones(k)
    levels = np.array([10, -10, 5, -5, 0])
    if k % 512:
        return np.exp2(np.random.permutation(np.resize(levels, k // 32))).repeat(32)
    a = np.empty((k // 512, 16))
    for p in range(k // 512):
        a[p, :8] = np.random.permutation(np.resize(levels, 8))
        for g in range(8):
            far = levels[np.abs(levels - a[p, g]) >= 10]
            a[p, g + 8] = far[np.random.randint(len(far))]
    return np.exp2(a.ravel()).repeat(32)


def f64(x):
    return np.asarray(x).astype(np.float64)


def striped(idx):
    return np.tile(idx.reshape(-1, 16).T, (8, 1)).astype(np.uint16)


def unstriped(offs):
    return offs[:16].T.reshape(-1).astype(np.int64)


K, T, E, C, N = 2560, 768, 4, 128, 512
M = 512


def by_expert(wq, xq):
    return np.concatenate([wq[e].T @ xq[:, e * C:(e + 1) * C] for e in range(E)], axis=1)


def setup_inputs():
    n = np.random.standard_normal
    s = mx_kscale(K)[:, None]
    v = mx_kscale(N)
    return {
        "xT": (n((K, T)) * s).astype(np.float32),
        "w": (n((E, K, N)) / np.sqrt(K) / s[None] * v[None, None, :]).astype(np.float32),
        "b": (0.3 * n((N, E)) * v[:, None]).astype(np.float32),
        "wp": (n((N, M)) / np.sqrt(N) / v[:, None]).astype(np.float32),
        "gate": np.tile(np.random.uniform(0.2, 1.0, E * C), (N, 1)).astype(np.float32),
        "offs": striped(np.random.permutation(T)[:E * C]),
    }


def reference(xT, w, b, wp, gate, offs):
    idx = unstriped(offs)
    xq = mxq(f64(xT)[:, idx], 0, "e4m3")
    y = by_expert(mxq(f64(w), 1, "e4m3"), xq)
    y = y + np.repeat(f64(b), C, axis=1)
    c = np.zeros((N, T))
    c[:, idx] = f64(gate) * y
    return mxq(f64(wp), 0, "e4m3").T @ mxq(c, 0, "e4m3")

@@ -1,0 +1,299 @@
+from contextlib import ExitStack
+
+import concourse.mybir as mybir
+
+K, T, E, C, N, M = 2560, 768, 4, 128, 512, 512
+
+FLOPS = 2 * E * C * K * N + 2 * E * C * N * M
+
+F32 = mybir.dt.float32
+BF16 = mybir.dt.bfloat16
+U32 = mybir.dt.uint32
+I32 = mybir.dt.int32
+U16 = mybir.dt.uint16
+U8 = mybir.dt.uint8
+FP8X4 = mybir.dt.float8_e4m3fn_x4
+
+MULT = mybir.AluOpType.mult
+IDENTITY = mybir.ActivationFunctionType.Identity
+
+P = 128
+PACK = 4
+K_PASS = P * PACK
+PASSES = K // K_PASS
+SLOTS = E * C
+TOKENS_A = 512
+LOOKAHEAD = 8
+X_BUFS = 3
+G_BUFS = 6
+Q_BUFS = 5
+X_TAIL = "svsvs"
+GROUP_START = {0: 1, 1: 1, 2: 1, 3: 1, 4: 1}
+GROUP_END = {0: 1, 1: 1, 2: 1, 3: 1, 4: 1}
+SHARES = {
+    0: ((0, 128, "s", 0, 4),),
+    1: ((0, 64, "s", 0, 4), (64, 128, "s", 0, 4)),
+    2: ((0, 128, "v", 0, 2), (0, 128, "s", 2, 4)),
+    3: ((0, 32, "s", 0, 4), (32, 64, "s", 0, 4), (64, 96, "s", 0, 4), (96, 128, "s", 0, 4)),
+    4: ((0, 128, "v", 0, 4),),
+    5: ((0, 128, "v", 0, 2), (0, 64, "s", 2, 4), (64, 128, "s", 2, 4)),
+    6: ((0, 64, "v", 0, 4), (64, 96, "s", 0, 4), (96, 128, "s", 0, 4)),
+    7: ((0, 32, "v", 0, 4), (32, 64, "s", 0, 4), (64, 96, "s", 0, 4), (96, 128, "s", 0, 4)),
+}
+LAST_SHARES = ((0, 64, "s", 0, 4), (64, 128, "v", 0, 2), (64, 128, "s", 2, 4))
+WP_COPY = ((0, 512, "v"),)
+WP_AT = 2
+SC_LAG = (2, 2, 2, 0)
+EP_LAG = (0, 0, 0, 0)
+SC_STEP = 2
+W_SPLIT = (6, 2, 3, 5, 2, 2, 6, 7, 3, 2, 2, 5, 6, 0, 0, 2, 2, 2, 1, 2)
+
+
+def tile_moe_nxt_lin_bias_kernel(tc, xT, w, b, wp, gate, offs, out):
+    nc = tc.nc
+    w_rows = w.rearrange("e k n -> (e k) n")
+
+    with ExitStack() as ctx:
+        held = ctx.enter_context(tc.tile_pool(name="held", bufs=1))
+        x_in = ctx.enter_context(tc.tile_pool(name="x_in", bufs=X_BUFS))
+        w_in = ctx.enter_context(tc.tile_pool(name="w_in", bufs=LOOKAHEAD))
+        mid = ctx.enter_context(tc.tile_pool(name="mid", bufs=2))
+        w_mid = ctx.enter_context(tc.tile_pool(name="w_mid", bufs=G_BUFS))
+        w_q = ctx.enter_context(tc.tile_pool(name="w_q", bufs=Q_BUFS))
+        o_pool = ctx.enter_context(tc.tile_pool(name="o_pool", bufs=4))
+        acc_pool = ctx.enter_context(tc.psum_pool(name="acc_pool", bufs=6))
+        proj_pool = ctx.enter_context(tc.psum_pool(name="proj_pool", bufs=2))
+
+        offsets = held.tile([P, SLOTS // 16], U16, name="offsets")
+        nc.sync.dma_start(offsets[:], offs)
+
+        gate_sb = held.tile([P, SLOTS], F32, name="gate_sb")
+        bias_sb = held.tile([P, PACK, E], F32, name="bias_sb")
+
+        x_codes = [held.tile([P, T], U32, name=f"x_codes{a}", align_bytes=64) for a in range(PASSES)]
+        x_planes = [held.tile([P, T], U8, name=f"x_planes{i}", align_bytes=64) for i in range(2)]
+        s_codes = [held.tile([P, SLOTS], U32, name=f"s_codes{a}", align_bytes=64) for a in range(PASSES)]
+        s_planes = [held.tile([P, SLOTS], U8, name=f"s_planes{i}", align_bytes=64) for i in range(2)]
+        wp_codes = held.tile([P, M], U32, name="wp_codes", align_bytes=64)
+        wp_scales = held.tile([P, M], U8, name="wp_scales", align_bytes=64)
+        out_sb = [held.tile([P, T], F32, name=f"out_sb{f}") for f in range(M // P)]
+        x_raw = {}
+        wp_raw = held.tile([P, PACK, M], F32, name="wp_raw")
+
+        for plane in x_planes:
+            nc.gpsimd.memset(plane[:], 0)
+        for f in range(M // P):
+            nc.gpsimd.memset(out_sb[f][:], 0.0)
+
+        units = [("x", a) for a in range(PASSES)] + [("w", u) for u in range(E * PASSES)]
+        units.insert(PASSES + WP_AT, ("p", 0))
+        last = ("w", E * PASSES - 1)
+        w_raw, w_half, w_code, acc = {}, {}, {}, {}
+
+        def load(unit):
+            kind, i = unit
+            if kind == "x":
+                x_raw[i] = x_in.tile([P, PACK, T], F32, name="x_in_tile")
+                src = xT[i * K_PASS : (i + 1) * K_PASS, :].rearrange("(p j) t -> p j t", j=PACK)
+                if i == 0:
+                    for lo, hi in ((0, 256), (256, 512), (512, T)):
+                        nc.sync.dma_start(x_raw[0][:, :, lo:hi], src[:, :, lo:hi])
+                    nc.sync.dma_start(bias_sb[:], b.rearrange("(p t) e -> p t e", t=PACK))
+                else:
+                    nc.sync.dma_start(x_raw[i][:], src)
+            elif kind == "p":
+                nc.sync.dma_start(wp_raw[:], wp.rearrange("(p j) f -> p j f", j=PACK))
+                nc.sync.dma_start(gate_sb[:], gate[0:P, :])
+            else:
+                raw = w_in.tile([P, PACK, N], F32, name="raw")
+                src = w_rows[i * K_PASS : (i + 1) * K_PASS, :].rearrange("(p j) n -> p j n", j=PACK)
+                if unit == last:
+                    for h in range(2):
+                        nc.sync.dma_start(raw[:, :, 256 * h : 256 * h + 256], src[:, :, 256 * h : 256 * h + 256])
+                else:
+                    nc.sync.dma_start(raw[:], src)
+                w_raw[i] = raw
+
+        def copy(unit):
+            kind, i = unit
+            if kind == "x":
+                ga = mid.tile([P, TOKENS_A, PACK], BF16, name="ga", align_bytes=64)
+                gb = mid.tile([P, T - TOKENS_A, PACK], BF16, name="gb", align_bytes=64)
+                ga_parts = ((0, 256), (256, TOKENS_A)) if i == 0 else ((0, TOKENS_A),)
+                parts = [(ga[:, lo:hi, :], lo, hi, "v" if i == 0 and lo == 0 and X_TAIL[0] == "v" else "s") for lo, hi in ga_parts]
+                parts.append((gb[:], TOKENS_A, T, X_TAIL[i]))
+                for tile, lo, hi, eng in parts:
+                    dst = tile.rearrange("p (c i) j -> p c j i", i=4)
+                    src = x_raw[i][:, :, lo:hi].rearrange("p j (c i) -> p c j i", i=4)
+                    if eng == "s":
+                        nc.scalar.copy(dst, src)
+                    else:
+                        nc.vector.tensor_copy(dst, src)
+                w_half[unit] = (ga, gb)
+            else:
+                if kind == "p":
+                    g = mid.tile([P, N, PACK], BF16, name="wpg", align_bytes=64)
+                    w_half[unit] = (g,)
+                    for lo, hi, eng in WP_COPY:
+                        dst = g[:, lo:hi, :].rearrange("p (c i) j -> p c j i", i=4)
+                        src = wp_raw[:, :, lo:hi].rearrange("p j (c i) -> p c j i", i=4)
+                        if eng == "v":
+                            nc.vector.tensor_copy(dst, src)
+                        else:
+                            nc.scalar.copy(dst, src)
+                else:
+                    e, a = divmod(i, PASSES)
+                    if a in GROUP_START:
+                        w_half[i] = w_mid.tile([P, GROUP_START[a], N, PACK], BF16, name="g", align_bytes=64)
+                    else:
+                        w_half[i] = w_half[i - 1]
+                    g = w_half[i][:, 0 if a in GROUP_START else 1, :, :]
+                    for lo, hi, eng, t0, t1 in LAST_SHARES if unit == last else SHARES[W_SPLIT[i]]:
+                        if True:
+                            dst = g[:, t0 * P : t1 * P, :].rearrange("p (t m) j -> p m j t", m=P)[:, lo:hi, :, :]
+                            src = w_raw[i][:].rearrange("p j (m t) -> p m j t", t=4)[:, lo:hi, :, t0:t1]
+                            if eng == "v":
+                                nc.vector.tensor_copy(dst, src)
+                            else:
+                                nc.scalar.copy(dst, src)
+
+        def quantize(unit):
+            kind, i = unit
+            if kind == "x":
+                codes, scales = x_codes[i], x_planes[i // 4][4 * (i % 4) : P, :]
+                tiles = w_half[unit]
+                cols = ((0, TOKENS_A, tiles[0][:]), (TOKENS_A, T, tiles[1][:]))
+            elif kind == "p":
+                codes, scales, cols = wp_codes, wp_scales[:], ((0, M, w_half[unit][0][:]),)
+            else:
+                a = i % PASSES
+                if a in GROUP_START and GROUP_START[a] == 2:
+                    return
+                n = 1 if a in GROUP_START else 2
+                codes = w_q.tile([P, n * N], U32, name="codes", align_bytes=64)
+                plane = w_q.tile([P, n * N], U8, name="plane", align_bytes=64)
+                w_code[i] = (codes, plane, (n - 1) * N)
+                w_code[i + 1 - n] = (codes, plane, 0)
+                scales = plane[:]
+                g = w_half[i][:].rearrange("p a c j -> p (a c) j")
+                if unit == last:
+                    cols = ((0, 256, g[:, 0:256, :]), (256, 512, g[:, 256:512, :]))
+                else:
+                    cols = ((0, n * N, g),)
+            for lo, hi, src in cols:
+                nc.vector.quantize_mx(
+                    out=codes[:, lo:hi].bitcast(FP8X4),
+                    scales=scales[:, lo:hi],
+                    in_=src.rearrange("p c j -> p (c j)"),
+                )
+
+        def use(unit):
+            kind, i = unit
+            if kind == "x":
+                nc.vector.tensor_copy(s_codes[i][:], x_codes[i][:].indirect(offsets[:]))
+                if i == 3 or i == 4:
+                    nc.vector.tensor_copy(s_planes[i // 4][:], x_planes[i // 4][:].indirect(offsets[:]))
+            elif kind == "w":
+                e, a = divmod(i, PASSES)
+                if a == 0:
+                    acc[e] = [acc_pool.tile([P, C], F32, name="acc_t") for t in range(PACK)]
+                codes, scales, base = w_code[i]
+                slots = slice(e * C, (e + 1) * C)
+                for t in range(PACK):
+                    cols = slice(base + t * P, base + (t + 1) * P)
+                    nc.tensor.matmul_mx(
+                        out=acc[e][t][:],
+                        lhsT=codes[:, cols].bitcast(FP8X4),
+                        lhsT_scale=scales[:, cols],
+                        rhs=s_codes[a][:, slots].bitcast(FP8X4),
+                        rhs_scale=s_planes[a // 4][4 * (a % 4) : P, slots],
+                        start=(a == 0),
+                        stop=(a == PASSES - 1),
+                    )
+
+        def finish(e):
+            slots = slice(e * C, (e + 1) * C)
+            y = mid.tile([P, PACK, C], F32, name="y")
+            c_grouped = mid.tile([P, C, PACK], BF16, name="c_grouped", align_bytes=64)
+            c_codes = mid.tile([P, C], U32, name="c_codes", align_bytes=64)
+            c_scales = mid.tile([P, C], U8, name="c_scales", align_bytes=64)
+            o_sb = o_pool.tile([P, M // P, C], F32, name="o_sb")
+            proj = proj_pool.tile([P, M // P, C], F32, name="proj")
+
+            def bias():
+                for t in range(PACK):
+                    if e == E - 1 and t % 2 == 1:
+                        nc.vector.tensor_scalar_add(y[:, t, :], acc[e][t][:], bias_sb[:, t, e : e + 1])
+                    else:
+                        nc.scalar.activation(y[:, t, :], acc[e][t][:], IDENTITY, bias=bias_sb[:, t, e : e + 1])
+
+            def gated():
+                nc.vector.tensor_tensor(
+                    c_grouped[:],
+                    y[:].rearrange("p t j -> p j t"),
+                    gate_sb[:, slots].unsqueeze(2).to_broadcast([P, C, PACK]),
+                    MULT,
+                )
+
+            def quant():
+                nc.vector.quantize_mx(
+                    out=c_codes[:].bitcast(FP8X4), scales=c_scales[:], in_=c_grouped[:].rearrange("p c j -> p (c j)")
+                )
+
+            def project():
+                for f in range(M // P):
+                    cols = slice(f * P, (f + 1) * P)
+                    nc.tensor.matmul_mx(
+                        out=proj[:, f, :],
+                        lhsT=wp_codes[:, cols].bitcast(FP8X4),
+                        lhsT_scale=wp_scales[:, cols],
+                        rhs=c_codes[:].bitcast(FP8X4),
+                        rhs_scale=c_scales[:],
+                        start=True,
+                        stop=True,
+                    )
+
+            def leave():
+                if e == E - 1:
+                    for f in range(M // P):
+                        nc.scalar.copy(o_sb[:, f, :], proj[:, f, :])
+                else:
+                    nc.scalar.copy(o_sb[:], proj[:])
+
+            def scatter(f):
+                nc.vector.tensor_copy(out_sb[f][:].indirect(offsets[:, e * C // 16 : (e + 1) * C // 16]), o_sb[:, f, :])
+                if e == E - 1:
+                    nc.sync.dma_start(out[f * P : (f + 1) * P, :], out_sb[f][:])
+
+            return bias, gated, quant, project, leave, scatter
+
+        loaded = 0
+        while loaded < X_BUFS:
+            load(units[loaded])
+            loaded += 1
+        pending = []
+        for s in range(len(units) + 1):
+            while pending and pending[0][0] <= s:
+                pending.pop(0)[1]()
+            if s >= 2 and units[s - 2][0] == "x":
+                use(units[s - 2])
+            if s >= 1:
+                kind, i = units[s - 1]
+                quantize(units[s - 1])
+                if kind == "w" and i % PASSES in GROUP_END:
+                    for u in range(i + 1 - GROUP_END[i % PASSES], i + 1):
+                        use(("w", u))
+                    if i % PASSES == PASSES - 1:
+                        bias, gated, quant, project, leave, scatter = finish(i // PASSES)
+                        bias()
+                        e = i // PASSES
+                        pending += [(s + EP_LAG[e], step) for step in (gated, quant, project, leave)]
+                        pending += [(s + SC_LAG[e] + f // SC_STEP, lambda f=f, scatter=scatter: scatter(f)) for f in range(M // P)]
+                        pending = sorted(pending, key=lambda x: x[0])
+            if s < len(units):
+                copy(units[s])
+            while loaded < len(units) and loaded <= s + (X_BUFS if units[loaded][0] == "x" else LOOKAHEAD):
+                load(units[loaded])
+                loaded += 1
+        for _, task in pending:
+            task()

@@ -1,6 +1,7 @@
 from contextlib import ExitStack
 
 import concourse.mybir as mybir
+from concourse.masks import make_identity
 
 K, T, E, C, N, M = 2560, 768, 4, 128, 512, 512
 
@@ -15,38 +16,23 @@ U8 = mybir.dt.uint8
 FP8X4 = mybir.dt.float8_e4m3fn_x4
 
 MULT = mybir.AluOpType.mult
-IDENTITY = mybir.ActivationFunctionType.Identity
+ADD = mybir.AluOpType.add
+COPY = mybir.ActivationFunctionType.Copy
 
 P = 128
 PACK = 4
 K_PASS = P * PACK
 PASSES = K // K_PASS
 SLOTS = E * C
-TOKENS_A = 512
-LOOKAHEAD = 8
+RUN = 4
+HALF = 256
+BEFORE_LEAVE = 160
+W_BUFS = 9
 X_BUFS = 3
-G_BUFS = 6
-Q_BUFS = 5
-X_TAIL = "svsvs"
-GROUP_START = {0: 1, 1: 1, 2: 1, 3: 1, 4: 1}
-GROUP_END = {0: 1, 1: 1, 2: 1, 3: 1, 4: 1}
-SHARES = {
-    0: ((0, 128, "s", 0, 4),),
-    1: ((0, 64, "s", 0, 4), (64, 128, "s", 0, 4)),
-    2: ((0, 128, "v", 0, 2), (0, 128, "s", 2, 4)),
-    3: ((0, 32, "s", 0, 4), (32, 64, "s", 0, 4), (64, 96, "s", 0, 4), (96, 128, "s", 0, 4)),
-    4: ((0, 128, "v", 0, 4),),
-    5: ((0, 128, "v", 0, 2), (0, 64, "s", 2, 4), (64, 128, "s", 2, 4)),
-    6: ((0, 64, "v", 0, 4), (64, 96, "s", 0, 4), (96, 128, "s", 0, 4)),
-    7: ((0, 32, "v", 0, 4), (32, 64, "s", 0, 4), (64, 96, "s", 0, 4), (96, 128, "s", 0, 4)),
-}
-LAST_SHARES = ((0, 64, "s", 0, 4), (64, 128, "v", 0, 2), (64, 128, "s", 2, 4))
-WP_COPY = ((0, 512, "v"),)
-WP_AT = 2
-SC_LAG = (2, 2, 2, 0)
-EP_LAG = (0, 0, 0, 0)
-SC_STEP = 2
-W_SPLIT = (6, 2, 3, 5, 2, 2, 6, 7, 3, 2, 2, 5, 6, 0, 0, 2, 2, 2, 1, 2)
+W_ON_VECTOR = (256, 256, 0, 128, 192)
+LAST_LOADS = ((0, 384), (384, 512))
+LAST_GROUPS = ((0, 256), (256, 384), (384, 512))
+LAST_SHARES = ((0, 224, "v"), (224, 384, "s"), (384, 448, "v"), (448, 512, "s"))
 
 
 def tile_moe_nxt_lin_bias_kernel(tc, xT, w, b, wp, gate, offs, out):
@@ -56,195 +42,165 @@ def tile_moe_nxt_lin_bias_kernel(tc, xT, w, b, wp, gate, offs, out):
     with ExitStack() as ctx:
         held = ctx.enter_context(tc.tile_pool(name="held", bufs=1))
         x_in = ctx.enter_context(tc.tile_pool(name="x_in", bufs=X_BUFS))
-        w_in = ctx.enter_context(tc.tile_pool(name="w_in", bufs=LOOKAHEAD))
+        w_in = ctx.enter_context(tc.tile_pool(name="w_in", bufs=W_BUFS))
         mid = ctx.enter_context(tc.tile_pool(name="mid", bufs=2))
-        w_mid = ctx.enter_context(tc.tile_pool(name="w_mid", bufs=G_BUFS))
-        w_q = ctx.enter_context(tc.tile_pool(name="w_q", bufs=Q_BUFS))
-        o_pool = ctx.enter_context(tc.tile_pool(name="o_pool", bufs=4))
-        acc_pool = ctx.enter_context(tc.psum_pool(name="acc_pool", bufs=6))
-        proj_pool = ctx.enter_context(tc.psum_pool(name="proj_pool", bufs=2))
+        w_mid = ctx.enter_context(tc.tile_pool(name="w_mid", bufs=5))
+        w_q = ctx.enter_context(tc.tile_pool(name="w_q", bufs=7))
+        banks2 = ctx.enter_context(tc.psum_pool(name="banks2", bufs=2))
+        banks1 = ctx.enter_context(tc.psum_pool(name="banks1", bufs=1))
 
         offsets = held.tile([P, SLOTS // 16], U16, name="offsets")
-        nc.sync.dma_start(offsets[:], offs)
-
-        gate_sb = held.tile([P, SLOTS], F32, name="gate_sb")
+        ident = held.tile([P, P], F32, name="ident")
+        gate_rows = held.tile([P, C], F32, name="gate_rows")
+        gate_col = held.tile([P, E], F32, name="gate_col")
         bias_sb = held.tile([P, PACK, E], F32, name="bias_sb")
-
-        x_codes = [held.tile([P, T], U32, name=f"x_codes{a}", align_bytes=64) for a in range(PASSES)]
+        gated_bias = [held.tile([P, N], F32, name=f"gated_bias{e}") for e in range(E)]
         x_planes = [held.tile([P, T], U8, name=f"x_planes{i}", align_bytes=64) for i in range(2)]
         s_codes = [held.tile([P, SLOTS], U32, name=f"s_codes{a}", align_bytes=64) for a in range(PASSES)]
         s_planes = [held.tile([P, SLOTS], U8, name=f"s_planes{i}", align_bytes=64) for i in range(2)]
         wp_codes = held.tile([P, M], U32, name="wp_codes", align_bytes=64)
         wp_scales = held.tile([P, M], U8, name="wp_scales", align_bytes=64)
         out_sb = [held.tile([P, T], F32, name=f"out_sb{f}") for f in range(M // P)]
-        x_raw = {}
-        wp_raw = held.tile([P, PACK, M], F32, name="wp_raw")
 
-        for plane in x_planes:
-            nc.gpsimd.memset(plane[:], 0)
-        for f in range(M // P):
-            nc.gpsimd.memset(out_sb[f][:], 0.0)
+        units = [("w", 0)] + [("x", a) for a in range(PASSES)] + [("w", u) for u in range(1, PASSES - 1)]
+        units += [("p", 0)] + [("w", u) for u in range(PASSES - 1, E * PASSES)]
+        last = units[-1]
+        raw, grouped, coded, acc = {}, {}, {}, {}
 
-        units = [("x", a) for a in range(PASSES)] + [("w", u) for u in range(E * PASSES)]
-        units.insert(PASSES + WP_AT, ("p", 0))
-        last = ("w", E * PASSES - 1)
-        w_raw, w_half, w_code, acc = {}, {}, {}, {}
+        def rows_of(unit):
+            kind, i = unit
+            src = {"x": xT, "w": w_rows, "p": wp}[kind]
+            return src[i * K_PASS : (i + 1) * K_PASS, :].rearrange("(p j) c -> p j c", j=PACK)
 
         def load(unit):
-            kind, i = unit
-            if kind == "x":
-                x_raw[i] = x_in.tile([P, PACK, T], F32, name="x_in_tile")
-                src = xT[i * K_PASS : (i + 1) * K_PASS, :].rearrange("(p j) t -> p j t", j=PACK)
-                if i == 0:
-                    for lo, hi in ((0, 256), (256, 512), (512, T)):
-                        nc.sync.dma_start(x_raw[0][:, :, lo:hi], src[:, :, lo:hi])
-                    nc.sync.dma_start(bias_sb[:], b.rearrange("(p t) e -> p t e", t=PACK))
+            width = T if unit[0] == "x" else N
+            raw[unit] = []
+            for lo, hi in LAST_LOADS if unit == last else ((0, width),):
+                if unit[0] == "x":
+                    tile = x_in.tile([P, PACK, hi - lo], F32, name="x_raw")
                 else:
-                    nc.sync.dma_start(x_raw[i][:], src)
-            elif kind == "p":
-                nc.sync.dma_start(wp_raw[:], wp.rearrange("(p j) f -> p j f", j=PACK))
-                nc.sync.dma_start(gate_sb[:], gate[0:P, :])
-            else:
-                raw = w_in.tile([P, PACK, N], F32, name="raw")
-                src = w_rows[i * K_PASS : (i + 1) * K_PASS, :].rearrange("(p j) n -> p j n", j=PACK)
-                if unit == last:
-                    for h in range(2):
-                        nc.sync.dma_start(raw[:, :, 256 * h : 256 * h + 256], src[:, :, 256 * h : 256 * h + 256])
-                else:
-                    nc.sync.dma_start(raw[:], src)
-                w_raw[i] = raw
+                    tile = w_in.tile([P, PACK, hi - lo], F32, name="w_raw")
+                nc.sync.dma_start(tile[:], rows_of(unit)[:, :, lo:hi])
+                raw[unit].append((lo, hi, tile))
 
-        def copy(unit):
+        def shares(unit):
             kind, i = unit
+            if unit == last:
+                return LAST_SHARES
             if kind == "x":
-                ga = mid.tile([P, TOKENS_A, PACK], BF16, name="ga", align_bytes=64)
-                gb = mid.tile([P, T - TOKENS_A, PACK], BF16, name="gb", align_bytes=64)
-                ga_parts = ((0, 256), (256, TOKENS_A)) if i == 0 else ((0, TOKENS_A),)
-                parts = [(ga[:, lo:hi, :], lo, hi, "v" if i == 0 and lo == 0 and X_TAIL[0] == "v" else "s") for lo, hi in ga_parts]
-                parts.append((gb[:], TOKENS_A, T, X_TAIL[i]))
-                for tile, lo, hi, eng in parts:
-                    dst = tile.rearrange("p (c i) j -> p c j i", i=4)
-                    src = x_raw[i][:, :, lo:hi].rearrange("p j (c i) -> p c j i", i=4)
-                    if eng == "s":
-                        nc.scalar.copy(dst, src)
-                    else:
-                        nc.vector.tensor_copy(dst, src)
-                w_half[unit] = (ga, gb)
+                return ((0, HALF, "s"), (HALF, 2 * HALF, "s"), (2 * HALF, T, "v"))
+            if unit == units[0]:
+                return ((0, N, "v"),)
+            on_vector = HALF if kind == "p" else HALF if i < PASSES else W_ON_VECTOR[i % PASSES]
+            if kind == "w" and i > PASSES and i % PASSES == 1:
+                return ((N - on_vector, N, "v"), (0, BEFORE_LEAVE, "s"), (BEFORE_LEAVE, N - on_vector, "s"))
+            if kind == "w" and i >= PASSES and i % PASSES == 0:
+                mid_col = N - on_vector // 2
+                return ((mid_col, N, "v"), (0, N - on_vector, "s"), (N - on_vector, mid_col, "v"))
+            if on_vector:
+                return ((0, N - on_vector, "s"), (N - on_vector, N, "v"))
+            return ((0, HALF, "s"), (HALF, N, "s"))
+
+        def copy(unit, between=None):
+            if unit[0] == "x":
+                g = mid.tile([P, T, PACK], BF16, name="x_grouped", align_bytes=64)
             else:
-                if kind == "p":
-                    g = mid.tile([P, N, PACK], BF16, name="wpg", align_bytes=64)
-                    w_half[unit] = (g,)
-                    for lo, hi, eng in WP_COPY:
-                        dst = g[:, lo:hi, :].rearrange("p (c i) j -> p c j i", i=4)
-                        src = wp_raw[:, :, lo:hi].rearrange("p j (c i) -> p c j i", i=4)
-                        if eng == "v":
-                            nc.vector.tensor_copy(dst, src)
-                        else:
-                            nc.scalar.copy(dst, src)
+                g = w_mid.tile([P, N, PACK], BF16, name="w_grouped", align_bytes=64)
+            grouped[unit] = g
+            for n, (lo, hi, eng) in enumerate(shares(unit)):
+                if between and n == 2:
+                    between()
+                base, tile = [(a, t) for a, z, t in raw[unit] if a <= lo and hi <= z][0]
+                dst = g[:, lo:hi, :].rearrange("p (c i) j -> p c j i", i=RUN)
+                src = tile[:, :, lo - base : hi - base].rearrange("p j (c i) -> p c j i", i=RUN)
+                if eng == "v":
+                    nc.vector.tensor_copy(dst, src)
                 else:
-                    e, a = divmod(i, PASSES)
-                    if a in GROUP_START:
-                        w_half[i] = w_mid.tile([P, GROUP_START[a], N, PACK], BF16, name="g", align_bytes=64)
-                    else:
-                        w_half[i] = w_half[i - 1]
-                    g = w_half[i][:, 0 if a in GROUP_START else 1, :, :]
-                    for lo, hi, eng, t0, t1 in LAST_SHARES if unit == last else SHARES[W_SPLIT[i]]:
-                        if True:
-                            dst = g[:, t0 * P : t1 * P, :].rearrange("p (t m) j -> p m j t", m=P)[:, lo:hi, :, :]
-                            src = w_raw[i][:].rearrange("p j (m t) -> p m j t", t=4)[:, lo:hi, :, t0:t1]
-                            if eng == "v":
-                                nc.vector.tensor_copy(dst, src)
-                            else:
-                                nc.scalar.copy(dst, src)
+                    nc.scalar.copy(dst, src)
+
+        def quantize_cols(codes, scales, g, lo, hi):
+            nc.vector.quantize_mx(
+                out=codes[:, lo:hi].bitcast(FP8X4),
+                scales=scales[:, lo:hi],
+                in_=g[:, lo:hi, :].rearrange("p c j -> p (c j)"),
+            )
 
         def quantize(unit):
             kind, i = unit
             if kind == "x":
-                codes, scales = x_codes[i], x_planes[i // 4][4 * (i % 4) : P, :]
-                tiles = w_half[unit]
-                cols = ((0, TOKENS_A, tiles[0][:]), (TOKENS_A, T, tiles[1][:]))
+                codes = mid.tile([P, T], U32, name="x_codes", align_bytes=64)
+                coded[unit] = codes
+                for lo, hi in ((0, 2 * HALF), (2 * HALF, T)):
+                    quantize_cols(codes, x_planes[i // 4][4 * (i % 4) : P, :], grouped[unit], lo, hi)
             elif kind == "p":
-                codes, scales, cols = wp_codes, wp_scales[:], ((0, M, w_half[unit][0][:]),)
+                quantize_cols(wp_codes, wp_scales, grouped[unit], 0, M)
             else:
-                a = i % PASSES
-                if a in GROUP_START and GROUP_START[a] == 2:
-                    return
-                n = 1 if a in GROUP_START else 2
-                codes = w_q.tile([P, n * N], U32, name="codes", align_bytes=64)
-                plane = w_q.tile([P, n * N], U8, name="plane", align_bytes=64)
-                w_code[i] = (codes, plane, (n - 1) * N)
-                w_code[i + 1 - n] = (codes, plane, 0)
-                scales = plane[:]
-                g = w_half[i][:].rearrange("p a c j -> p (a c) j")
-                if unit == last:
-                    cols = ((0, 256, g[:, 0:256, :]), (256, 512, g[:, 256:512, :]))
-                else:
-                    cols = ((0, n * N, g),)
-            for lo, hi, src in cols:
-                nc.vector.quantize_mx(
-                    out=codes[:, lo:hi].bitcast(FP8X4),
-                    scales=scales[:, lo:hi],
-                    in_=src.rearrange("p c j -> p (c j)"),
+                codes = w_q.tile([P, N], U32, name="w_codes", align_bytes=64)
+                plane = w_q.tile([P, N], U8, name="w_plane", align_bytes=64)
+                coded[unit] = (codes, plane)
+                for lo, hi in LAST_GROUPS if unit == last else ((0, N),):
+                    quantize_cols(codes, plane, grouped[unit], lo, hi)
+
+        def gather(a):
+            nc.vector.tensor_copy(s_codes[a][:], coded[("x", a)][:].indirect(offsets[:]))
+            if a >= PASSES - 2:
+                nc.vector.tensor_copy(s_planes[a // 4][:], x_planes[a // 4][:].indirect(offsets[:]))
+
+        def groups_of(e):
+            return LAST_GROUPS if e == E - 1 else ((0, N),)
+
+        def multiply(u):
+            e, a = divmod(u, PASSES)
+            if a == 0:
+                acc[e] = [banks2.tile([P, groups_of(e)[0][1]], F32, name="acc")]
+                acc[e] += [banks1.tile([P, hi - lo], F32, name=f"bank{k}") for k, (lo, hi) in enumerate(groups_of(e)[1:])]
+            codes, plane = coded[("w", u)]
+            slots = slice(e * C, (e + 1) * C)
+            for bank, (lo, hi) in zip(acc[e], groups_of(e)):
+                nc.tensor.matmul_mx(
+                    out=bank[:],
+                    lhsT=s_codes[a][:, slots].bitcast(FP8X4),
+                    lhsT_scale=s_planes[a // 4][4 * (a % 4) : P, slots],
+                    rhs=codes[:, lo:hi].bitcast(FP8X4),
+                    rhs_scale=plane[:, lo:hi],
+                    start=(a == 0),
+                    stop=(a == PASSES - 1),
                 )
 
-        def use(unit):
-            kind, i = unit
-            if kind == "x":
-                nc.vector.tensor_copy(s_codes[i][:], x_codes[i][:].indirect(offsets[:]))
-                if i == 3 or i == 4:
-                    nc.vector.tensor_copy(s_planes[i // 4][:], x_planes[i // 4][:].indirect(offsets[:]))
-            elif kind == "w":
-                e, a = divmod(i, PASSES)
-                if a == 0:
-                    acc[e] = [acc_pool.tile([P, C], F32, name="acc_t") for t in range(PACK)]
-                codes, scales, base = w_code[i]
-                slots = slice(e * C, (e + 1) * C)
-                for t in range(PACK):
-                    cols = slice(base + t * P, base + (t + 1) * P)
-                    nc.tensor.matmul_mx(
-                        out=acc[e][t][:],
-                        lhsT=codes[:, cols].bitcast(FP8X4),
-                        lhsT_scale=scales[:, cols],
-                        rhs=s_codes[a][:, slots].bitcast(FP8X4),
-                        rhs_scale=s_planes[a // 4][4 * (a % 4) : P, slots],
-                        start=(a == 0),
-                        stop=(a == PASSES - 1),
-                    )
-
         def finish(e):
-            slots = slice(e * C, (e + 1) * C)
-            y = mid.tile([P, PACK, C], F32, name="y")
+            c_rows = mid.tile([P, N], BF16, name="c_rows", align_bytes=64)
             c_grouped = mid.tile([P, C, PACK], BF16, name="c_grouped", align_bytes=64)
             c_codes = mid.tile([P, C], U32, name="c_codes", align_bytes=64)
             c_scales = mid.tile([P, C], U8, name="c_scales", align_bytes=64)
-            o_sb = o_pool.tile([P, M // P, C], F32, name="o_sb")
-            proj = proj_pool.tile([P, M // P, C], F32, name="proj")
-
-            def bias():
-                for t in range(PACK):
-                    if e == E - 1 and t % 2 == 1:
-                        nc.vector.tensor_scalar_add(y[:, t, :], acc[e][t][:], bias_sb[:, t, e : e + 1])
-                    else:
-                        nc.scalar.activation(y[:, t, :], acc[e][t][:], IDENTITY, bias=bias_sb[:, t, e : e + 1])
+            turned = banks2.tile([P, 2, C], F32, name="turned")
+            projected = []
+            o_first = mid.tile([P, C], F32, name="o_first")
+            o_rest = mid.tile([P, M // P - 1, C], F32, name="o_rest")
 
             def gated():
-                nc.vector.tensor_tensor(
-                    c_grouped[:],
-                    y[:].rearrange("p t j -> p j t"),
-                    gate_sb[:, slots].unsqueeze(2).to_broadcast([P, C, PACK]),
-                    MULT,
-                )
+                for bank, (lo, hi) in zip(acc[e], groups_of(e)):
+                    nc.vector.scalar_tensor_tensor(
+                        c_rows[:, lo:hi], bank[:], gate_col[:, e : e + 1], gated_bias[e][:, lo:hi], MULT, ADD
+                    )
+                words = c_rows[:].bitcast(F32)
+                for u in range(2):
+                    nc.tensor.transpose(turned[:, u, :], words[:, u : N // 2 : 2], ident[:])
 
-            def quant():
-                nc.vector.quantize_mx(
-                    out=c_codes[:].bitcast(FP8X4), scales=c_scales[:], in_=c_grouped[:].rearrange("p c j -> p (c j)")
+            def regroup():
+                nc.scalar.copy(
+                    c_grouped[:].rearrange("p s j -> p (s j)").bitcast(F32).rearrange("p (s u) -> p s u", u=2),
+                    turned[:].rearrange("p u s -> p s u"),
                 )
 
             def project():
+                quantize_cols(c_codes, c_scales, c_grouped, 0, C)
+                first = banks1.tile([P, C], F32, name="bank2")
+                rest = banks1.tile([P, M // P - 1, C], F32, name="bank3")
+                projected.extend((first, rest))
                 for f in range(M // P):
                     cols = slice(f * P, (f + 1) * P)
                     nc.tensor.matmul_mx(
-                        out=proj[:, f, :],
+                        out=first[:] if f == 0 else rest[:, f - 1, :],
                         lhsT=wp_codes[:, cols].bitcast(FP8X4),
                         lhsT_scale=wp_scales[:, cols],
                         rhs=c_codes[:].bitcast(FP8X4),
@@ -254,46 +210,84 @@ def tile_moe_nxt_lin_bias_kernel(tc, xT, w, b, wp, gate, offs, out):
                     )
 
             def leave():
-                if e == E - 1:
-                    for f in range(M // P):
-                        nc.scalar.copy(o_sb[:, f, :], proj[:, f, :])
-                else:
-                    nc.scalar.copy(o_sb[:], proj[:])
+                first, rest = projected
+                nc.scalar.copy(o_first[:], first[:])
+                nc.scalar.copy(o_rest[:], rest[:])
 
             def scatter(f):
-                nc.vector.tensor_copy(out_sb[f][:].indirect(offsets[:, e * C // 16 : (e + 1) * C // 16]), o_sb[:, f, :])
+                src = o_first[:] if f == 0 else o_rest[:, f - 1, :]
+                nc.vector.tensor_copy(out_sb[f][:].indirect(offsets[:, e * C // 16 : (e + 1) * C // 16]), src)
                 if e == E - 1:
                     nc.sync.dma_start(out[f * P : (f + 1) * P, :], out_sb[f][:])
 
-            return bias, gated, quant, project, leave, scatter
+            return gated, regroup, project, leave, scatter
 
-        loaded = 0
-        while loaded < X_BUFS:
+        load(units[0])
+        nc.gpsimd.memset(gate_rows[:], 0.0)
+        nc.sync.dma_start(gate_rows[0:E, :], gate[0:1, :].rearrange("o (e c) -> (o e) c", c=C))
+        nc.sync.dma_start(bias_sb[:], b.rearrange("(p a) e -> p a e", a=PACK))
+        nc.sync.dma_start(offsets[:], offs)
+        make_identity(nc, ident[:])
+        for plane in x_planes:
+            nc.vector.memset(plane[:].bitcast(I32), 0)
+        for f in range(M // P):
+            nc.vector.memset(out_sb[f][:], 0.0)
+
+        gate_turned = banks2.tile([P, P], F32, name="turned")
+        nc.tensor.transpose(gate_turned[:], gate_rows[:], ident[:])
+        nc.scalar.copy(gate_col[:], gate_turned[:, 0:E])
+        for e in range(E):
+            spread = banks1.tile([P, PACK, P], F32, name=f"bank{e}")
+            for a in range(PACK):
+                nc.tensor.transpose(spread[:, a, :], bias_sb[:, a, e : e + 1].to_broadcast([P, P]), ident[:])
+            nc.scalar.activation(
+                gated_bias[e][:].rearrange("q (p a) -> q p a", a=PACK),
+                spread[:].rearrange("q a p -> q p a"),
+                COPY,
+                scale=gate_col[:, e : e + 1],
+            )
+
+        def room(s, nxt):
+            ahead = [u for u in units[s + 1 : nxt + 1] if (u[0] == "x") == (units[nxt][0] == "x")]
+            return len(ahead) + (units[nxt] == last) <= (X_BUFS if units[nxt][0] == "x" else W_BUFS)
+
+        loaded = 1
+        while room(-1, loaded):
             load(units[loaded])
             loaded += 1
-        pending = []
+        gathered = 0
+        multiplied = 0
+        quantized = 0
+        steps = None
         for s in range(len(units) + 1):
-            while pending and pending[0][0] <= s:
-                pending.pop(0)[1]()
             if s >= 2 and units[s - 2][0] == "x":
-                use(units[s - 2])
+                gather(units[s - 2][1])
+                gathered = units[s - 2][1] + 1 if units[s - 2][1] >= PASSES - 2 else 0
             if s >= 1:
-                kind, i = units[s - 1]
                 quantize(units[s - 1])
-                if kind == "w" and i % PASSES in GROUP_END:
-                    for u in range(i + 1 - GROUP_END[i % PASSES], i + 1):
-                        use(("w", u))
-                    if i % PASSES == PASSES - 1:
-                        bias, gated, quant, project, leave, scatter = finish(i // PASSES)
-                        bias()
-                        e = i // PASSES
-                        pending += [(s + EP_LAG[e], step) for step in (gated, quant, project, leave)]
-                        pending += [(s + SC_LAG[e] + f // SC_STEP, lambda f=f, scatter=scatter: scatter(f)) for f in range(M // P)]
-                        pending = sorted(pending, key=lambda x: x[0])
+                if units[s - 1][0] == "w":
+                    quantized = units[s - 1][1] + 1
+            closing, steps = steps, None
+            if closing:
+                closing[2]()
+            while multiplied < quantized and multiplied % PASSES < gathered:
+                multiply(multiplied)
+                multiplied += 1
+                if multiplied % PASSES == 0:
+                    steps = finish(multiplied // PASSES - 1)
             if s < len(units):
-                copy(units[s])
-            while loaded < len(units) and loaded <= s + (X_BUFS if units[loaded][0] == "x" else LOOKAHEAD):
+                copy(units[s], closing[3] if closing else steps[0] if steps else None)
+            elif steps:
+                steps[0]()
+            if closing:
+                for f in range(M // P):
+                    closing[4](f)
+            if steps:
+                steps[1]()
+            while loaded < len(units) and room(s, loaded):
                 load(units[loaded])
                 loaded += 1
-        for _, task in pending:
-            task()
+        steps[2]()
+        steps[3]()
+        for f in range(M // P):
+            steps[4](f)

@@ -26,10 +26,13 @@ PASSES = K // K_PASS
 SLOTS = E * C
 RUN = 4
 HALF = 256
-BEFORE_LEAVE = 160
 W_BUFS = 9
 X_BUFS = 3
-W_ON_VECTOR = (256, 256, 0, 128, 192)
+AFTER_CLOSE = (((384, 512, "v"), (0, 256, "s"), (0, 0, "step"), (256, 384, "v")), ((256, 512, "v"), (0, 160, "s"), (0, 0, "step"), (160, 256, "s")), ((0, 384, "g"), (384, 512, "s")), ((0, 256, "s"), (256, 512, "s")))
+LAST_PASS = ((0, 320, "s"), (320, 512, "v"))
+ELSE = ((0, 512, "s"),)
+EARLY = ((0, 256, "s"), (256, 512, "v"))
+X_SHARES = ((0, 256, "s"), (256, 512, "s"), (512, 768, "v"))
 LAST_LOADS = ((0, 384), (384, 512))
 LAST_GROUPS = ((0, 256), (256, 384), (384, 512))
 LAST_SHARES = ((0, 224, "v"), (224, 384, "s"), (384, 448, "v"), (448, 512, "s"))
@@ -83,23 +86,22 @@ def tile_moe_nxt_lin_bias_kernel(tc, xT, w, b, wp, gate, offs, out):
                 nc.sync.dma_start(tile[:], rows_of(unit)[:, :, lo:hi])
                 raw[unit].append((lo, hi, tile))
 
+        closers = [units.index(("w", e * PASSES + PASSES - 1)) for e in range(E)]
+
         def shares(unit):
-            kind, i = unit
+            at = units.index(unit)
             if unit == last:
                 return LAST_SHARES
-            if kind == "x":
-                return ((0, HALF, "s"), (HALF, 2 * HALF, "s"), (2 * HALF, T, "v"))
-            if unit == units[0]:
+            if unit[0] == "x":
+                return X_SHARES
+            if at == 0:
                 return ((0, N, "v"),)
-            on_vector = HALF if kind == "p" else HALF if i < PASSES else W_ON_VECTOR[i % PASSES]
-            if kind == "w" and i > PASSES and i % PASSES == 1:
-                return ((N - on_vector, N, "v"), (0, BEFORE_LEAVE, "s"), (BEFORE_LEAVE, N - on_vector, "s"))
-            if kind == "w" and i >= PASSES and i % PASSES == 0:
-                mid_col = N - on_vector // 2
-                return ((mid_col, N, "v"), (0, N - on_vector, "s"), (N - on_vector, mid_col, "v"))
-            if on_vector:
-                return ((0, N - on_vector, "s"), (N - on_vector, N, "v"))
-            return ((0, HALF, "s"), (HALF, N, "s"))
+            if at <= closers[0]:
+                return EARLY
+            if at in closers:
+                return LAST_PASS
+            since = at - max(c for c in closers if c < at)
+            return AFTER_CLOSE[since - 1] if since <= len(AFTER_CLOSE) else ELSE
 
         def copy(unit, between=None):
             if unit[0] == "x":
@@ -107,14 +109,17 @@ def tile_moe_nxt_lin_bias_kernel(tc, xT, w, b, wp, gate, offs, out):
             else:
                 g = w_mid.tile([P, N, PACK], BF16, name="w_grouped", align_bytes=64)
             grouped[unit] = g
-            for n, (lo, hi, eng) in enumerate(shares(unit)):
-                if between and n == 2:
+            for lo, hi, eng in shares(unit):
+                if eng == "step":
                     between()
+                    continue
                 base, tile = [(a, t) for a, z, t in raw[unit] if a <= lo and hi <= z][0]
                 dst = g[:, lo:hi, :].rearrange("p (c i) j -> p c j i", i=RUN)
                 src = tile[:, :, lo - base : hi - base].rearrange("p j (c i) -> p c j i", i=RUN)
                 if eng == "v":
                     nc.vector.tensor_copy(dst, src)
+                elif eng == "g":
+                    nc.gpsimd.tensor_scalar(dst, src, 1.0, 0.0, MULT, ADD)
                 else:
                     nc.scalar.copy(dst, src)
 

@@ -26,16 +26,16 @@ PASSES = K // K_PASS
 SLOTS = E * C
 RUN = 4
 HALF = 256
+HELD = (0, 1, 2)
 W_BUFS = 9
-X_BUFS = 3
-AFTER_CLOSE = (((384, 512, "v"), (0, 256, "s"), (0, 0, "step"), (256, 384, "v")), ((256, 512, "v"), (0, 160, "s"), (0, 0, "step"), (160, 256, "s")), ((0, 384, "g"), (384, 512, "s")), ((0, 256, "s"), (256, 512, "s")))
-LAST_PASS = ((0, 320, "s"), (320, 512, "v"))
+AFTER_CLOSE = (((384, 512, "v"), (0, 384, "s"), (0, 0, "step")), ((0, 160, "s"), (384, 512, "v"), (0, 0, "step"), (160, 384, "s")), ((0, 320, "g"), (320, 512, "s")), ((0, 320, "s"), (320, 512, "v")))
+LAST_PASS = ((0, 256, "v"), (320, 512, "s"), (256, 320, "v"))
 ELSE = ((0, 512, "s"),)
 EARLY = ((0, 256, "s"), (256, 512, "v"))
 X_SHARES = ((0, 256, "s"), (256, 512, "s"), (512, 768, "v"))
 LAST_LOADS = ((0, 384), (384, 512))
 LAST_GROUPS = ((0, 256), (256, 384), (384, 512))
-LAST_SHARES = ((0, 224, "v"), (224, 384, "s"), (384, 448, "v"), (448, 512, "s"))
+LAST_SHARES = ((0, 256, "v"), (256, 384, "s"), (384, 448, "v"), (448, 512, "s"))
 
 
 def tile_moe_nxt_lin_bias_kernel(tc, xT, w, b, wp, gate, offs, out):
@@ -44,11 +44,11 @@ def tile_moe_nxt_lin_bias_kernel(tc, xT, w, b, wp, gate, offs, out):
 
     with ExitStack() as ctx:
         held = ctx.enter_context(tc.tile_pool(name="held", bufs=1))
-        x_in = ctx.enter_context(tc.tile_pool(name="x_in", bufs=X_BUFS))
         w_in = ctx.enter_context(tc.tile_pool(name="w_in", bufs=W_BUFS))
         mid = ctx.enter_context(tc.tile_pool(name="mid", bufs=2))
         w_mid = ctx.enter_context(tc.tile_pool(name="w_mid", bufs=5))
         w_q = ctx.enter_context(tc.tile_pool(name="w_q", bufs=7))
+        late = ctx.enter_context(tc.tile_pool(name="late", bufs=1))
         banks2 = ctx.enter_context(tc.psum_pool(name="banks2", bufs=2))
         banks1 = ctx.enter_context(tc.psum_pool(name="banks1", bufs=1))
 
@@ -57,7 +57,7 @@ def tile_moe_nxt_lin_bias_kernel(tc, xT, w, b, wp, gate, offs, out):
         gate_rows = held.tile([P, C], F32, name="gate_rows")
         gate_col = held.tile([P, E], F32, name="gate_col")
         bias_sb = held.tile([P, PACK, E], F32, name="bias_sb")
-        gated_bias = [held.tile([P, N], F32, name=f"gated_bias{e}") for e in range(E)]
+        gated_bias = [late.tile([P, N], F32, name=f"gated_bias{e}") for e in range(E)]
         x_planes = [held.tile([P, T], U8, name=f"x_planes{i}", align_bytes=64) for i in range(2)]
         s_codes = [held.tile([P, SLOTS], U32, name=f"s_codes{a}", align_bytes=64) for a in range(PASSES)]
         s_planes = [held.tile([P, SLOTS], U8, name=f"s_planes{i}", align_bytes=64) for i in range(2)]
@@ -79,10 +79,7 @@ def tile_moe_nxt_lin_bias_kernel(tc, xT, w, b, wp, gate, offs, out):
             width = T if unit[0] == "x" else N
             raw[unit] = []
             for lo, hi in LAST_LOADS if unit == last else ((0, width),):
-                if unit[0] == "x":
-                    tile = x_in.tile([P, PACK, hi - lo], F32, name="x_raw")
-                else:
-                    tile = w_in.tile([P, PACK, hi - lo], F32, name="w_raw")
+                tile = w_in.tile([P, PACK, hi - lo], F32, name="w_raw")
                 nc.sync.dma_start(tile[:], rows_of(unit)[:, :, lo:hi])
                 raw[unit].append((lo, hi, tile))
 
@@ -96,7 +93,7 @@ def tile_moe_nxt_lin_bias_kernel(tc, xT, w, b, wp, gate, offs, out):
                 return X_SHARES
             if at == 0:
                 return ((0, N, "v"),)
-            if at <= closers[0]:
+            if at < closers[0]:
                 return EARLY
             if at in closers:
                 return LAST_PASS
@@ -143,7 +140,7 @@ def tile_moe_nxt_lin_bias_kernel(tc, xT, w, b, wp, gate, offs, out):
                 codes = w_q.tile([P, N], U32, name="w_codes", align_bytes=64)
                 plane = w_q.tile([P, N], U8, name="w_plane", align_bytes=64)
                 coded[unit] = (codes, plane)
-                for lo, hi in LAST_GROUPS if unit == last else ((0, N),):
+                for lo, hi in groups_of(i // PASSES) if i % PASSES == PASSES - 1 else ((0, N),):
                     quantize_cols(codes, plane, grouped[unit], lo, hi)
 
         def gather(a):
@@ -152,7 +149,7 @@ def tile_moe_nxt_lin_bias_kernel(tc, xT, w, b, wp, gate, offs, out):
                 nc.vector.tensor_copy(s_planes[a // 4][:], x_planes[a // 4][:].indirect(offsets[:]))
 
         def groups_of(e):
-            return LAST_GROUPS if e == E - 1 else ((0, N),)
+            return LAST_GROUPS if e == E - 1 else ((0, HALF), (HALF, N))
 
         def multiply(u):
             e, a = divmod(u, PASSES)
@@ -172,6 +169,8 @@ def tile_moe_nxt_lin_bias_kernel(tc, xT, w, b, wp, gate, offs, out):
                     stop=(a == PASSES - 1),
                 )
 
+        waiting = []
+
         def finish(e):
             c_rows = mid.tile([P, N], BF16, name="c_rows", align_bytes=64)
             c_grouped = mid.tile([P, C, PACK], BF16, name="c_grouped", align_bytes=64)
@@ -180,7 +179,10 @@ def tile_moe_nxt_lin_bias_kernel(tc, xT, w, b, wp, gate, offs, out):
             turned = banks2.tile([P, 2, C], F32, name="turned")
             projected = []
             o_first = mid.tile([P, C], F32, name="o_first")
-            o_rest = mid.tile([P, M // P - 1, C], F32, name="o_rest")
+            now = M // P - 1 if e in HELD else M // P
+            o_rest = mid.tile([P, now - 1, C], F32, name="o_rest")
+
+            out_of_psum = nc.scalar.copy if e == E - 1 else nc.vector.tensor_copy
 
             def gated():
                 for bank, (lo, hi) in zip(acc[e], groups_of(e)):
@@ -190,6 +192,9 @@ def tile_moe_nxt_lin_bias_kernel(tc, xT, w, b, wp, gate, offs, out):
                 words = c_rows[:].bitcast(F32)
                 for u in range(2):
                     nc.tensor.transpose(turned[:, u, :], words[:, u : N // 2 : 2], ident[:])
+
+                if waiting:
+                    waiting.pop()()
 
             def regroup():
                 nc.scalar.copy(
@@ -217,9 +222,17 @@ def tile_moe_nxt_lin_bias_kernel(tc, xT, w, b, wp, gate, offs, out):
             def leave():
                 first, rest = projected
                 nc.scalar.copy(o_first[:], first[:])
-                nc.scalar.copy(o_rest[:], rest[:])
+                nc.scalar.copy(o_rest[:], rest[:, 0 : now - 1, :])
+
+            def held_back():
+                o_last = late.tile([P, C], F32, name=f"gated_bias{e + 1}")
+                (nc.scalar.copy if e == E - 2 else nc.vector.tensor_copy)(o_last[:], projected[1][:, now - 1, :])
+                nc.vector.tensor_copy(out_sb[now][:].indirect(offsets[:, e * C // 16 : (e + 1) * C // 16]), o_last[:])
 
             def scatter(f):
+                if f == now:
+                    waiting.append(held_back)
+                    return
                 src = o_first[:] if f == 0 else o_rest[:, f - 1, :]
                 nc.vector.tensor_copy(out_sb[f][:].indirect(offsets[:, e * C // 16 : (e + 1) * C // 16]), src)
                 if e == E - 1:
@@ -253,8 +266,7 @@ def tile_moe_nxt_lin_bias_kernel(tc, xT, w, b, wp, gate, offs, out):
             )
 
         def room(s, nxt):
-            ahead = [u for u in units[s + 1 : nxt + 1] if (u[0] == "x") == (units[nxt][0] == "x")]
-            return len(ahead) + (units[nxt] == last) <= (X_BUFS if units[nxt][0] == "x" else W_BUFS)
+            return nxt - s + (units[nxt] == last) <= W_BUFS
 
         loaded = 1
         while room(-1, loaded):
@@ -268,13 +280,13 @@ def tile_moe_nxt_lin_bias_kernel(tc, xT, w, b, wp, gate, offs, out):
             if s >= 2 and units[s - 2][0] == "x":
                 gather(units[s - 2][1])
                 gathered = units[s - 2][1] + 1 if units[s - 2][1] >= PASSES - 2 else 0
+            closing, steps = steps, None
+            if closing:
+                closing[2]()
             if s >= 1:
                 quantize(units[s - 1])
                 if units[s - 1][0] == "w":
                     quantized = units[s - 1][1] + 1
-            closing, steps = steps, None
-            if closing:
-                closing[2]()
             while multiplied < quantized and multiplied % PASSES < gathered:
                 multiply(multiplied)
                 multiplied += 1

@@ -26,16 +26,13 @@ PASSES = K // K_PASS
 SLOTS = E * C
 RUN = 4
 HALF = 256
-HELD = (0, 1, 2)
 W_BUFS = 9
-AFTER_CLOSE = (((384, 512, "v"), (0, 384, "s"), (0, 0, "step")), ((0, 160, "s"), (384, 512, "v"), (0, 0, "step"), (160, 384, "s")), ((0, 320, "g"), (320, 512, "s")), ((0, 320, "s"), (320, 512, "v")))
-LAST_PASS = ((0, 256, "v"), (320, 512, "s"), (256, 320, "v"))
-ELSE = ((0, 512, "s"),)
-EARLY = ((0, 256, "s"), (256, 512, "v"))
-X_SHARES = ((0, 256, "s"), (256, 512, "s"), (512, 768, "v"))
-LAST_LOADS = ((0, 384), (384, 512))
-LAST_GROUPS = ((0, 256), (256, 384), (384, 512))
-LAST_SHARES = ((0, 256, "v"), (256, 384, "s"), (384, 448, "v"), (448, 512, "s"))
+X_ON_SCALAR = 576
+EARLY_ON_SCALAR = 320
+FOURTH_ON_VECTOR = (256, 256, 256)
+LAST_LOADS = ((0, 512),)
+LAST_GROUPS = ((0, 256), (256, 512))
+LAST_SHARES = (((0, 256, "v"),), ((256, 320, "v"), (320, 512, "s")))
 
 
 def tile_moe_nxt_lin_bias_kernel(tc, xT, w, b, wp, gate, offs, out):
@@ -46,7 +43,7 @@ def tile_moe_nxt_lin_bias_kernel(tc, xT, w, b, wp, gate, offs, out):
         held = ctx.enter_context(tc.tile_pool(name="held", bufs=1))
         w_in = ctx.enter_context(tc.tile_pool(name="w_in", bufs=W_BUFS))
         mid = ctx.enter_context(tc.tile_pool(name="mid", bufs=2))
-        w_mid = ctx.enter_context(tc.tile_pool(name="w_mid", bufs=5))
+        w_mid = ctx.enter_context(tc.tile_pool(name="w_mid", bufs=6))
         w_q = ctx.enter_context(tc.tile_pool(name="w_q", bufs=7))
         late = ctx.enter_context(tc.tile_pool(name="late", bufs=1))
         banks2 = ctx.enter_context(tc.psum_pool(name="banks2", bufs=2))
@@ -68,7 +65,8 @@ def tile_moe_nxt_lin_bias_kernel(tc, xT, w, b, wp, gate, offs, out):
         units = [("w", 0)] + [("x", a) for a in range(PASSES)] + [("w", u) for u in range(1, PASSES - 1)]
         units += [("p", 0)] + [("w", u) for u in range(PASSES - 1, E * PASSES)]
         last = units[-1]
-        raw, grouped, coded, acc = {}, {}, {}, {}
+        raw, coded, acc = {}, {}, {}
+        state = {"loaded": 0, "freed": 0}
 
         def rows_of(unit):
             kind, i = unit
@@ -83,165 +81,95 @@ def tile_moe_nxt_lin_bias_kernel(tc, xT, w, b, wp, gate, offs, out):
                 nc.sync.dma_start(tile[:], rows_of(unit)[:, :, lo:hi])
                 raw[unit].append((lo, hi, tile))
 
-        closers = [units.index(("w", e * PASSES + PASSES - 1)) for e in range(E)]
+        def refill():
+            while state["loaded"] < len(units):
+                nxt = units[state["loaded"]]
+                if state["loaded"] - state["freed"] + (nxt == last) >= W_BUFS:
+                    break
+                load(nxt)
+                state["loaded"] += 1
 
-        def shares(unit):
-            at = units.index(unit)
-            if unit == last:
-                return LAST_SHARES
-            if unit[0] == "x":
-                return X_SHARES
-            if at == 0:
-                return ((0, N, "v"),)
-            if at < closers[0]:
-                return EARLY
-            if at in closers:
-                return LAST_PASS
-            since = at - max(c for c in closers if c < at)
-            return AFTER_CLOSE[since - 1] if since <= len(AFTER_CLOSE) else ELSE
+        def freed():
+            state["freed"] += 1
+            refill()
 
-        def copy(unit, between=None):
-            if unit[0] == "x":
-                g = mid.tile([P, T, PACK], BF16, name="x_grouped", align_bytes=64)
+        def part(lo, hi, tag=None):
+            if tag:
+                return (lo, hi, late.tile([P, hi - lo, PACK], BF16, name=tag, align_bytes=64))
+            return (lo, hi, w_mid.tile([P, hi - lo, PACK], BF16, name="grouped", align_bytes=64))
+
+        def interleave(unit, into, lo, hi, eng):
+            base, tile = [(a, t) for a, z, t in raw[unit] if a <= lo and hi <= z][0]
+            dst = into[2][:, lo - into[0] : hi - into[0], :].rearrange("p (c i) j -> p c j i", i=RUN)
+            src = tile[:, :, lo - base : hi - base].rearrange("p j (c i) -> p c j i", i=RUN)
+            if eng == "v":
+                nc.vector.tensor_copy(dst, src)
+            elif eng == "g":
+                nc.gpsimd.tensor_scalar(dst, src, 1.0, 0.0, MULT, ADD)
             else:
-                g = w_mid.tile([P, N, PACK], BF16, name="w_grouped", align_bytes=64)
-            grouped[unit] = g
-            for lo, hi, eng in shares(unit):
-                if eng == "step":
-                    between()
-                    continue
-                base, tile = [(a, t) for a, z, t in raw[unit] if a <= lo and hi <= z][0]
-                dst = g[:, lo:hi, :].rearrange("p (c i) j -> p c j i", i=RUN)
-                src = tile[:, :, lo - base : hi - base].rearrange("p j (c i) -> p c j i", i=RUN)
-                if eng == "v":
-                    nc.vector.tensor_copy(dst, src)
-                elif eng == "g":
-                    nc.gpsimd.tensor_scalar(dst, src, 1.0, 0.0, MULT, ADD)
-                else:
-                    nc.scalar.copy(dst, src)
+                nc.scalar.copy(dst, src)
 
-        def quantize_cols(codes, scales, g, lo, hi):
-            nc.vector.quantize_mx(
-                out=codes[:, lo:hi].bitcast(FP8X4),
-                scales=scales[:, lo:hi],
-                in_=g[:, lo:hi, :].rearrange("p c j -> p (c j)"),
-            )
-
-        def quantize(unit):
-            kind, i = unit
-            if kind == "x":
-                codes = mid.tile([P, T], U32, name="x_codes", align_bytes=64)
-                coded[unit] = codes
-                for lo, hi in ((0, 2 * HALF), (2 * HALF, T)):
-                    quantize_cols(codes, x_planes[i // 4][4 * (i % 4) : P, :], grouped[unit], lo, hi)
-            elif kind == "p":
-                quantize_cols(wp_codes, wp_scales, grouped[unit], 0, M)
-            else:
-                codes = w_q.tile([P, N], U32, name="w_codes", align_bytes=64)
-                plane = w_q.tile([P, N], U8, name="w_plane", align_bytes=64)
-                coded[unit] = (codes, plane)
-                for lo, hi in groups_of(i // PASSES) if i % PASSES == PASSES - 1 else ((0, N),):
-                    quantize_cols(codes, plane, grouped[unit], lo, hi)
-
-        def gather(a):
-            nc.vector.tensor_copy(s_codes[a][:], coded[("x", a)][:].indirect(offsets[:]))
-            if a >= PASSES - 2:
-                nc.vector.tensor_copy(s_planes[a // 4][:], x_planes[a // 4][:].indirect(offsets[:]))
+        def quantize(codes, scales, grouped):
+            nc.vector.quantize_mx(out=codes.bitcast(FP8X4), scales=scales, in_=grouped.rearrange("p c j -> p (c j)"))
 
         def groups_of(e):
             return LAST_GROUPS if e == E - 1 else ((0, HALF), (HALF, N))
 
-        def multiply(u):
+        def quantize_w(u, piece):
+            lo, hi, grouped = piece
+            if u not in coded:
+                codes = w_q.tile([P, N], U32, name="w_codes", align_bytes=64)
+                plane = w_q.tile([P, N], U8, name="w_plane", align_bytes=64)
+                coded[u] = (codes, plane)
+            quantize(coded[u][0][:, lo:hi], coded[u][1][:, lo:hi], grouped[:])
+
+        def multiply(u, lo, hi):
             e, a = divmod(u, PASSES)
-            if a == 0:
-                acc[e] = [banks2.tile([P, groups_of(e)[0][1]], F32, name="acc")]
-                acc[e] += [banks1.tile([P, hi - lo], F32, name=f"bank{k}") for k, (lo, hi) in enumerate(groups_of(e)[1:])]
-            codes, plane = coded[("w", u)]
+            codes, plane = coded[u]
             slots = slice(e * C, (e + 1) * C)
-            for bank, (lo, hi) in zip(acc[e], groups_of(e)):
+            for k, (first, end) in enumerate(groups_of(e)):
+                if not (lo <= first and end <= hi):
+                    continue
+                if a == 0 and k == 0:
+                    acc[e, k] = banks2.tile([P, end - first], F32, name="acc")
+                elif a == 0:
+                    acc[e, k] = banks1.tile([P, end - first], F32, name=f"bank{k - 1}")
                 nc.tensor.matmul_mx(
-                    out=bank[:],
+                    out=acc[e, k][:],
                     lhsT=s_codes[a][:, slots].bitcast(FP8X4),
                     lhsT_scale=s_planes[a // 4][4 * (a % 4) : P, slots],
-                    rhs=codes[:, lo:hi].bitcast(FP8X4),
-                    rhs_scale=plane[:, lo:hi],
+                    rhs=codes[:, first:end].bitcast(FP8X4),
+                    rhs_scale=plane[:, first:end],
                     start=(a == 0),
                     stop=(a == PASSES - 1),
                 )
 
-        waiting = []
+        def use(u, piece):
+            quantize_w(u, piece)
+            multiply(u, piece[0], piece[1])
 
-        def finish(e):
-            c_rows = mid.tile([P, N], BF16, name="c_rows", align_bytes=64)
-            c_grouped = mid.tile([P, C, PACK], BF16, name="c_grouped", align_bytes=64)
-            c_codes = mid.tile([P, C], U32, name="c_codes", align_bytes=64)
-            c_scales = mid.tile([P, C], U8, name="c_scales", align_bytes=64)
-            turned = banks2.tile([P, 2, C], F32, name="turned")
-            projected = []
-            o_first = mid.tile([P, C], F32, name="o_first")
-            now = M // P - 1 if e in HELD else M // P
-            o_rest = mid.tile([P, now - 1, C], F32, name="o_rest")
+        def scatter(e, f, src):
+            nc.vector.tensor_copy(out_sb[f][:].indirect(offsets[:, e * C // 16 : (e + 1) * C // 16]), src)
+            if e == E - 1:
+                nc.sync.dma_start(out[f * P : (f + 1) * P, :], out_sb[f][:])
 
-            out_of_psum = nc.scalar.copy if e == E - 1 else nc.vector.tensor_copy
+        def spread_bias(e):
+            spread = banks1.tile([P, PACK, P], F32, name=f"bank{e}")
+            for a in range(PACK):
+                nc.tensor.transpose(spread[:, a, :], bias_sb[:, a, e : e + 1].to_broadcast([P, P]), ident[:])
+            return spread
 
-            def gated():
-                for bank, (lo, hi) in zip(acc[e], groups_of(e)):
-                    nc.vector.scalar_tensor_tensor(
-                        c_rows[:, lo:hi], bank[:], gate_col[:, e : e + 1], gated_bias[e][:, lo:hi], MULT, ADD
-                    )
-                words = c_rows[:].bitcast(F32)
-                for u in range(2):
-                    nc.tensor.transpose(turned[:, u, :], words[:, u : N // 2 : 2], ident[:])
-
-                if waiting:
-                    waiting.pop()()
-
-            def regroup():
-                nc.scalar.copy(
-                    c_grouped[:].rearrange("p s j -> p (s j)").bitcast(F32).rearrange("p (s u) -> p s u", u=2),
-                    turned[:].rearrange("p u s -> p s u"),
-                )
-
-            def project():
-                quantize_cols(c_codes, c_scales, c_grouped, 0, C)
-                first = banks1.tile([P, C], F32, name="bank2")
-                rest = banks1.tile([P, M // P - 1, C], F32, name="bank3")
-                projected.extend((first, rest))
-                for f in range(M // P):
-                    cols = slice(f * P, (f + 1) * P)
-                    nc.tensor.matmul_mx(
-                        out=first[:] if f == 0 else rest[:, f - 1, :],
-                        lhsT=wp_codes[:, cols].bitcast(FP8X4),
-                        lhsT_scale=wp_scales[:, cols],
-                        rhs=c_codes[:].bitcast(FP8X4),
-                        rhs_scale=c_scales[:],
-                        start=True,
-                        stop=True,
-                    )
-
-            def leave():
-                first, rest = projected
-                nc.scalar.copy(o_first[:], first[:])
-                nc.scalar.copy(o_rest[:], rest[:, 0 : now - 1, :])
-
-            def held_back():
-                o_last = late.tile([P, C], F32, name=f"gated_bias{e + 1}")
-                (nc.scalar.copy if e == E - 2 else nc.vector.tensor_copy)(o_last[:], projected[1][:, now - 1, :])
-                nc.vector.tensor_copy(out_sb[now][:].indirect(offsets[:, e * C // 16 : (e + 1) * C // 16]), o_last[:])
-
-            def scatter(f):
-                if f == now:
-                    waiting.append(held_back)
-                    return
-                src = o_first[:] if f == 0 else o_rest[:, f - 1, :]
-                nc.vector.tensor_copy(out_sb[f][:].indirect(offsets[:, e * C // 16 : (e + 1) * C // 16]), src)
-                if e == E - 1:
-                    nc.sync.dma_start(out[f * P : (f + 1) * P, :], out_sb[f][:])
-
-            return gated, regroup, project, leave, scatter
+        def gate_bias(e, spread):
+            nc.scalar.activation(
+                gated_bias[e][:].rearrange("q (p a) -> q p a", a=PACK),
+                spread[:].rearrange("q a p -> q p a"),
+                COPY,
+                scale=gate_col[:, e : e + 1],
+            )
 
         load(units[0])
-        nc.gpsimd.memset(gate_rows[:], 0.0)
+        state["loaded"] = 1
+        nc.vector.memset(gate_rows[:], 0.0)
         nc.sync.dma_start(gate_rows[0:E, :], gate[0:1, :].rearrange("o (e c) -> (o e) c", c=C))
         nc.sync.dma_start(bias_sb[:], b.rearrange("(p a) e -> p a e", a=PACK))
         nc.sync.dma_start(offsets[:], offs)
@@ -250,61 +178,137 @@ def tile_moe_nxt_lin_bias_kernel(tc, xT, w, b, wp, gate, offs, out):
             nc.vector.memset(plane[:].bitcast(I32), 0)
         for f in range(M // P):
             nc.vector.memset(out_sb[f][:], 0.0)
+        refill()
 
         gate_turned = banks2.tile([P, P], F32, name="turned")
         nc.tensor.transpose(gate_turned[:], gate_rows[:], ident[:])
         nc.scalar.copy(gate_col[:], gate_turned[:, 0:E])
+        spreads = [spread_bias(e) for e in range(E)]
+
+
+        early = units[: units.index(("w", PASSES - 1))]
+        pieces, x_codes = {}, {}
+        for s in range(len(early) + 2):
+            if s < len(early):
+                kind, i = early[s]
+                if kind == "x":
+                    pieces[s] = (0, T, mid.tile([P, T, PACK], BF16, name="x_grouped", align_bytes=64))
+                else:
+                    pieces[s] = part(0, N)
+                cut = 0 if s == 0 else X_ON_SCALAR if kind == "x" else N if s <= PASSES + 2 else EARLY_ON_SCALAR
+                if cut:
+                    interleave(early[s], pieces[s], 0, cut, "s")
+                if s > PASSES and s - PASSES - 1 >= 0:
+                    gate_bias(s - PASSES - 1, spreads[s - PASSES - 1])
+            if 2 <= s and early[s - 2][0] == "x":
+                a = early[s - 2][1]
+                nc.vector.tensor_copy(s_codes[a][:], x_codes[a][:].indirect(offsets[:]))
+                if a >= PASSES - 2:
+                    nc.vector.tensor_copy(s_planes[a // 4][:], x_planes[a // 4][:].indirect(offsets[:]))
+            if 1 <= s <= len(early):
+                kind, i = early[s - 1]
+                grouped = pieces[s - 1][2]
+                if kind == "x":
+                    x_codes[i] = mid.tile([P, T], U32, name="x_codes", align_bytes=64)
+                    for lo, hi in ((0, 2 * HALF), (2 * HALF, T)):
+                        quantize(x_codes[i][:, lo:hi], x_planes[i // 4][4 * (i % 4) : P, lo:hi], grouped[:, lo:hi, :])
+                elif kind == "p":
+                    quantize(wp_codes[:], wp_scales[:], grouped[:])
+                else:
+                    quantize_w(i, pieces[s - 1])
+            if s < len(early):
+                if cut < pieces[s][1]:
+                    interleave(early[s], pieces[s], cut, pieces[s][1], "v")
+                freed()
+        for u in range(PASSES - 1):
+            multiply(u, 0, N)
+
+        held_back = None
         for e in range(E):
-            spread = banks1.tile([P, PACK, P], F32, name=f"bank{e}")
-            for a in range(PACK):
-                nc.tensor.transpose(spread[:, a, :], bias_sb[:, a, e : e + 1].to_broadcast([P, P]), ident[:])
-            nc.scalar.activation(
-                gated_bias[e][:].rearrange("q (p a) -> q p a", a=PACK),
-                spread[:].rearrange("q a p -> q p a"),
-                COPY,
-                scale=gate_col[:, e : e + 1],
+            more = e < E - 1
+            closing = e * PASSES + PASSES - 1
+            shares = ((( 0, HALF, "v"),), ((HALF, N, "s"),)) if more else LAST_SHARES
+            parts = [part(lo, hi, "side_a" if more and k == 1 else None) for k, (lo, hi) in enumerate(groups_of(e))]
+            for piece, share in zip(parts, shares):
+                for lo, hi, eng in share:
+                    interleave(("w", closing), piece, lo, hi, eng)
+            freed()
+            for piece in parts:
+                use(closing, piece)
+
+            nxt = [("w", closing + 1 + a) for a in range(PASSES - 1)]
+            if more:
+                first_a = part(0, HALF, "side_a")
+                first_b = part(HALF, N)
+                interleave(nxt[0], first_a, 0, 128, "g")
+                interleave(nxt[0], first_b, HALF, N, "s")
+                interleave(nxt[0], first_a, 128, HALF, "s")
+                freed()
+
+            c_rows = mid.tile([P, N], BF16, name="c_rows", align_bytes=64)
+            for k, (lo, hi) in enumerate(groups_of(e)):
+                nc.vector.scalar_tensor_tensor(
+                    c_rows[:, lo:hi], acc[e, k][:], gate_col[:, e : e + 1], gated_bias[e][:, lo:hi], MULT, ADD
+                )
+            turned = banks2.tile([P, 2, C], F32, name="turned")
+            words = c_rows[:].bitcast(F32)
+            for u in range(2):
+                nc.tensor.transpose(turned[:, u, :], words[:, u : N // 2 : 2], ident[:])
+            if held_back:
+                o_last = late.tile([P, C], F32, name=f"gated_bias{e}")
+                (nc.vector.tensor_copy if more else nc.scalar.copy)(o_last[:], held_back)
+                scatter(e - 1, M // P - 1, o_last[:])
+            c_grouped = mid.tile([P, C, PACK], BF16, name="c_grouped", align_bytes=64)
+            nc.scalar.copy(
+                c_grouped[:].rearrange("p s j -> p (s j)").bitcast(F32).rearrange("p (s u) -> p s u", u=2),
+                turned[:].rearrange("p u s -> p s u"),
             )
-
-        def room(s, nxt):
-            return nxt - s + (units[nxt] == last) <= W_BUFS
-
-        loaded = 1
-        while room(-1, loaded):
-            load(units[loaded])
-            loaded += 1
-        gathered = 0
-        multiplied = 0
-        quantized = 0
-        steps = None
-        for s in range(len(units) + 1):
-            if s >= 2 and units[s - 2][0] == "x":
-                gather(units[s - 2][1])
-                gathered = units[s - 2][1] + 1 if units[s - 2][1] >= PASSES - 2 else 0
-            closing, steps = steps, None
-            if closing:
-                closing[2]()
-            if s >= 1:
-                quantize(units[s - 1])
-                if units[s - 1][0] == "w":
-                    quantized = units[s - 1][1] + 1
-            while multiplied < quantized and multiplied % PASSES < gathered:
-                multiply(multiplied)
-                multiplied += 1
-                if multiplied % PASSES == 0:
-                    steps = finish(multiplied // PASSES - 1)
-            if s < len(units):
-                copy(units[s], closing[3] if closing else steps[0] if steps else None)
-            elif steps:
-                steps[0]()
-            if closing:
-                for f in range(M // P):
-                    closing[4](f)
-            if steps:
-                steps[1]()
-            while loaded < len(units) and room(s, loaded):
-                load(units[loaded])
-                loaded += 1
-        steps[2]()
-        steps[3]()
-        for f in range(M // P):
-            steps[4](f)
+            c_codes = late.tile([P, C], U32, name="side_c", align_bytes=64)
+            c_scales = mid.tile([P, C], U8, name="c_scales", align_bytes=64)
+            quantize(c_codes[:], c_scales[:], c_grouped[:])
+            first = banks1.tile([P, C], F32, name="bank2")
+            rest = banks1.tile([P, M // P - 1, C], F32, name="bank3")
+            for f in range(M // P):
+                cols = slice(f * P, (f + 1) * P)
+                nc.tensor.matmul_mx(
+                    out=first[:] if f == 0 else rest[:, f - 1, :],
+                    lhsT=wp_codes[:, cols].bitcast(FP8X4),
+                    lhsT_scale=wp_scales[:, cols],
+                    rhs=c_codes[:].bitcast(FP8X4),
+                    rhs_scale=c_scales[:],
+                    start=True,
+                    stop=True,
+                )
+            if more:
+                second_a = part(0, HALF, "side_b")
+                interleave(nxt[1], second_a, 0, HALF, "s")
+                use(nxt[0][1], first_b)
+                use(nxt[0][1], first_a)
+            now = M // P - 1 if more else M // P
+            o_first = mid.tile([P, C], F32, name="o_first")
+            o_rest = mid.tile([P, now - 1, C], F32, name="o_rest")
+            nc.scalar.copy(o_first[:], first[:])
+            nc.scalar.copy(o_rest[:], rest[:, 0 : now - 1, :])
+            held_back = rest[:, now - 1, :] if more else None
+            if more:
+                use(nxt[1][1], second_a)
+                second_b = part(HALF, N, "side_c")
+                interleave(nxt[1], second_b, HALF, N, "s")
+                freed()
+                third_a = part(0, HALF, "side_b")
+                third_b = part(HALF, N)
+                interleave(nxt[2], third_a, 0, 192, "g")
+                interleave(nxt[2], third_a, 192, HALF, "s")
+                interleave(nxt[2], third_b, HALF, N, "s")
+                freed()
+            for f in range(now):
+                scatter(e, f, o_first[:] if f == 0 else o_rest[:, f - 1, :])
+            if more:
+                fourth = part(0, N)
+                interleave(nxt[3], fourth, 0, N - FOURTH_ON_VECTOR[e], "s")
+                use(nxt[1][1], second_b)
+                interleave(nxt[3], fourth, N - FOURTH_ON_VECTOR[e], N, "v")
+                freed()
+                use(nxt[2][1], third_a)
+                use(nxt[2][1], third_b)
+                use(nxt[3][1], fourth)

@@ -24,15 +24,18 @@ PACK = 4
 K_PASS = P * PACK
 PASSES = K // K_PASS
 SLOTS = E * C
+OUT_TILES = M // P
 RUN = 4
-HALF = 256
-W_BUFS = 9
-X_ON_SCALAR = 576
-EARLY_ON_SCALAR = 320
-FOURTH_ON_VECTOR = (256, 256, 256)
-LAST_LOADS = ((0, 512),)
-LAST_GROUPS = ((0, 256), (256, 512))
-LAST_SHARES = (((0, 256, "v"),), ((256, 320, "v"), (320, 512, "s")))
+HALF = N // 2
+HALVES = ((0, HALF), (HALF, N))
+
+LOAD_BUFS = 9
+GROUPED_BUFS = 6
+CODE_BUFS = 7
+
+GPSIMD_UNDER_GATING = 128
+GPSIMD_UNDER_SCATTERS = 192
+LAST_EXTRA_ON_VECTOR = 64
 
 
 def tile_moe_nxt_lin_bias_kernel(tc, xT, w, b, wp, gate, offs, out):
@@ -41,11 +44,11 @@ def tile_moe_nxt_lin_bias_kernel(tc, xT, w, b, wp, gate, offs, out):
 
     with ExitStack() as ctx:
         held = ctx.enter_context(tc.tile_pool(name="held", bufs=1))
-        w_in = ctx.enter_context(tc.tile_pool(name="w_in", bufs=W_BUFS))
-        mid = ctx.enter_context(tc.tile_pool(name="mid", bufs=2))
-        w_mid = ctx.enter_context(tc.tile_pool(name="w_mid", bufs=6))
-        w_q = ctx.enter_context(tc.tile_pool(name="w_q", bufs=7))
-        late = ctx.enter_context(tc.tile_pool(name="late", bufs=1))
+        loads = ctx.enter_context(tc.tile_pool(name="loads", bufs=LOAD_BUFS))
+        pairs = ctx.enter_context(tc.tile_pool(name="pairs", bufs=2))
+        grouped_pool = ctx.enter_context(tc.tile_pool(name="grouped_pool", bufs=GROUPED_BUFS))
+        code_pool = ctx.enter_context(tc.tile_pool(name="code_pool", bufs=CODE_BUFS))
+        turns = ctx.enter_context(tc.tile_pool(name="turns", bufs=1))
         banks2 = ctx.enter_context(tc.psum_pool(name="banks2", bufs=2))
         banks1 = ctx.enter_context(tc.psum_pool(name="banks1", bufs=1))
 
@@ -54,72 +57,63 @@ def tile_moe_nxt_lin_bias_kernel(tc, xT, w, b, wp, gate, offs, out):
         gate_rows = held.tile([P, C], F32, name="gate_rows")
         gate_col = held.tile([P, E], F32, name="gate_col")
         bias_sb = held.tile([P, PACK, E], F32, name="bias_sb")
-        gated_bias = [late.tile([P, N], F32, name=f"gated_bias{e}") for e in range(E)]
+        gated_bias = [turns.tile([P, N], F32, name=f"gated_bias{e}") for e in range(E)]
         x_planes = [held.tile([P, T], U8, name=f"x_planes{i}", align_bytes=64) for i in range(2)]
         s_codes = [held.tile([P, SLOTS], U32, name=f"s_codes{a}", align_bytes=64) for a in range(PASSES)]
         s_planes = [held.tile([P, SLOTS], U8, name=f"s_planes{i}", align_bytes=64) for i in range(2)]
         wp_codes = held.tile([P, M], U32, name="wp_codes", align_bytes=64)
         wp_scales = held.tile([P, M], U8, name="wp_scales", align_bytes=64)
-        out_sb = [held.tile([P, T], F32, name=f"out_sb{f}") for f in range(M // P)]
+        out_sb = [held.tile([P, T], F32, name=f"out_sb{f}") for f in range(OUT_TILES)]
 
         units = [("w", 0)] + [("x", a) for a in range(PASSES)] + [("w", u) for u in range(1, PASSES - 1)]
         units += [("p", 0)] + [("w", u) for u in range(PASSES - 1, E * PASSES)]
-        last = units[-1]
         raw, coded, acc = {}, {}, {}
-        state = {"loaded": 0, "freed": 0}
+        count = {"loaded": 0, "freed": 0}
 
-        def rows_of(unit):
-            kind, i = unit
-            src = {"x": xT, "w": w_rows, "p": wp}[kind]
-            return src[i * K_PASS : (i + 1) * K_PASS, :].rearrange("(p j) c -> p j c", j=PACK)
-
-        def load(unit):
-            width = T if unit[0] == "x" else N
-            raw[unit] = []
-            for lo, hi in LAST_LOADS if unit == last else ((0, width),):
-                tile = w_in.tile([P, PACK, hi - lo], F32, name="w_raw")
-                nc.sync.dma_start(tile[:], rows_of(unit)[:, :, lo:hi])
-                raw[unit].append((lo, hi, tile))
+        def load_next():
+            kind, i = unit = units[count["loaded"]]
+            rows = {"x": xT, "w": w_rows, "p": wp}[kind][i * K_PASS : (i + 1) * K_PASS, :]
+            raw[unit] = loads.tile([P, PACK, T if kind == "x" else N], F32, name="raw")
+            nc.sync.dma_start(raw[unit][:], rows.rearrange("(p j) c -> p j c", j=PACK))
+            count["loaded"] += 1
 
         def refill():
-            while state["loaded"] < len(units):
-                nxt = units[state["loaded"]]
-                if state["loaded"] - state["freed"] + (nxt == last) >= W_BUFS:
-                    break
-                load(nxt)
-                state["loaded"] += 1
+            while count["loaded"] < len(units) and count["loaded"] - count["freed"] < LOAD_BUFS:
+                load_next()
 
         def freed():
-            state["freed"] += 1
+            count["freed"] += 1
             refill()
 
-        def part(lo, hi, tag=None):
-            if tag:
-                return (lo, hi, late.tile([P, hi - lo, PACK], BF16, name=tag, align_bytes=64))
-            return (lo, hi, w_mid.tile([P, hi - lo, PACK], BF16, name="grouped", align_bytes=64))
+        def piece(lo, hi, turn=None):
+            if turn:
+                return (lo, hi, turns.tile([P, hi - lo, PACK], BF16, name=turn, align_bytes=64))
+            return (lo, hi, grouped_pool.tile([P, hi - lo, PACK], BF16, name="grouped", align_bytes=64))
 
-        def interleave(unit, into, lo, hi, eng):
-            base, tile = [(a, t) for a, z, t in raw[unit] if a <= lo and hi <= z][0]
-            dst = into[2][:, lo - into[0] : hi - into[0], :].rearrange("p (c i) j -> p c j i", i=RUN)
-            src = tile[:, :, lo - base : hi - base].rearrange("p j (c i) -> p c j i", i=RUN)
-            if eng == "v":
+        def interleave(unit, into, lo, hi, engine):
+            dst = into[2][:, lo - into[0] : hi - into[0], :]
+            src = raw[unit][:, :, lo:hi]
+            if engine == "gpsimd":
+                nc.gpsimd.tensor_scalar(dst, src.rearrange("p j c -> p c j"), 1.0, 0.0, MULT, ADD)
+                return
+            dst = dst.rearrange("p (c i) j -> p c j i", i=RUN)
+            src = src.rearrange("p j (c i) -> p c j i", i=RUN)
+            if engine == "vector":
                 nc.vector.tensor_copy(dst, src)
-            elif eng == "g":
-                nc.gpsimd.tensor_scalar(dst, src, 1.0, 0.0, MULT, ADD)
             else:
                 nc.scalar.copy(dst, src)
 
         def quantize(codes, scales, grouped):
             nc.vector.quantize_mx(out=codes.bitcast(FP8X4), scales=scales, in_=grouped.rearrange("p c j -> p (c j)"))
 
-        def groups_of(e):
-            return LAST_GROUPS if e == E - 1 else ((0, HALF), (HALF, N))
-
-        def quantize_w(u, piece):
-            lo, hi, grouped = piece
+        def quantize_w(u, source, turn=None):
+            lo, hi, grouped = source
             if u not in coded:
-                codes = w_q.tile([P, N], U32, name="w_codes", align_bytes=64)
-                plane = w_q.tile([P, N], U8, name="w_plane", align_bytes=64)
+                if turn:
+                    codes = turns.tile([P, N], U32, name=turn, align_bytes=64)
+                else:
+                    codes = code_pool.tile([P, N], U32, name="w_codes", align_bytes=64)
+                plane = code_pool.tile([P, N], U8, name="w_plane", align_bytes=64)
                 coded[u] = (codes, plane)
             quantize(coded[u][0][:, lo:hi], coded[u][1][:, lo:hi], grouped[:])
 
@@ -127,48 +121,32 @@ def tile_moe_nxt_lin_bias_kernel(tc, xT, w, b, wp, gate, offs, out):
             e, a = divmod(u, PASSES)
             codes, plane = coded[u]
             slots = slice(e * C, (e + 1) * C)
-            for k, (first, end) in enumerate(groups_of(e)):
-                if not (lo <= first and end <= hi):
-                    continue
-                if a == 0 and k == 0:
-                    acc[e, k] = banks2.tile([P, end - first], F32, name="acc")
+            for h in range(lo // HALF, hi // HALF):
+                cols = slice(h * HALF, (h + 1) * HALF)
+                if a == 0 and h == 0:
+                    acc[e, h] = banks2.tile([P, HALF], F32, name="acc")
                 elif a == 0:
-                    acc[e, k] = banks1.tile([P, end - first], F32, name=f"bank{k - 1}")
+                    acc[e, h] = banks1.tile([P, HALF], F32, name="bank0")
                 nc.tensor.matmul_mx(
-                    out=acc[e, k][:],
+                    out=acc[e, h][:],
                     lhsT=s_codes[a][:, slots].bitcast(FP8X4),
                     lhsT_scale=s_planes[a // 4][4 * (a % 4) : P, slots],
-                    rhs=codes[:, first:end].bitcast(FP8X4),
-                    rhs_scale=plane[:, first:end],
+                    rhs=codes[:, cols].bitcast(FP8X4),
+                    rhs_scale=plane[:, cols],
                     start=(a == 0),
                     stop=(a == PASSES - 1),
                 )
 
-        def use(u, piece):
-            quantize_w(u, piece)
-            multiply(u, piece[0], piece[1])
+        def use(u, source, turn=None):
+            quantize_w(u, source, turn)
+            multiply(u, source[0], source[1])
 
         def scatter(e, f, src):
             nc.vector.tensor_copy(out_sb[f][:].indirect(offsets[:, e * C // 16 : (e + 1) * C // 16]), src)
             if e == E - 1:
                 nc.sync.dma_start(out[f * P : (f + 1) * P, :], out_sb[f][:])
 
-        def spread_bias(e):
-            spread = banks1.tile([P, PACK, P], F32, name=f"bank{e}")
-            for a in range(PACK):
-                nc.tensor.transpose(spread[:, a, :], bias_sb[:, a, e : e + 1].to_broadcast([P, P]), ident[:])
-            return spread
-
-        def gate_bias(e, spread):
-            nc.scalar.activation(
-                gated_bias[e][:].rearrange("q (p a) -> q p a", a=PACK),
-                spread[:].rearrange("q a p -> q p a"),
-                COPY,
-                scale=gate_col[:, e : e + 1],
-            )
-
-        load(units[0])
-        state["loaded"] = 1
+        load_next()
         nc.vector.memset(gate_rows[:], 0.0)
         nc.sync.dma_start(gate_rows[0:E, :], gate[0:1, :].rearrange("o (e c) -> (o e) c", c=C))
         nc.sync.dma_start(bias_sb[:], b.rearrange("(p a) e -> p a e", a=PACK))
@@ -176,41 +154,60 @@ def tile_moe_nxt_lin_bias_kernel(tc, xT, w, b, wp, gate, offs, out):
         make_identity(nc, ident[:])
         for plane in x_planes:
             nc.vector.memset(plane[:].bitcast(I32), 0)
-        for f in range(M // P):
+        for f in range(OUT_TILES):
             nc.vector.memset(out_sb[f][:], 0.0)
         refill()
 
         gate_turned = banks2.tile([P, P], F32, name="turned")
         nc.tensor.transpose(gate_turned[:], gate_rows[:], ident[:])
         nc.scalar.copy(gate_col[:], gate_turned[:, 0:E])
-        spreads = [spread_bias(e) for e in range(E)]
+        spreads = []
+        for e in range(E):
+            spread = banks1.tile([P, PACK, P], F32, name=f"bank{e}")
+            for a in range(PACK):
+                nc.tensor.transpose(spread[:, a, :], bias_sb[:, a, e : e + 1].to_broadcast([P, P]), ident[:])
+            spreads.append(spread)
 
+        def on_scalar(unit):
+            kind, i = unit
+            if kind == "x":
+                return T // 3 if i == 0 else 2 * T // 3
+            if unit == units[0]:
+                return 0
+            if kind == "w" and i < PASSES - 2:
+                return N
+            return HALF
 
         early = units[: units.index(("w", PASSES - 1))]
         pieces, x_codes = {}, {}
-        for s in range(len(early) + 2):
+        for s in range(len(early) + 1):
             if s < len(early):
-                kind, i = early[s]
-                if kind == "x":
-                    pieces[s] = (0, T, mid.tile([P, T, PACK], BF16, name="x_grouped", align_bytes=64))
+                if early[s][0] == "x":
+                    pieces[s] = (0, T, pairs.tile([P, T, PACK], BF16, name="x_grouped", align_bytes=64))
                 else:
-                    pieces[s] = part(0, N)
-                cut = 0 if s == 0 else X_ON_SCALAR if kind == "x" else N if s <= PASSES + 2 else EARLY_ON_SCALAR
+                    pieces[s] = piece(0, N)
+                cut = on_scalar(early[s])
                 if cut:
-                    interleave(early[s], pieces[s], 0, cut, "s")
-                if s > PASSES and s - PASSES - 1 >= 0:
-                    gate_bias(s - PASSES - 1, spreads[s - PASSES - 1])
-            if 2 <= s and early[s - 2][0] == "x":
+                    interleave(early[s], pieces[s], 0, cut, "scalar")
+                if s > PASSES:
+                    e = s - PASSES - 1
+                    nc.scalar.activation(
+                        gated_bias[e][:].rearrange("q (m a) -> q m a", a=PACK),
+                        spreads[e][:].rearrange("q a m -> q m a"),
+                        COPY,
+                        scale=gate_col[:, e : e + 1],
+                    )
+            if s >= 2 and early[s - 2][0] == "x":
                 a = early[s - 2][1]
                 nc.vector.tensor_copy(s_codes[a][:], x_codes[a][:].indirect(offsets[:]))
-                if a >= PASSES - 2:
+                if a % 4 == 3 or a == PASSES - 1:
                     nc.vector.tensor_copy(s_planes[a // 4][:], x_planes[a // 4][:].indirect(offsets[:]))
-            if 1 <= s <= len(early):
+            if s >= 1:
                 kind, i = early[s - 1]
                 grouped = pieces[s - 1][2]
                 if kind == "x":
-                    x_codes[i] = mid.tile([P, T], U32, name="x_codes", align_bytes=64)
-                    for lo, hi in ((0, 2 * HALF), (2 * HALF, T)):
+                    x_codes[i] = pairs.tile([P, T], U32, name="x_codes", align_bytes=64)
+                    for lo, hi in ((0, 2 * T // 3), (2 * T // 3, T)):
                         quantize(x_codes[i][:, lo:hi], x_planes[i // 4][4 * (i % 4) : P, lo:hi], grouped[:, lo:hi, :])
                 elif kind == "p":
                     quantize(wp_codes[:], wp_scales[:], grouped[:])
@@ -218,57 +215,59 @@ def tile_moe_nxt_lin_bias_kernel(tc, xT, w, b, wp, gate, offs, out):
                     quantize_w(i, pieces[s - 1])
             if s < len(early):
                 if cut < pieces[s][1]:
-                    interleave(early[s], pieces[s], cut, pieces[s][1], "v")
+                    interleave(early[s], pieces[s], cut, pieces[s][1], "vector")
                 freed()
         for u in range(PASSES - 1):
             multiply(u, 0, N)
 
-        held_back = None
+        waiting = None
         for e in range(E):
             more = e < E - 1
             closing = e * PASSES + PASSES - 1
-            shares = ((( 0, HALF, "v"),), ((HALF, N, "s"),)) if more else LAST_SHARES
-            parts = [part(lo, hi, "side_a" if more and k == 1 else None) for k, (lo, hi) in enumerate(groups_of(e))]
-            for piece, share in zip(parts, shares):
-                for lo, hi, eng in share:
-                    interleave(("w", closing), piece, lo, hi, eng)
-            freed()
-            for piece in parts:
-                use(closing, piece)
+            u0, u1, u2, u3 = range(closing + 1, closing + PASSES)
 
-            nxt = [("w", closing + 1 + a) for a in range(PASSES - 1)]
+            lower = piece(0, HALF)
+            upper = piece(HALF, N, "before_gating" if more else None)
+            extra = 0 if more else LAST_EXTRA_ON_VECTOR
+            interleave(("w", closing), lower, 0, HALF, "vector")
+            if extra:
+                interleave(("w", closing), upper, HALF, HALF + extra, "vector")
+            interleave(("w", closing), upper, HALF + extra, N, "scalar")
+            freed()
+            use(closing, lower)
+            use(closing, upper)
+
             if more:
-                first_a = part(0, HALF, "side_a")
-                first_b = part(HALF, N)
-                interleave(nxt[0], first_a, 0, 128, "g")
-                interleave(nxt[0], first_b, HALF, N, "s")
-                interleave(nxt[0], first_a, 128, HALF, "s")
+                pass0 = piece(0, N, "before_gating")
+                interleave(("w", u0), pass0, 0, GPSIMD_UNDER_GATING, "gpsimd")
+                interleave(("w", u0), pass0, GPSIMD_UNDER_GATING, N, "scalar")
                 freed()
 
-            c_rows = mid.tile([P, N], BF16, name="c_rows", align_bytes=64)
-            for k, (lo, hi) in enumerate(groups_of(e)):
+            c_rows = pairs.tile([P, N], BF16, name="c_rows", align_bytes=64)
+            for h, (lo, hi) in enumerate(HALVES):
                 nc.vector.scalar_tensor_tensor(
-                    c_rows[:, lo:hi], acc[e, k][:], gate_col[:, e : e + 1], gated_bias[e][:, lo:hi], MULT, ADD
+                    c_rows[:, lo:hi], acc[e, h][:], gate_col[:, e : e + 1], gated_bias[e][:, lo:hi], MULT, ADD
                 )
             turned = banks2.tile([P, 2, C], F32, name="turned")
             words = c_rows[:].bitcast(F32)
             for u in range(2):
                 nc.tensor.transpose(turned[:, u, :], words[:, u : N // 2 : 2], ident[:])
-            if held_back:
-                o_last = late.tile([P, C], F32, name=f"gated_bias{e}")
-                (nc.vector.tensor_copy if more else nc.scalar.copy)(o_last[:], held_back)
-                scatter(e - 1, M // P - 1, o_last[:])
-            c_grouped = mid.tile([P, C, PACK], BF16, name="c_grouped", align_bytes=64)
+            if waiting is not None:
+                o_last = turns.tile([P, C], F32, name=f"gated_bias{e}")
+                (nc.vector.tensor_copy if more else nc.scalar.copy)(o_last[:], waiting)
+                scatter(e - 1, OUT_TILES - 1, o_last[:])
+            c_grouped = turns.tile([P, C, PACK], BF16, name="c_first", align_bytes=64)
             nc.scalar.copy(
                 c_grouped[:].rearrange("p s j -> p (s j)").bitcast(F32).rearrange("p (s u) -> p s u", u=2),
                 turned[:].rearrange("p u s -> p s u"),
             )
-            c_codes = late.tile([P, C], U32, name="side_c", align_bytes=64)
-            c_scales = mid.tile([P, C], U8, name="c_scales", align_bytes=64)
+            c_codes = turns.tile([P, C], U32, name="projection_first", align_bytes=64)
+            c_scales = pairs.tile([P, C], U8, name="c_scales", align_bytes=64)
             quantize(c_codes[:], c_scales[:], c_grouped[:])
+
             first = banks1.tile([P, C], F32, name="bank2")
-            rest = banks1.tile([P, M // P - 1, C], F32, name="bank3")
-            for f in range(M // P):
+            rest = banks1.tile([P, OUT_TILES - 1, C], F32, name="bank3")
+            for f in range(OUT_TILES):
                 cols = slice(f * P, (f + 1) * P)
                 nc.tensor.matmul_mx(
                     out=first[:] if f == 0 else rest[:, f - 1, :],
@@ -280,35 +279,32 @@ def tile_moe_nxt_lin_bias_kernel(tc, xT, w, b, wp, gate, offs, out):
                     stop=True,
                 )
             if more:
-                second_a = part(0, HALF, "side_b")
-                interleave(nxt[1], second_a, 0, HALF, "s")
-                use(nxt[0][1], first_b)
-                use(nxt[0][1], first_a)
-            now = M // P - 1 if more else M // P
-            o_first = mid.tile([P, C], F32, name="o_first")
-            o_rest = mid.tile([P, now - 1, C], F32, name="o_rest")
+                pass1_lower = piece(0, HALF, "before_scatters")
+                interleave(("w", u1), pass1_lower, 0, HALF, "scalar")
+                use(u0, pass0, "c_first")
+
+            now = OUT_TILES - 1 if more else OUT_TILES
+            o_first = pairs.tile([P, C], F32, name="o_first")
+            o_rest = pairs.tile([P, now - 1, C], F32, name="o_rest")
             nc.scalar.copy(o_first[:], first[:])
             nc.scalar.copy(o_rest[:], rest[:, 0 : now - 1, :])
-            held_back = rest[:, now - 1, :] if more else None
+            waiting = rest[:, now - 1, :] if more else None
             if more:
-                use(nxt[1][1], second_a)
-                second_b = part(HALF, N, "side_c")
-                interleave(nxt[1], second_b, HALF, N, "s")
+                use(u1, pass1_lower)
+                pass1_upper = piece(HALF, N, "projection_first")
+                interleave(("w", u1), pass1_upper, HALF, N, "scalar")
                 freed()
-                third_a = part(0, HALF, "side_b")
-                third_b = part(HALF, N)
-                interleave(nxt[2], third_a, 0, 192, "g")
-                interleave(nxt[2], third_a, 192, HALF, "s")
-                interleave(nxt[2], third_b, HALF, N, "s")
+                pass2 = piece(0, N, "before_scatters")
+                interleave(("w", u2), pass2, 0, GPSIMD_UNDER_SCATTERS, "gpsimd")
+                interleave(("w", u2), pass2, GPSIMD_UNDER_SCATTERS, N, "scalar")
                 freed()
             for f in range(now):
                 scatter(e, f, o_first[:] if f == 0 else o_rest[:, f - 1, :])
             if more:
-                fourth = part(0, N)
-                interleave(nxt[3], fourth, 0, N - FOURTH_ON_VECTOR[e], "s")
-                use(nxt[1][1], second_b)
-                interleave(nxt[3], fourth, N - FOURTH_ON_VECTOR[e], N, "v")
+                pass3 = piece(0, N)
+                interleave(("w", u3), pass3, 0, HALF, "scalar")
+                use(u1, pass1_upper)
+                interleave(("w", u3), pass3, HALF, N, "vector")
                 freed()
-                use(nxt[2][1], third_a)
-                use(nxt[2][1], third_b)
-                use(nxt[3][1], fourth)
+                use(u2, pass2)
+                use(u3, pass3)

@@ -5,7 +5,7 @@ from concourse.masks import make_identity
 
 K, T, E, C, N, M = 2560, 768, 4, 128, 512, 512
 
-FLOPS = 2 * E * C * K * N + 2 * E * C * N * M
+FLOPS = 2 * E * C * K * N + 2 * T * N * M
 
 F32 = mybir.dt.float32
 BF16 = mybir.dt.bfloat16
@@ -30,12 +30,12 @@ HALF = N // 2
 HALVES = ((0, HALF), (HALF, N))
 
 LOAD_BUFS = 9
-GROUPED_BUFS = 6
+GROUPED_BUFS = 5
 CODE_BUFS = 7
-
-GPSIMD_UNDER_GATING = 128
-GPSIMD_UNDER_SCATTERS = 192
-LAST_EXTRA_ON_VECTOR = 64
+TOKEN_CUTS = ((0, 512), (512, T))
+W_ON_SCALAR = 352
+W_ON_SCALAR_CLOSING = 384
+W_ON_SCALAR_LAST = 288
 
 
 def tile_moe_nxt_lin_bias_kernel(tc, xT, w, b, wp, gate, offs, out):
@@ -49,24 +49,29 @@ def tile_moe_nxt_lin_bias_kernel(tc, xT, w, b, wp, gate, offs, out):
         grouped_pool = ctx.enter_context(tc.tile_pool(name="grouped_pool", bufs=GROUPED_BUFS))
         code_pool = ctx.enter_context(tc.tile_pool(name="code_pool", bufs=CODE_BUFS))
         turns = ctx.enter_context(tc.tile_pool(name="turns", bufs=1))
-        banks2 = ctx.enter_context(tc.psum_pool(name="banks2", bufs=2))
-        banks1 = ctx.enter_context(tc.psum_pool(name="banks1", bufs=1))
+        banks = ctx.enter_context(tc.psum_pool(name="banks", bufs=1))
 
         offsets = held.tile([P, SLOTS // 16], U16, name="offsets")
         ident = held.tile([P, P], F32, name="ident")
         gate_rows = held.tile([P, C], F32, name="gate_rows")
         gate_col = held.tile([P, E], F32, name="gate_col")
         bias_sb = held.tile([P, PACK, E], F32, name="bias_sb")
-        gated_bias = [turns.tile([P, N], F32, name=f"gated_bias{e}") for e in range(E)]
+        gated_bias = [turns.tile([P, N], F32, name=f"gated_bias{e}", align_bytes=64) for e in range(E)]
         x_planes = [held.tile([P, T], U8, name=f"x_planes{i}", align_bytes=64) for i in range(2)]
         s_codes = [held.tile([P, SLOTS], U32, name=f"s_codes{a}", align_bytes=64) for a in range(PASSES)]
         s_planes = [held.tile([P, SLOTS], U8, name=f"s_planes{i}", align_bytes=64) for i in range(2)]
         wp_codes = held.tile([P, M], U32, name="wp_codes", align_bytes=64)
         wp_scales = held.tile([P, M], U8, name="wp_scales", align_bytes=64)
+        c_tokens = [held.tile([P, T], F32, name=f"c_tokens{u}") for u in range(2)]
+        c_joined = held.tile([P, 2, T], F32, name="c_joined")
+        t_codes = {}
+        t_scales = held.tile([P, T], U8, name="t_scales", align_bytes=64)
         out_sb = [held.tile([P, T], F32, name=f"out_sb{f}") for f in range(OUT_TILES)]
 
-        units = [("w", 0)] + [("x", a) for a in range(PASSES)] + [("w", u) for u in range(1, PASSES - 1)]
-        units += [("p", 0)] + [("w", u) for u in range(PASSES - 1, E * PASSES)]
+        X, W = "x", "w"
+        units = [(X, 0), (W, 0), (X, 1), (W, 1), (X, 2), (X, 3), (W, 2), (X, 4), (W, 3)]
+        early = list(units)
+        units += [(W, u) for u in range(PASSES - 1, E * PASSES)] + [("p", 0)]
         raw, coded, acc = {}, {}, {}
         count = {"loaded": 0, "freed": 0}
 
@@ -106,45 +111,61 @@ def tile_moe_nxt_lin_bias_kernel(tc, xT, w, b, wp, gate, offs, out):
         def quantize(codes, scales, grouped):
             nc.vector.quantize_mx(out=codes.bitcast(FP8X4), scales=scales, in_=grouped.rearrange("p c j -> p (c j)"))
 
-        def quantize_w(u, source, turn=None):
+        def quantize_w(u, source):
             lo, hi, grouped = source
             if u not in coded:
-                if turn:
-                    codes = turns.tile([P, N], U32, name=turn, align_bytes=64)
-                else:
-                    codes = code_pool.tile([P, N], U32, name="w_codes", align_bytes=64)
+                codes = code_pool.tile([P, N], U32, name="w_codes", align_bytes=64)
                 plane = code_pool.tile([P, N], U8, name="w_plane", align_bytes=64)
                 coded[u] = (codes, plane)
             quantize(coded[u][0][:, lo:hi], coded[u][1][:, lo:hi], grouped[:])
+
+        def mx(dst, lhs, lhs_scale, rhs, rhs_scale, start=True, stop=True):
+            nc.tensor.matmul_mx(
+                out=dst,
+                lhsT=lhs.bitcast(FP8X4),
+                lhsT_scale=lhs_scale,
+                rhs=rhs.bitcast(FP8X4),
+                rhs_scale=rhs_scale,
+                start=start,
+                stop=stop,
+            )
+
+        def cuts(e):
+            return HALVES if e == E - 1 else ((0, N),)
 
         def multiply(u, lo, hi):
             e, a = divmod(u, PASSES)
             codes, plane = coded[u]
             slots = slice(e * C, (e + 1) * C)
-            for h in range(lo // HALF, hi // HALF):
-                cols = slice(h * HALF, (h + 1) * HALF)
-                if a == 0 and h == 0:
-                    acc[e, h] = banks2.tile([P, HALF], F32, name="acc")
-                elif a == 0:
-                    acc[e, h] = banks1.tile([P, HALF], F32, name="bank0")
-                nc.tensor.matmul_mx(
-                    out=acc[e, h][:],
-                    lhsT=s_codes[a][:, slots].bitcast(FP8X4),
-                    lhsT_scale=s_planes[a // 4][4 * (a % 4) : P, slots],
-                    rhs=codes[:, cols].bitcast(FP8X4),
-                    rhs_scale=plane[:, cols],
-                    start=(a == 0),
-                    stop=(a == PASSES - 1),
+            for h, (c0, c1) in enumerate(cuts(e)):
+                if c0 < lo or c1 > hi:
+                    continue
+                if a == 0:
+                    bank = h if e == E - 1 else 5 + e % 2
+                    acc[e, h] = banks.tile([P, c1 - c0], F32, name=f"bank{bank}")
+                mx(
+                    acc[e, h][:],
+                    s_codes[a][:, slots],
+                    s_planes[a // 4][4 * (a % 4) : P, slots],
+                    codes[:, c0:c1],
+                    plane[:, c0:c1],
+                    a == 0,
+                    a == PASSES - 1,
                 )
 
-        def use(u, source, turn=None):
-            quantize_w(u, source, turn)
+        def use(u, source):
+            quantize_w(u, source)
             multiply(u, source[0], source[1])
 
-        def scatter(e, f, src):
-            nc.vector.tensor_copy(out_sb[f][:].indirect(offsets[:, e * C // 16 : (e + 1) * C // 16]), src)
-            if e == E - 1:
-                nc.sync.dma_start(out[f * P : (f + 1) * P, :], out_sb[f][:])
+        def take(u, cut, turn=None):
+            whole = piece(0, N, turn)
+            interleave((W, u), whole, 0, cut, "scalar")
+            interleave((W, u), whole, cut, N, "vector")
+            freed()
+            return whole
+
+        def entries(e):
+            return offsets[:, e * C // 16 : (e + 1) * C // 16]
 
         load_next()
         nc.vector.memset(gate_rows[:], 0.0)
@@ -154,157 +175,181 @@ def tile_moe_nxt_lin_bias_kernel(tc, xT, w, b, wp, gate, offs, out):
         make_identity(nc, ident[:])
         for plane in x_planes:
             nc.vector.memset(plane[:].bitcast(I32), 0)
-        for f in range(OUT_TILES):
-            nc.vector.memset(out_sb[f][:], 0.0)
+        for u in range(2):
+            nc.vector.memset(c_tokens[u][:], 0.0)
         refill()
 
-        gate_turned = banks2.tile([P, P], F32, name="turned")
+        gate_turned = banks.tile([P, P], F32, name="bank2")
         nc.tensor.transpose(gate_turned[:], gate_rows[:], ident[:])
         nc.scalar.copy(gate_col[:], gate_turned[:, 0:E])
         spreads = []
         for e in range(E):
-            spread = banks1.tile([P, PACK, P], F32, name=f"bank{e}")
+            spread = banks.tile([P, PACK, P], F32, name=f"bank{(3, 4, 7, 0)[e]}")
             for a in range(PACK):
                 nc.tensor.transpose(spread[:, a, :], bias_sb[:, a, e : e + 1].to_broadcast([P, P]), ident[:])
             spreads.append(spread)
 
         def on_scalar(unit):
             kind, i = unit
-            if kind == "x":
+            if kind == X:
                 return T // 3 if i == 0 else 2 * T // 3
-            if unit == units[0]:
-                return 0
-            if kind == "w" and i < PASSES - 2:
-                return N
-            return HALF
+            return W_ON_SCALAR
 
-        early = units[: units.index(("w", PASSES - 1))]
         pieces, x_codes = {}, {}
-        for s in range(len(early) + 1):
+        for s in range(len(early) + 2):
             if s < len(early):
-                if early[s][0] == "x":
+                if early[s][0] == X:
                     pieces[s] = (0, T, pairs.tile([P, T, PACK], BF16, name="x_grouped", align_bytes=64))
                 else:
                     pieces[s] = piece(0, N)
                 cut = on_scalar(early[s])
-                if cut:
-                    interleave(early[s], pieces[s], 0, cut, "scalar")
-                if s > PASSES:
-                    e = s - PASSES - 1
+                interleave(early[s], pieces[s], 0, cut, "scalar")
+                if early[s][0] == W:
+                    e = early[s][1]
                     nc.scalar.activation(
                         gated_bias[e][:].rearrange("q (m a) -> q m a", a=PACK),
                         spreads[e][:].rearrange("q a m -> q m a"),
                         COPY,
                         scale=gate_col[:, e : e + 1],
                     )
-            if s >= 2 and early[s - 2][0] == "x":
+            if s >= 2 and early[s - 2][0] == X:
                 a = early[s - 2][1]
                 nc.vector.tensor_copy(s_codes[a][:], x_codes[a][:].indirect(offsets[:]))
                 if a % 4 == 3 or a == PASSES - 1:
                     nc.vector.tensor_copy(s_planes[a // 4][:], x_planes[a // 4][:].indirect(offsets[:]))
-            if s >= 1:
+            if 1 <= s <= len(early):
                 kind, i = early[s - 1]
                 grouped = pieces[s - 1][2]
-                if kind == "x":
+                if kind == X:
                     x_codes[i] = pairs.tile([P, T], U32, name="x_codes", align_bytes=64)
-                    for lo, hi in ((0, 2 * T // 3), (2 * T // 3, T)):
+                    for lo, hi in TOKEN_CUTS:
                         quantize(x_codes[i][:, lo:hi], x_planes[i // 4][4 * (i % 4) : P, lo:hi], grouped[:, lo:hi, :])
-                elif kind == "p":
-                    quantize(wp_codes[:], wp_scales[:], grouped[:])
                 else:
                     quantize_w(i, pieces[s - 1])
             if s < len(early):
-                if cut < pieces[s][1]:
-                    interleave(early[s], pieces[s], cut, pieces[s][1], "vector")
+                interleave(early[s], pieces[s], cut, pieces[s][1], "vector")
                 freed()
         for u in range(PASSES - 1):
             multiply(u, 0, N)
 
-        waiting = None
-        for e in range(E):
-            more = e < E - 1
-            closing = e * PASSES + PASSES - 1
-            u0, u1, u2, u3 = range(closing + 1, closing + PASSES)
-
-            lower = piece(0, HALF)
-            upper = piece(HALF, N, "before_gating" if more else None)
-            extra = 0 if more else LAST_EXTRA_ON_VECTOR
-            interleave(("w", closing), lower, 0, HALF, "vector")
-            if extra:
-                interleave(("w", closing), upper, HALF, HALF + extra, "vector")
-            interleave(("w", closing), upper, HALF + extra, N, "scalar")
-            freed()
-            use(closing, lower)
-            use(closing, upper)
-
-            if more:
-                pass0 = piece(0, N, "before_gating")
-                interleave(("w", u0), pass0, 0, GPSIMD_UNDER_GATING, "gpsimd")
-                interleave(("w", u0), pass0, GPSIMD_UNDER_GATING, N, "scalar")
-                freed()
-
+        def gate_and_turn(e):
             c_rows = pairs.tile([P, N], BF16, name="c_rows", align_bytes=64)
-            for h, (lo, hi) in enumerate(HALVES):
+            for h, (lo, hi) in enumerate(cuts(e)):
                 nc.vector.scalar_tensor_tensor(
                     c_rows[:, lo:hi], acc[e, h][:], gate_col[:, e : e + 1], gated_bias[e][:, lo:hi], MULT, ADD
                 )
-            turned = banks2.tile([P, 2, C], F32, name="turned")
+            turned = banks.tile([P, 2, C], F32, name="bank2")
             words = c_rows[:].bitcast(F32)
             for u in range(2):
                 nc.tensor.transpose(turned[:, u, :], words[:, u : N // 2 : 2], ident[:])
-            if waiting is not None:
-                o_last = turns.tile([P, C], F32, name=f"gated_bias{e}")
-                (nc.vector.tensor_copy if more else nc.scalar.copy)(o_last[:], waiting)
-                scatter(e - 1, OUT_TILES - 1, o_last[:])
-            c_grouped = turns.tile([P, C, PACK], BF16, name="c_first", align_bytes=64)
-            nc.scalar.copy(
-                c_grouped[:].rearrange("p s j -> p (s j)").bitcast(F32).rearrange("p (s u) -> p s u", u=2),
-                turned[:].rearrange("p u s -> p s u"),
-            )
-            c_codes = turns.tile([P, C], U32, name="projection_first", align_bytes=64)
-            c_scales = pairs.tile([P, C], U8, name="c_scales", align_bytes=64)
-            quantize(c_codes[:], c_scales[:], c_grouped[:])
+            return turned
 
-            first = banks1.tile([P, C], F32, name="bank2")
-            rest = banks1.tile([P, OUT_TILES - 1, C], F32, name="bank3")
-            for f in range(OUT_TILES):
-                cols = slice(f * P, (f + 1) * P)
-                nc.tensor.matmul_mx(
-                    out=first[:] if f == 0 else rest[:, f - 1, :],
-                    lhsT=wp_codes[:, cols].bitcast(FP8X4),
-                    lhsT_scale=wp_scales[:, cols],
-                    rhs=c_codes[:].bitcast(FP8X4),
-                    rhs_scale=c_scales[:],
-                    start=True,
-                    stop=True,
-                )
-            if more:
-                pass1_lower = piece(0, HALF, "before_scatters")
-                interleave(("w", u1), pass1_lower, 0, HALF, "scalar")
-                use(u0, pass0, "c_first")
+        for e in range(E - 1):
+            closing = e * PASSES + PASSES - 1
+            u0, u1, u2, u3 = range(closing + 1, closing + PASSES)
+            last = e == E - 2
+            use(closing, take(closing, W_ON_SCALAR_CLOSING if last else W_ON_SCALAR))
+            turned = gate_and_turn(e)
+            pass0 = take(u0, W_ON_SCALAR_CLOSING if last else W_ON_SCALAR, "before_scatters" if last else None)
+            c_words = pairs.tile([P, 2, C], F32, name="c_words")
+            nc.scalar.copy(c_words[:], turned[:])
+            use(u0, pass0)
+            for u in range(2):
+                nc.vector.tensor_copy(c_tokens[u][:].indirect(entries(e)), c_words[:, u, :])
+            if not last:
+                for u in (u1, u2, u3):
+                    use(u, take(u, W_ON_SCALAR))
+                continue
+            lower = piece(0, HALF, "before_scatters")
+            upper = piece(HALF, N)
+            interleave((W, u1), lower, 0, HALF, "gpsimd")
+            interleave((W, u1), upper, HALF, N, "scalar")
+            freed()
+            for u in range(2):
+                nc.scalar.copy(c_joined[:, u, :].bitcast(U32), c_tokens[u][:].bitcast(U32))
+            use(u1, lower)
+            use(u1, upper)
+            pass2 = take(u2, W_ON_SCALAR_LAST, "before_scatters")
+            t_grouped = held.tile([P, T, PACK], BF16, name="t_grouped", align_bytes=64)
+            t_words = t_grouped[:].rearrange("p t j -> p (t j)").bitcast(I32).rearrange("p (t u) -> p t u", u=2)
+            nc.vector.tensor_copy(t_words, c_joined[:].bitcast(I32).rearrange("p u t -> p t u"))
+            use(u2, pass2)
+            pass3 = take(u3, W_ON_SCALAR_LAST, "pass3")
+            use(u3, pass3)
 
-            now = OUT_TILES - 1 if more else OUT_TILES
-            o_first = pairs.tile([P, C], F32, name="o_first")
-            o_rest = pairs.tile([P, now - 1, C], F32, name="o_rest")
-            nc.scalar.copy(o_first[:], first[:])
-            nc.scalar.copy(o_rest[:], rest[:, 0 : now - 1, :])
-            waiting = rest[:, now - 1, :] if more else None
-            if more:
-                use(u1, pass1_lower)
-                pass1_upper = piece(HALF, N, "projection_first")
-                interleave(("w", u1), pass1_upper, HALF, N, "scalar")
-                freed()
-                pass2 = piece(0, N, "before_scatters")
-                interleave(("w", u2), pass2, 0, GPSIMD_UNDER_SCATTERS, "gpsimd")
-                interleave(("w", u2), pass2, GPSIMD_UNDER_SCATTERS, N, "scalar")
-                freed()
-            for f in range(now):
-                scatter(e, f, o_first[:] if f == 0 else o_rest[:, f - 1, :])
-            if more:
-                pass3 = piece(0, N)
-                interleave(("w", u3), pass3, 0, HALF, "scalar")
-                use(u1, pass1_upper)
-                interleave(("w", u3), pass3, HALF, N, "vector")
-                freed()
-                use(u2, pass2)
-                use(u3, pass3)
+        e = E - 1
+        closing = E * PASSES - 1
+        lower = piece(0, HALF, "last_lower")
+        upper = piece(HALF, N, "last_upper")
+        interleave((W, closing), lower, 0, HALF, "vector")
+        interleave((W, closing), upper, HALF, N, "scalar")
+        use(closing, lower)
+        use(closing, upper)
+
+        def quantize_tokens(part, turn):
+            lo, hi = TOKEN_CUTS[part]
+            t_codes[part] = turns.tile([P, hi - lo], U32, name=turn, align_bytes=64)
+            quantize(t_codes[part][:], t_scales[:, lo:hi], t_grouped[:, lo:hi, :])
+
+        quantize_tokens(1, "last_upper")
+        turned = gate_and_turn(e)
+
+        wp_pieces = {}
+
+        def prepare(f, engine, turn):
+            wp_pieces[f] = piece(f * P, (f + 1) * P, turn)
+            interleave(("p", 0), wp_pieces[f], f * P, (f + 1) * P, engine)
+
+        def quantize_wp(f):
+            quantize(wp_codes[:, f * P : (f + 1) * P], wp_scales[:, f * P : (f + 1) * P], wp_pieces[f][2][:])
+
+        token_banks = ((5, 6), (7, 0), (1, 2), (5, 6))
+
+        def project_tokens(f, part, engine):
+            cols = slice(f * P, (f + 1) * P)
+            lo, hi = TOKEN_CUTS[part]
+            sums = banks.tile([P, hi - lo], F32, name=f"bank{token_banks[f][part]}")
+            mx(sums[:], wp_codes[:, cols], wp_scales[:, cols], t_codes[part][:], t_scales[:, lo:hi])
+            (nc.vector.tensor_copy if engine == "vector" else nc.scalar.copy)(out_sb[f][:, lo:hi], sums[:])
+
+        c_grouped = held.tile([P, C, PACK], BF16, name="c_grouped", align_bytes=64)
+        c_codes = held.tile([P, C], U32, name="c_codes", align_bytes=64)
+        c_scales = held.tile([P, C], U8, name="c_scales", align_bytes=64)
+
+        def project_slots(f):
+            cols = slice(f * P, (f + 1) * P)
+            sums = banks.tile([P, C], F32, name=f"bank{3 + f % 2}")
+            mx(sums[:], wp_codes[:, cols], wp_scales[:, cols], c_codes[:], c_scales[:])
+            o_slots = pairs.tile([P, C], F32, name="o_slots")
+            nc.scalar.copy(o_slots[:], sums[:])
+            return o_slots
+
+        def finish(f, o_slots):
+            nc.vector.tensor_copy(out_sb[f][:].indirect(entries(e)), o_slots[:])
+            nc.sync.dma_start(out[f * P : (f + 1) * P, :], out_sb[f][:])
+
+        prepare(0, "scalar", "pass3")
+        prepare(1, "scalar", "before_scatters")
+        prepare(2, "gpsimd", "last_lower")
+        nc.scalar.copy(
+            c_grouped[:].rearrange("p s j -> p (s j)").bitcast(F32).rearrange("p (s u) -> p s u", u=2),
+            turned[:].rearrange("p u s -> p s u"),
+        )
+        quantize_wp(0)
+        quantize_tokens(0, f"gated_bias{e}")
+        quantize(c_codes[:], c_scales[:], c_grouped[:])
+        quantize_wp(1)
+        quantize_wp(2)
+        prepare(3, "gpsimd", "last_lower")
+        project_tokens(0, 1, "scalar")
+        project_tokens(0, 0, "scalar")
+        first = project_slots(0)
+        project_tokens(1, 1, "vector")
+        project_tokens(2, 1, "vector")
+        finish(0, first)
+        quantize_wp(3)
+        for f in range(1, OUT_TILES):
+            project_tokens(f, 0, "scalar")
+            if f == OUT_TILES - 1:
+                project_tokens(f, 1, "scalar")
+            finish(f, project_slots(f))

@@ -29,12 +29,13 @@ RUN = 4
 HALF = N // 2
 HALVES = ((0, HALF), (HALF, N))
 
-LOAD_BUFS = 9
+LOAD_BUFS = 7
 GROUPED_BUFS = 5
 CODE_BUFS = 7
 TOKEN_CUTS = ((0, 512), (512, T))
 W_ON_SCALAR = 352
-W_ON_SCALAR_CLOSING = 384
+W_ON_SCALAR_CLOSING = 320
+JOIN = T // PACK
 W_ON_SCALAR_LAST = 288
 
 
@@ -63,27 +64,34 @@ def tile_moe_nxt_lin_bias_kernel(tc, xT, w, b, wp, gate, offs, out):
         wp_codes = held.tile([P, M], U32, name="wp_codes", align_bytes=64)
         wp_scales = held.tile([P, M], U8, name="wp_scales", align_bytes=64)
         c_tokens = [held.tile([P, T], F32, name=f"c_tokens{u}") for u in range(2)]
-        c_joined = held.tile([P, 2, T], F32, name="c_joined")
         t_codes = {}
         t_scales = held.tile([P, T], U8, name="t_scales", align_bytes=64)
         out_sb = [held.tile([P, T], F32, name=f"out_sb{f}") for f in range(OUT_TILES)]
 
         X, W = "x", "w"
-        units = [(X, 0), (W, 0), (X, 1), (W, 1), (X, 2), (X, 3), (W, 2), (X, 4), (W, 3)]
+        units = [(X, 0), (W, 0), (W, 1), (X, 1), (X, 2), (X, 3), (W, 2), (W, 3), (X, 4)]
         early = list(units)
         units += [(W, u) for u in range(PASSES - 1, E * PASSES)] + [("p", 0)]
+        paired = range(0, (E - 1) * PASSES - 1, 2)
+        firsts = [n for n, (kind, i) in enumerate(units) if kind != W or i - 1 not in paired]
+        ends = firsts[1:] + [len(units)]
         raw, coded, acc = {}, {}, {}
         count = {"loaded": 0, "freed": 0}
 
         def load_next():
-            kind, i = unit = units[count["loaded"]]
-            rows = {"x": xT, "w": w_rows, "p": wp}[kind][i * K_PASS : (i + 1) * K_PASS, :]
-            raw[unit] = loads.tile([P, PACK, T if kind == "x" else N], F32, name="raw")
-            nc.sync.dma_start(raw[unit][:], rows.rearrange("(p j) c -> p j c", j=PACK))
+            g = count["loaded"]
+            size = ends[g] - firsts[g]
+            kind, i = units[firsts[g]]
+            rows = {"x": xT, "w": w_rows, "p": wp}[kind][i * K_PASS : (i + size) * K_PASS, :]
+            tile = loads.tile([P, size, PACK, T if kind == "x" else N], F32, name="raw")
+            nc.sync.dma_start(tile[:], rows.rearrange("(a p j) c -> p a j c", a=size, j=PACK))
+            for a in range(size):
+                raw[kind, i + a] = tile[:, a]
             count["loaded"] += 1
 
         def refill():
-            while count["loaded"] < len(units) and count["loaded"] - count["freed"] < LOAD_BUFS:
+            done = len([n for n in ends if n <= count["freed"]])
+            while count["loaded"] < len(ends) and count["loaded"] - done < LOAD_BUFS:
                 load_next()
 
         def freed():
@@ -140,7 +148,8 @@ def tile_moe_nxt_lin_bias_kernel(tc, xT, w, b, wp, gate, offs, out):
             for h, (c0, c1) in enumerate(cuts(e)):
                 if c0 < lo or c1 > hi:
                     continue
-                if a == 0:
+                opening = 2 if e == E - 1 else 0
+                if a == opening:
                     bank = h if e == E - 1 else 5 + e % 2
                     acc[e, h] = banks.tile([P, c1 - c0], F32, name=f"bank{bank}")
                 mx(
@@ -149,7 +158,7 @@ def tile_moe_nxt_lin_bias_kernel(tc, xT, w, b, wp, gate, offs, out):
                     s_planes[a // 4][4 * (a % 4) : P, slots],
                     codes[:, c0:c1],
                     plane[:, c0:c1],
-                    a == 0,
+                    a == opening,
                     a == PASSES - 1,
                 )
 
@@ -248,34 +257,40 @@ def tile_moe_nxt_lin_bias_kernel(tc, xT, w, b, wp, gate, offs, out):
             closing = e * PASSES + PASSES - 1
             u0, u1, u2, u3 = range(closing + 1, closing + PASSES)
             last = e == E - 2
-            use(closing, take(closing, W_ON_SCALAR_CLOSING if last else W_ON_SCALAR))
+            use(closing, take(closing, HALF if last else W_ON_SCALAR))
             turned = gate_and_turn(e)
             pass0 = take(u0, W_ON_SCALAR_CLOSING if last else W_ON_SCALAR, "before_scatters" if last else None)
             c_words = pairs.tile([P, 2, C], F32, name="c_words")
             nc.scalar.copy(c_words[:], turned[:])
-            use(u0, pass0)
+            if last:
+                quantize_w(u0, pass0)
+            else:
+                use(u0, pass0)
             for u in range(2):
                 nc.vector.tensor_copy(c_tokens[u][:].indirect(entries(e)), c_words[:, u, :])
             if not last:
                 for u in (u1, u2, u3):
                     use(u, take(u, W_ON_SCALAR))
                 continue
-            lower = piece(0, HALF, "before_scatters")
-            upper = piece(HALF, N)
-            interleave((W, u1), lower, 0, HALF, "gpsimd")
-            interleave((W, u1), upper, HALF, N, "scalar")
+            pass1 = piece(0, N, "before_scatters")
+            interleave((W, u1), pass1, JOIN, N, "gpsimd")
+            interleave((W, u1), pass1, 0, JOIN, "scalar")
             freed()
+            c_joined = raw[W, u1][:, :, 0 : 2 * JOIN]
             for u in range(2):
-                nc.scalar.copy(c_joined[:, u, :].bitcast(U32), c_tokens[u][:].bitcast(U32))
-            use(u1, lower)
-            use(u1, upper)
+                nc.scalar.copy(
+                    c_joined[:, :, u * JOIN : (u + 1) * JOIN], c_tokens[u][:].rearrange("p (r c) -> p r c", c=JOIN)
+                )
+            quantize_w(u1, pass1)
             pass2 = take(u2, W_ON_SCALAR_LAST, "before_scatters")
-            t_grouped = held.tile([P, T, PACK], BF16, name="t_grouped", align_bytes=64)
-            t_words = t_grouped[:].rearrange("p t j -> p (t j)").bitcast(I32).rearrange("p (t u) -> p t u", u=2)
-            nc.vector.tensor_copy(t_words, c_joined[:].bitcast(I32).rearrange("p u t -> p t u"))
+            t_grouped = pairs.tile([P, T, PACK], BF16, name="x_grouped", align_bytes=64)
+            t_words = t_grouped[:].rearrange("p t j -> p (t j)").bitcast(F32).rearrange("p (r c u) -> p r c u", c=JOIN, u=2)
+            nc.vector.tensor_copy(t_words, c_joined.rearrange("p r (u c) -> p r c u", u=2))
             use(u2, pass2)
+            multiply(u0, 0, N)
             pass3 = take(u3, W_ON_SCALAR_LAST, "pass3")
             use(u3, pass3)
+            multiply(u1, 0, N)
 
         e = E - 1
         closing = E * PASSES - 1

@@ -28,15 +28,22 @@ OUT_TILES = M // P
 RUN = 4
 HALF = N // 2
 HALVES = ((0, HALF), (HALF, N))
+LAST = E - 1
+LAST_OPENS_WITH = 2
 
 LOAD_BUFS = 7
 GROUPED_BUFS = 5
 CODE_BUFS = 7
 TOKEN_CUTS = ((0, 512), (512, T))
-W_ON_SCALAR = 352
-W_ON_SCALAR_CLOSING = 320
 JOIN = T // PACK
-W_ON_SCALAR_LAST = 288
+
+W_ON_SCALAR = 352
+W_ON_SCALAR_PASS0 = 272
+W_ON_SCALAR_LATE = 288
+
+TURN_BANK = 2
+BIAS_BANKS = (3, 4, 7, 0)
+TOKEN_BANKS = ((5, 6), (7, 0), (1, 2), (5, 6))
 
 
 def tile_moe_nxt_lin_bias_kernel(tc, xT, w, b, wp, gate, offs, out):
@@ -64,15 +71,13 @@ def tile_moe_nxt_lin_bias_kernel(tc, xT, w, b, wp, gate, offs, out):
         wp_codes = held.tile([P, M], U32, name="wp_codes", align_bytes=64)
         wp_scales = held.tile([P, M], U8, name="wp_scales", align_bytes=64)
         c_tokens = [held.tile([P, T], F32, name=f"c_tokens{u}") for u in range(2)]
-        t_codes = {}
         t_scales = held.tile([P, T], U8, name="t_scales", align_bytes=64)
         out_sb = [held.tile([P, T], F32, name=f"out_sb{f}") for f in range(OUT_TILES)]
 
-        X, W = "x", "w"
-        units = [(X, 0), (W, 0), (W, 1), (X, 1), (X, 2), (X, 3), (W, 2), (W, 3), (X, 4)]
-        early = list(units)
-        units += [(W, u) for u in range(PASSES - 1, E * PASSES)] + [("p", 0)]
-        paired = range(0, (E - 1) * PASSES - 1, 2)
+        X, W, WP = "x", "w", "wp"
+        early = [(X, 0), (W, 0), (W, 1), (X, 1), (X, 2), (X, 3), (W, 2), (W, 3), (X, 4)]
+        units = early + [(W, u) for u in range(PASSES - 1, E * PASSES)] + [(WP, 0)]
+        paired = range(0, LAST * PASSES - 1, 2)
         firsts = [n for n, (kind, i) in enumerate(units) if kind != W or i - 1 not in paired]
         ends = firsts[1:] + [len(units)]
         raw, coded, acc = {}, {}, {}
@@ -82,8 +87,8 @@ def tile_moe_nxt_lin_bias_kernel(tc, xT, w, b, wp, gate, offs, out):
             g = count["loaded"]
             size = ends[g] - firsts[g]
             kind, i = units[firsts[g]]
-            rows = {"x": xT, "w": w_rows, "p": wp}[kind][i * K_PASS : (i + size) * K_PASS, :]
-            tile = loads.tile([P, size, PACK, T if kind == "x" else N], F32, name="raw")
+            rows = {X: xT, W: w_rows, WP: wp}[kind][i * K_PASS : (i + size) * K_PASS, :]
+            tile = loads.tile([P, size, PACK, T if kind == X else N], F32, name="raw")
             nc.sync.dma_start(tile[:], rows.rearrange("(a p j) c -> p a j c", a=size, j=PACK))
             for a in range(size):
                 raw[kind, i + a] = tile[:, a]
@@ -139,18 +144,18 @@ def tile_moe_nxt_lin_bias_kernel(tc, xT, w, b, wp, gate, offs, out):
             )
 
         def cuts(e):
-            return HALVES if e == E - 1 else ((0, N),)
+            return HALVES if e >= LAST - 1 else ((0, N),)
 
         def multiply(u, lo, hi):
             e, a = divmod(u, PASSES)
+            opening = LAST_OPENS_WITH if e == LAST else 0
             codes, plane = coded[u]
             slots = slice(e * C, (e + 1) * C)
             for h, (c0, c1) in enumerate(cuts(e)):
                 if c0 < lo or c1 > hi:
                     continue
-                opening = 2 if e == E - 1 else 0
                 if a == opening:
-                    bank = h if e == E - 1 else 5 + e % 2
+                    bank = h if e == LAST else 5 + (e + h) % 2
                     acc[e, h] = banks.tile([P, c1 - c0], F32, name=f"bank{bank}")
                 mx(
                     acc[e, h][:],
@@ -188,12 +193,12 @@ def tile_moe_nxt_lin_bias_kernel(tc, xT, w, b, wp, gate, offs, out):
             nc.vector.memset(c_tokens[u][:], 0.0)
         refill()
 
-        gate_turned = banks.tile([P, P], F32, name="bank2")
+        gate_turned = banks.tile([P, P], F32, name=f"bank{TURN_BANK}")
         nc.tensor.transpose(gate_turned[:], gate_rows[:], ident[:])
         nc.scalar.copy(gate_col[:], gate_turned[:, 0:E])
         spreads = []
         for e in range(E):
-            spread = banks.tile([P, PACK, P], F32, name=f"bank{(3, 4, 7, 0)[e]}")
+            spread = banks.tile([P, PACK, P], F32, name=f"bank{BIAS_BANKS[e]}")
             for a in range(PACK):
                 nc.tensor.transpose(spread[:, a, :], bias_sb[:, a, e : e + 1].to_broadcast([P, P]), ident[:])
             spreads.append(spread)
@@ -247,89 +252,97 @@ def tile_moe_nxt_lin_bias_kernel(tc, xT, w, b, wp, gate, offs, out):
                 nc.vector.scalar_tensor_tensor(
                     c_rows[:, lo:hi], acc[e, h][:], gate_col[:, e : e + 1], gated_bias[e][:, lo:hi], MULT, ADD
                 )
-            turned = banks.tile([P, 2, C], F32, name="bank2")
+            turned = banks.tile([P, 2, C], F32, name=f"bank{TURN_BANK}")
             words = c_rows[:].bitcast(F32)
             for u in range(2):
                 nc.tensor.transpose(turned[:, u, :], words[:, u : N // 2 : 2], ident[:])
             return turned
 
-        for e in range(E - 1):
-            closing = e * PASSES + PASSES - 1
-            u0, u1, u2, u3 = range(closing + 1, closing + PASSES)
-            last = e == E - 2
-            use(closing, take(closing, HALF if last else W_ON_SCALAR))
-            turned = gate_and_turn(e)
-            pass0 = take(u0, W_ON_SCALAR_CLOSING if last else W_ON_SCALAR, "before_scatters" if last else None)
+        def pairs_to_sbuf(turned):
             c_words = pairs.tile([P, 2, C], F32, name="c_words")
             nc.scalar.copy(c_words[:], turned[:])
-            if last:
-                quantize_w(u0, pass0)
-            else:
-                use(u0, pass0)
+            return c_words
+
+        def scatter_pairs(e, c_words):
             for u in range(2):
                 nc.vector.tensor_copy(c_tokens[u][:].indirect(entries(e)), c_words[:, u, :])
-            if not last:
-                for u in (u1, u2, u3):
-                    use(u, take(u, W_ON_SCALAR))
-                continue
-            pass1 = piece(0, N, "before_scatters")
-            interleave((W, u1), pass1, JOIN, N, "gpsimd")
-            interleave((W, u1), pass1, 0, JOIN, "scalar")
-            freed()
-            c_joined = raw[W, u1][:, :, 0 : 2 * JOIN]
-            for u in range(2):
-                nc.scalar.copy(
-                    c_joined[:, :, u * JOIN : (u + 1) * JOIN], c_tokens[u][:].rearrange("p (r c) -> p r c", c=JOIN)
-                )
-            quantize_w(u1, pass1)
-            pass2 = take(u2, W_ON_SCALAR_LAST, "before_scatters")
-            t_grouped = pairs.tile([P, T, PACK], BF16, name="x_grouped", align_bytes=64)
-            t_words = t_grouped[:].rearrange("p t j -> p (t j)").bitcast(F32).rearrange("p (r c u) -> p r c u", c=JOIN, u=2)
-            nc.vector.tensor_copy(t_words, c_joined.rearrange("p r (u c) -> p r c u", u=2))
-            use(u2, pass2)
-            multiply(u0, 0, N)
-            pass3 = take(u3, W_ON_SCALAR_LAST, "pass3")
-            use(u3, pass3)
-            multiply(u1, 0, N)
 
-        e = E - 1
-        closing = E * PASSES - 1
+        for e in range(LAST - 1):
+            closing = e * PASSES + PASSES - 1
+            use(closing, take(closing, W_ON_SCALAR))
+            turned = gate_and_turn(e)
+            pass0 = take(closing + 1, W_ON_SCALAR)
+            c_words = pairs_to_sbuf(turned)
+            use(closing + 1, pass0)
+            scatter_pairs(e, c_words)
+            for u in range(closing + 2, closing + PASSES):
+                use(u, take(u, W_ON_SCALAR))
+
+        u0, u1, u2, u3, u4 = range(LAST * PASSES, E * PASSES)
+        lower = piece(0, HALF)
+        upper = piece(HALF, N)
+        interleave((W, u0 - 1), lower, 0, HALF, "vector")
+        interleave((W, u0 - 1), upper, HALF, N, "scalar")
+        freed()
+        use(u0 - 1, lower)
+        use(u0 - 1, upper)
+        turned = gate_and_turn(LAST - 1)
+        pass0 = take(u0, W_ON_SCALAR_PASS0, "before_scatters")
+        c_words = pairs_to_sbuf(turned)
+        quantize_w(u0, pass0)
+        scatter_pairs(LAST - 1, c_words)
+
+        pass1 = piece(0, N, "before_scatters")
+        interleave((W, u1), pass1, JOIN, N, "gpsimd")
+        interleave((W, u1), pass1, 0, JOIN, "scalar")
+        freed()
+
+        c_joined = raw[W, u1][:, :, 0 : 2 * JOIN]
+        for u in range(2):
+            nc.scalar.copy(
+                c_joined[:, :, u * JOIN : (u + 1) * JOIN], c_tokens[u][:].rearrange("p (r i) -> p r i", i=JOIN)
+            )
+        quantize_w(u1, pass1)
+        pass2 = take(u2, W_ON_SCALAR_LATE, "before_scatters")
+        t_grouped = pairs.tile([P, T, PACK], BF16, name="x_grouped", align_bytes=64)
+        t_words = t_grouped[:].rearrange("p t j -> p (t j)").bitcast(F32)
+        nc.vector.tensor_copy(
+            t_words.rearrange("p (r i u) -> p r i u", i=JOIN, u=2), c_joined.rearrange("p r (u i) -> p r i u", u=2)
+        )
+
+        use(u2, pass2)
+        multiply(u0, 0, N)
+        pass3 = take(u3, W_ON_SCALAR_LATE, "pass3")
+        use(u3, pass3)
+        multiply(u1, 0, N)
+
         lower = piece(0, HALF, "last_lower")
         upper = piece(HALF, N, "last_upper")
-        interleave((W, closing), lower, 0, HALF, "vector")
-        interleave((W, closing), upper, HALF, N, "scalar")
-        use(closing, lower)
-        use(closing, upper)
+        interleave((W, u4), lower, 0, HALF, "vector")
+        interleave((W, u4), upper, HALF, N, "scalar")
+        use(u4, lower)
+        use(u4, upper)
+
+        t_codes, wp_pieces = {}, {}
 
         def quantize_tokens(part, turn):
             lo, hi = TOKEN_CUTS[part]
             t_codes[part] = turns.tile([P, hi - lo], U32, name=turn, align_bytes=64)
             quantize(t_codes[part][:], t_scales[:, lo:hi], t_grouped[:, lo:hi, :])
 
-        quantize_tokens(1, "last_upper")
-        turned = gate_and_turn(e)
-
-        wp_pieces = {}
-
-        def prepare(f, engine, turn):
+        def interleave_wp(f, engine, turn):
             wp_pieces[f] = piece(f * P, (f + 1) * P, turn)
-            interleave(("p", 0), wp_pieces[f], f * P, (f + 1) * P, engine)
+            interleave((WP, 0), wp_pieces[f], f * P, (f + 1) * P, engine)
 
         def quantize_wp(f):
             quantize(wp_codes[:, f * P : (f + 1) * P], wp_scales[:, f * P : (f + 1) * P], wp_pieces[f][2][:])
 
-        token_banks = ((5, 6), (7, 0), (1, 2), (5, 6))
-
         def project_tokens(f, part, engine):
             cols = slice(f * P, (f + 1) * P)
             lo, hi = TOKEN_CUTS[part]
-            sums = banks.tile([P, hi - lo], F32, name=f"bank{token_banks[f][part]}")
+            sums = banks.tile([P, hi - lo], F32, name=f"bank{TOKEN_BANKS[f][part]}")
             mx(sums[:], wp_codes[:, cols], wp_scales[:, cols], t_codes[part][:], t_scales[:, lo:hi])
             (nc.vector.tensor_copy if engine == "vector" else nc.scalar.copy)(out_sb[f][:, lo:hi], sums[:])
-
-        c_grouped = held.tile([P, C, PACK], BF16, name="c_grouped", align_bytes=64)
-        c_codes = held.tile([P, C], U32, name="c_codes", align_bytes=64)
-        c_scales = held.tile([P, C], U8, name="c_scales", align_bytes=64)
 
         def project_slots(f):
             cols = slice(f * P, (f + 1) * P)
@@ -340,22 +353,29 @@ def tile_moe_nxt_lin_bias_kernel(tc, xT, w, b, wp, gate, offs, out):
             return o_slots
 
         def finish(f, o_slots):
-            nc.vector.tensor_copy(out_sb[f][:].indirect(entries(e)), o_slots[:])
+            nc.vector.tensor_copy(out_sb[f][:].indirect(entries(LAST)), o_slots[:])
             nc.sync.dma_start(out[f * P : (f + 1) * P, :], out_sb[f][:])
 
-        prepare(0, "scalar", "pass3")
-        prepare(1, "scalar", "before_scatters")
-        prepare(2, "gpsimd", "last_lower")
+        quantize_tokens(1, "last_upper")
+        turned = gate_and_turn(LAST)
+        c_grouped = held.tile([P, C, PACK], BF16, name="c_grouped", align_bytes=64)
+        c_codes = held.tile([P, C], U32, name="c_codes", align_bytes=64)
+        c_scales = held.tile([P, C], U8, name="c_scales", align_bytes=64)
+
+        interleave_wp(0, "scalar", "pass3")
+        interleave_wp(1, "scalar", "before_scatters")
+        interleave_wp(2, "gpsimd", "last_lower")
         nc.scalar.copy(
             c_grouped[:].rearrange("p s j -> p (s j)").bitcast(F32).rearrange("p (s u) -> p s u", u=2),
             turned[:].rearrange("p u s -> p s u"),
         )
         quantize_wp(0)
-        quantize_tokens(0, f"gated_bias{e}")
+        quantize_tokens(0, f"gated_bias{LAST}")
         quantize(c_codes[:], c_scales[:], c_grouped[:])
         quantize_wp(1)
         quantize_wp(2)
-        prepare(3, "gpsimd", "last_lower")
+        interleave_wp(3, "gpsimd", "last_lower")
+
         project_tokens(0, 1, "scalar")
         project_tokens(0, 0, "scalar")
         first = project_slots(0)

@@ -77,7 +77,7 @@ def tile_moe_nxt_lin_bias_kernel(tc, xT, w, b, wp, gate, offs, out):
         X, W, WP = "x", "w", "wp"
         early = [(X, 0), (W, 0), (W, 1), (X, 1), (X, 2), (X, 3), (W, 2), (W, 3), (X, 4)]
         units = early + [(W, u) for u in range(PASSES - 1, E * PASSES)] + [(WP, 0)]
-        paired = range(0, LAST * PASSES - 1, 2)
+        paired = range(0, PASSES - 1, 2)
         firsts = [n for n, (kind, i) in enumerate(units) if kind != W or i - 1 not in paired]
         ends = firsts[1:] + [len(units)]
         raw, coded, acc = {}, {}, {}

@@ -26,29 +26,23 @@ PASSES = K // K_PASS
 SLOTS = E * C
 OUT_TILES = M // P
 RUN = 4
-HALF = N // 2
-HALVES = ((0, HALF), (HALF, N))
+JOIN = 2 * RUN
 LAST = E - 1
 LAST_OPENS_WITH = 2
 
 LOAD_BUFS = 7
-GROUPED_BUFS = 5
+GROUPED_BUFS = 4
 CODE_BUFS = 7
 TOKEN_CUTS = ((0, 512), (512, T))
-JOIN = T // PACK
 
-W_ON_SCALAR = 352
-W_ON_SCALAR_PASS0 = 272
-W_ON_SCALAR_LATE = 288
-
-TURN_BANK = 2
-BIAS_BANKS = (3, 4, 7, 0)
-TOKEN_BANKS = ((5, 6), (7, 0), (1, 2), (5, 6))
+TOKEN_BANKS = ((0, 1), (2, 3), (4, 1), (5, 6))
+SLOT_BANKS = (4, 0)
 
 
 def tile_moe_nxt_lin_bias_kernel(tc, xT, w, b, wp, gate, offs, out):
     nc = tc.nc
     w_rows = w.rearrange("e k n -> (e k) n")
+    on_vector, on_scalar = nc.vector.tensor_copy, nc.scalar.copy
 
     with ExitStack() as ctx:
         held = ctx.enter_context(tc.tile_pool(name="held", bufs=1))
@@ -63,14 +57,12 @@ def tile_moe_nxt_lin_bias_kernel(tc, xT, w, b, wp, gate, offs, out):
         ident = held.tile([P, P], F32, name="ident")
         gate_rows = held.tile([P, C], F32, name="gate_rows")
         gate_col = held.tile([P, E], F32, name="gate_col")
-        bias_sb = held.tile([P, PACK, E], F32, name="bias_sb")
-        gated_bias = [turns.tile([P, N], F32, name=f"gated_bias{e}", align_bytes=64) for e in range(E)]
+        gate_all = held.tile([P, E, C], F32, name="gate_all")
+        bias_sb = [turns.tile([P, E], F32, name=f"bias_sb{t}", align_bytes=64) for t in range(PACK)]
         x_planes = [held.tile([P, T], U8, name=f"x_planes{i}", align_bytes=64) for i in range(2)]
         s_codes = [held.tile([P, SLOTS], U32, name=f"s_codes{a}", align_bytes=64) for a in range(PASSES)]
         s_planes = [held.tile([P, SLOTS], U8, name=f"s_planes{i}", align_bytes=64) for i in range(2)]
-        wp_codes = held.tile([P, M], U32, name="wp_codes", align_bytes=64)
-        wp_scales = held.tile([P, M], U8, name="wp_scales", align_bytes=64)
-        c_tokens = [held.tile([P, T], F32, name=f"c_tokens{u}") for u in range(2)]
+        c_tokens = [turns.tile([P, T], F32, name=f"c_tokens{u}", align_bytes=64) for u in range(2)]
         t_scales = held.tile([P, T], U8, name="t_scales", align_bytes=64)
         out_sb = [held.tile([P, T], F32, name=f"out_sb{f}") for f in range(OUT_TILES)]
 
@@ -87,9 +79,14 @@ def tile_moe_nxt_lin_bias_kernel(tc, xT, w, b, wp, gate, offs, out):
             g = count["loaded"]
             size = ends[g] - firsts[g]
             kind, i = units[firsts[g]]
-            rows = {X: xT, W: w_rows, WP: wp}[kind][i * K_PASS : (i + size) * K_PASS, :]
             tile = loads.tile([P, size, PACK, T if kind == X else N], F32, name="raw")
-            nc.sync.dma_start(tile[:], rows.rearrange("(a p j) c -> p a j c", a=size, j=PACK))
+            if kind == WP:
+                rows = wp.rearrange("(c t i) f -> t c i f", t=PACK, i=RUN)
+                for t in range(PACK):
+                    nc.sync.dma_start(tile[:, 0, t, :], rows[t])
+            else:
+                rows = {X: xT, W: w_rows}[kind][i * K_PASS : (i + size) * K_PASS, :]
+                nc.sync.dma_start(tile[:], rows.rearrange("(a p j) c -> p a j c", a=size, j=PACK))
             for a in range(size):
                 raw[kind, i + a] = tile[:, a]
             count["loaded"] += 1
@@ -110,27 +107,32 @@ def tile_moe_nxt_lin_bias_kernel(tc, xT, w, b, wp, gate, offs, out):
 
         def interleave(unit, into, lo, hi, engine):
             dst = into[2][:, lo - into[0] : hi - into[0], :]
-            src = raw[unit][:, :, lo:hi]
-            if engine == "gpsimd":
-                nc.gpsimd.tensor_scalar(dst, src.rearrange("p j c -> p c j"), 1.0, 0.0, MULT, ADD)
-                return
-            dst = dst.rearrange("p (c i) j -> p c j i", i=RUN)
-            src = src.rearrange("p j (c i) -> p c j i", i=RUN)
-            if engine == "vector":
-                nc.vector.tensor_copy(dst, src)
+            if unit[0] == W:
+                src = raw[unit].rearrange("p j (c t i) -> p t c j i", t=PACK, i=RUN)[:, lo // P : hi // P]
+                dst = dst.rearrange("p (t c i) j -> p t c j i", c=P // RUN, i=RUN)
             else:
-                nc.scalar.copy(dst, src)
+                src = raw[unit][:, :, lo:hi].rearrange("p j (t c i) -> p t c j i", c=P // RUN, i=RUN)
+                dst = dst.rearrange("p (t c i) j -> p t c j i", c=P // RUN, i=RUN)
+            if engine == "gpsimd":
+                for t in range((hi - lo) // P):
+                    nc.gpsimd.tensor_scalar(
+                        dst[:, t].rearrange("p c j i -> p c i j"), src[:, t].rearrange("p c j i -> p c i j"),
+                        1.0, 0.0, MULT, ADD,
+                    )
+            elif engine == "vector":
+                on_vector(dst, src)
+            else:
+                on_scalar(dst, src)
 
         def quantize(codes, scales, grouped):
             nc.vector.quantize_mx(out=codes.bitcast(FP8X4), scales=scales, in_=grouped.rearrange("p c j -> p (c j)"))
 
-        def quantize_w(u, source):
-            lo, hi, grouped = source
+        def quantize_w(u, source, lo=0, hi=N, turn=None):
             if u not in coded:
-                codes = code_pool.tile([P, N], U32, name="w_codes", align_bytes=64)
+                codes = (turns if turn else code_pool).tile([P, N], U32, name=turn or "w_codes", align_bytes=64)
                 plane = code_pool.tile([P, N], U8, name="w_plane", align_bytes=64)
                 coded[u] = (codes, plane)
-            quantize(coded[u][0][:, lo:hi], coded[u][1][:, lo:hi], grouped[:])
+            quantize(coded[u][0][:, lo:hi], coded[u][1][:, lo:hi], source[2][:, lo - source[0] : hi - source[0], :])
 
         def mx(dst, lhs, lhs_scale, rhs, rhs_scale, start=True, stop=True):
             nc.tensor.matmul_mx(
@@ -143,38 +145,33 @@ def tile_moe_nxt_lin_bias_kernel(tc, xT, w, b, wp, gate, offs, out):
                 stop=stop,
             )
 
-        def cuts(e):
-            return HALVES if e >= LAST - 1 else ((0, N),)
-
-        def multiply(u, lo, hi):
+        def multiply(u, quarters=range(PACK)):
             e, a = divmod(u, PASSES)
             opening = LAST_OPENS_WITH if e == LAST else 0
             codes, plane = coded[u]
             slots = slice(e * C, (e + 1) * C)
-            for h, (c0, c1) in enumerate(cuts(e)):
-                if c0 < lo or c1 > hi:
-                    continue
+            for t in quarters:
                 if a == opening:
-                    bank = h if e == LAST else 5 + (e + h) % 2
-                    acc[e, h] = banks.tile([P, c1 - c0], F32, name=f"bank{bank}")
+                    acc[e, t] = banks.tile([P, C], F32, name=f"bank{PACK * (e % 2) + t}")
+                cols = slice(t * P, (t + 1) * P)
                 mx(
-                    acc[e, h][:],
+                    acc[e, t][:],
+                    codes[:, cols],
+                    plane[:, cols],
                     s_codes[a][:, slots],
                     s_planes[a // 4][4 * (a % 4) : P, slots],
-                    codes[:, c0:c1],
-                    plane[:, c0:c1],
                     a == opening,
                     a == PASSES - 1,
                 )
 
         def use(u, source):
             quantize_w(u, source)
-            multiply(u, source[0], source[1])
+            multiply(u)
 
-        def take(u, cut, turn=None):
+        def take(u, quarters, turn=None, other="vector"):
             whole = piece(0, N, turn)
-            interleave((W, u), whole, 0, cut, "scalar")
-            interleave((W, u), whole, cut, N, "vector")
+            interleave((W, u), whole, 0, quarters * P, "scalar")
+            interleave((W, u), whole, quarters * P, N, other)
             freed()
             return whole
 
@@ -184,7 +181,6 @@ def tile_moe_nxt_lin_bias_kernel(tc, xT, w, b, wp, gate, offs, out):
         load_next()
         nc.vector.memset(gate_rows[:], 0.0)
         nc.sync.dma_start(gate_rows[0:E, :], gate[0:1, :].rearrange("o (e c) -> (o e) c", c=C))
-        nc.sync.dma_start(bias_sb[:], b.rearrange("(p a) e -> p a e", a=PACK))
         nc.sync.dma_start(offsets[:], offs)
         make_identity(nc, ident[:])
         for plane in x_planes:
@@ -192,22 +188,23 @@ def tile_moe_nxt_lin_bias_kernel(tc, xT, w, b, wp, gate, offs, out):
         for u in range(2):
             nc.vector.memset(c_tokens[u][:], 0.0)
         refill()
+        b_rows = b.rearrange("(c t i) e -> t c i e", t=PACK, i=RUN)
+        for t in range(PACK):
+            nc.sync.dma_start(bias_sb[t][:], b_rows[t])
 
-        gate_turned = banks.tile([P, P], F32, name=f"bank{TURN_BANK}")
+        gate_turned = banks.tile([P, P], F32, name="bank0")
         nc.tensor.transpose(gate_turned[:], gate_rows[:], ident[:])
-        nc.scalar.copy(gate_col[:], gate_turned[:, 0:E])
-        spreads = []
+        on_scalar(gate_col[:], gate_turned[:, 0:E])
+        spread = banks.tile([P, E, C], F32, name="bank1")
         for e in range(E):
-            spread = banks.tile([P, PACK, P], F32, name=f"bank{BIAS_BANKS[e]}")
-            for a in range(PACK):
-                nc.tensor.transpose(spread[:, a, :], bias_sb[:, a, e : e + 1].to_broadcast([P, P]), ident[:])
-            spreads.append(spread)
+            nc.tensor.transpose(spread[:, e, :], gate_col[:, e : e + 1].to_broadcast([P, P]), ident[:])
+        on_scalar(gate_all[:], spread[:])
 
-        def on_scalar(unit):
+        def scalar_share(unit):
             kind, i = unit
             if kind == X:
                 return T // 3 if i == 0 else 2 * T // 3
-            return W_ON_SCALAR
+            return 3 * P
 
         pieces, x_codes = {}, {}
         for s in range(len(early) + 2):
@@ -216,21 +213,13 @@ def tile_moe_nxt_lin_bias_kernel(tc, xT, w, b, wp, gate, offs, out):
                     pieces[s] = (0, T, pairs.tile([P, T, PACK], BF16, name="x_grouped", align_bytes=64))
                 else:
                     pieces[s] = piece(0, N)
-                cut = on_scalar(early[s])
+                cut = scalar_share(early[s])
                 interleave(early[s], pieces[s], 0, cut, "scalar")
-                if early[s][0] == W:
-                    e = early[s][1]
-                    nc.scalar.activation(
-                        gated_bias[e][:].rearrange("q (m a) -> q m a", a=PACK),
-                        spreads[e][:].rearrange("q a m -> q m a"),
-                        COPY,
-                        scale=gate_col[:, e : e + 1],
-                    )
             if s >= 2 and early[s - 2][0] == X:
                 a = early[s - 2][1]
-                nc.vector.tensor_copy(s_codes[a][:], x_codes[a][:].indirect(offsets[:]))
+                on_vector(s_codes[a][:], x_codes[a][:].indirect(offsets[:]))
                 if a % 4 == 3 or a == PASSES - 1:
-                    nc.vector.tensor_copy(s_planes[a // 4][:], x_planes[a // 4][:].indirect(offsets[:]))
+                    on_vector(s_planes[a // 4][:], x_planes[a // 4][:].indirect(offsets[:]))
             if 1 <= s <= len(early):
                 kind, i = early[s - 1]
                 grouped = pieces[s - 1][2]
@@ -244,147 +233,142 @@ def tile_moe_nxt_lin_bias_kernel(tc, xT, w, b, wp, gate, offs, out):
                 interleave(early[s], pieces[s], cut, pieces[s][1], "vector")
                 freed()
         for u in range(PASSES - 1):
-            multiply(u, 0, N)
+            multiply(u)
 
-        def gate_and_turn(e):
-            c_rows = pairs.tile([P, N], BF16, name="c_rows", align_bytes=64)
-            for h, (lo, hi) in enumerate(cuts(e)):
-                nc.vector.scalar_tensor_tensor(
-                    c_rows[:, lo:hi], acc[e, h][:], gate_col[:, e : e + 1], gated_bias[e][:, lo:hi], MULT, ADD
-                )
-            turned = banks.tile([P, 2, C], F32, name=f"bank{TURN_BANK}")
-            words = c_rows[:].bitcast(F32)
+        def gated(e, t, dst):
+            nc.vector.scalar_tensor_tensor(dst, acc[e, t][:], bias_sb[t][:, e : e + 1], gate_all[:, e, :], ADD, MULT)
+
+        def gate_into_pairs(e):
+            c_pairs = [turns.tile([P, C, 2], BF16, name=f"c_pairs{u}", align_bytes=64) for u in range(2)]
+            for t in range(PACK):
+                gated(e, t, c_pairs[t // 2][:, :, t % 2])
+            return c_pairs
+
+        def scatter_pairs(e, c_pairs):
             for u in range(2):
-                nc.tensor.transpose(turned[:, u, :], words[:, u : N // 2 : 2], ident[:])
-            return turned
-
-        def pairs_to_sbuf(turned):
-            c_words = pairs.tile([P, 2, C], F32, name="c_words")
-            nc.scalar.copy(c_words[:], turned[:])
-            return c_words
-
-        def scatter_pairs(e, c_words):
-            for u in range(2):
-                nc.vector.tensor_copy(c_tokens[u][:].indirect(entries(e)), c_words[:, u, :])
+                on_vector(c_tokens[u][:].indirect(entries(e)), c_pairs[u][:].rearrange("p s h -> p (s h)").bitcast(F32))
 
         for e in range(LAST - 1):
             closing = e * PASSES + PASSES - 1
-            use(closing, take(closing, W_ON_SCALAR))
-            turned = gate_and_turn(e)
-            pass0 = take(closing + 1, W_ON_SCALAR)
-            c_words = pairs_to_sbuf(turned)
-            use(closing + 1, pass0)
-            scatter_pairs(e, c_words)
+            use(closing, take(closing, 3))
+            c_pairs = gate_into_pairs(e)
+            use(closing + 1, take(closing + 1, 3))
+            scatter_pairs(e, c_pairs)
             for u in range(closing + 2, closing + PASSES):
-                use(u, take(u, W_ON_SCALAR))
+                use(u, take(u, 3))
+
+        def split(u, quarters, scalar_turn, other_turn):
+            lower = piece(0, quarters * P, scalar_turn)
+            upper = piece(quarters * P, N, other_turn)
+            interleave((W, u), lower, 0, quarters * P, "scalar")
+            interleave((W, u), upper, quarters * P, N, "vector")
+            freed()
+            return lower, upper
+
+        def quantize_both(u, parts, turn=None):
+            for part in reversed(parts):
+                quantize_w(u, part, part[0], part[1], turn)
+
+        def close_by_quarters(u, lower_turn, upper_turn):
+            lower = piece(0, N // 2, lower_turn)
+            upper = piece(N // 2, N, upper_turn)
+            for t in range(PACK):
+                interleave((W, u), upper if t >= 2 else lower, t * P, (t + 1) * P, "scalar" if t >= 2 else "vector")
+            freed()
+            for t in range(PACK):
+                quantize_w(u, upper if t >= 2 else lower, t * P, (t + 1) * P)
+                multiply(u, [t])
 
         u0, u1, u2, u3, u4 = range(LAST * PASSES, E * PASSES)
-        lower = piece(0, HALF)
-        upper = piece(HALF, N)
-        interleave((W, u0 - 1), lower, 0, HALF, "vector")
-        interleave((W, u0 - 1), upper, HALF, N, "scalar")
+        close_by_quarters(u0 - 1, None, "before_scatters")
+        scatter_pairs(LAST - 1, gate_into_pairs(LAST - 1))
+        pass0 = (piece(0, N // 2, "before_scatters"), piece(N // 2, N))
+        interleave((W, u0), pass0[0], 0, N // 2, "gpsimd")
+        interleave((W, u0), pass0[1], N // 2, N, "scalar")
         freed()
-        use(u0 - 1, lower)
-        use(u0 - 1, upper)
-        turned = gate_and_turn(LAST - 1)
-        pass0 = take(u0, W_ON_SCALAR_PASS0, "before_scatters")
-        c_words = pairs_to_sbuf(turned)
-        quantize_w(u0, pass0)
-        scatter_pairs(LAST - 1, c_words)
-
-        pass1 = piece(0, N, "before_scatters")
-        interleave((W, u1), pass1, JOIN, N, "gpsimd")
-        interleave((W, u1), pass1, 0, JOIN, "scalar")
-        freed()
-
-        c_joined = raw[W, u1][:, :, 0 : 2 * JOIN]
+        c_joined = raw[W, u0].rearrange("p j (c u i) -> p (j c) u i", u=2, i=JOIN)[:, 0 : T // JOIN]
         for u in range(2):
-            nc.scalar.copy(
-                c_joined[:, :, u * JOIN : (u + 1) * JOIN], c_tokens[u][:].rearrange("p (r i) -> p r i", i=JOIN)
-            )
-        quantize_w(u1, pass1)
-        pass2 = take(u2, W_ON_SCALAR_LATE, "before_scatters")
-        t_grouped = pairs.tile([P, T, PACK], BF16, name="x_grouped", align_bytes=64)
+            on_scalar(c_joined[:, :, u, :], c_tokens[u][:].rearrange("p (r i) -> p r i", i=JOIN))
+        quantize_both(u0, pass0)
+        pass1 = split(u1, 2, "scalar_a", "vector_a")
+        t_grouped = turns.tile([P, T, PACK], BF16, name="t_grouped", align_bytes=64)
         t_words = t_grouped[:].rearrange("p t j -> p (t j)").bitcast(F32)
-        nc.vector.tensor_copy(
-            t_words.rearrange("p (r i u) -> p r i u", i=JOIN, u=2), c_joined.rearrange("p r (u i) -> p r i u", u=2)
-        )
+        on_vector(t_words.rearrange("p (r i u) -> p r i u", i=JOIN, u=2), c_joined.rearrange("p r u i -> p r i u"))
+        quantize_both(u1, pass1)
+        t_codes = pairs.tile([P, T], U32, name="x_codes", align_bytes=64)
+        for lo, hi in TOKEN_CUTS:
+            quantize(t_codes[:, lo:hi], t_scales[:, lo:hi], t_grouped[:, lo:hi, :])
 
-        use(u2, pass2)
-        multiply(u0, 0, N)
-        pass3 = take(u3, W_ON_SCALAR_LATE, "pass3")
-        use(u3, pass3)
-        multiply(u1, 0, N)
+        quantize_both(u2, split(u2, 3, None, None))
+        multiply(u2)
+        multiply(u0)
+        quantize_both(u3, split(u3, 2, None, None))
+        multiply(u3)
+        multiply(u1)
+        close_by_quarters(u4, "vector_a", "scalar_a")
+        c_planes = turns.tile([P, PACK, C], BF16, name="c_planes", align_bytes=64)
+        for t in range(PACK):
+            gated(LAST, t, c_planes[:, t, :])
 
-        lower = piece(0, HALF, "last_lower")
-        upper = piece(HALF, N, "last_upper")
-        interleave((W, u4), lower, 0, HALF, "vector")
-        interleave((W, u4), upper, HALF, N, "scalar")
-        use(u4, lower)
-        use(u4, upper)
-
-        t_codes, wp_pieces = {}, {}
-
-        def quantize_tokens(part, turn):
-            lo, hi = TOKEN_CUTS[part]
-            t_codes[part] = turns.tile([P, hi - lo], U32, name=turn, align_bytes=64)
-            quantize(t_codes[part][:], t_scales[:, lo:hi], t_grouped[:, lo:hi, :])
+        wp_pieces, wp_coded, o_slots = {}, {}, {}
 
         def interleave_wp(f, engine, turn):
             wp_pieces[f] = piece(f * P, (f + 1) * P, turn)
             interleave((WP, 0), wp_pieces[f], f * P, (f + 1) * P, engine)
 
         def quantize_wp(f):
-            quantize(wp_codes[:, f * P : (f + 1) * P], wp_scales[:, f * P : (f + 1) * P], wp_pieces[f][2][:])
+            codes = turns.tile([P, P], U32, name=("bias_sb2", "c_planes", "wp_codes2", "c_planes")[f], align_bytes=64)
+            plane = held.tile([P, P], U8, name=f"wp_plane{f}", align_bytes=64)
+            wp_coded[f] = (codes[:], plane[:])
+            quantize(codes[:], plane[:], wp_pieces[f][2][:])
 
-        def project_tokens(f, part, engine):
-            cols = slice(f * P, (f + 1) * P)
+        def project_tokens(f, part, copy):
             lo, hi = TOKEN_CUTS[part]
             sums = banks.tile([P, hi - lo], F32, name=f"bank{TOKEN_BANKS[f][part]}")
-            mx(sums[:], wp_codes[:, cols], wp_scales[:, cols], t_codes[part][:], t_scales[:, lo:hi])
-            (nc.vector.tensor_copy if engine == "vector" else nc.scalar.copy)(out_sb[f][:, lo:hi], sums[:])
+            mx(sums[:], *wp_coded[f], t_codes[:, lo:hi], t_scales[:, lo:hi])
+            copy(out_sb[f][:, lo:hi], sums[:])
 
-        def project_slots(f):
-            cols = slice(f * P, (f + 1) * P)
-            sums = banks.tile([P, C], F32, name=f"bank{3 + f % 2}")
-            mx(sums[:], wp_codes[:, cols], wp_scales[:, cols], c_codes[:], c_scales[:])
-            o_slots = pairs.tile([P, C], F32, name="o_slots")
-            nc.scalar.copy(o_slots[:], sums[:])
-            return o_slots
+        def project_slots(f, copy):
+            sums = banks.tile([P, 2, C], F32, name=f"bank{SLOT_BANKS[f // 2]}")
+            for i in range(2):
+                mx(sums[:, i, :], *wp_coded[f + i], c_codes[:], c_scales[:])
+            both = pairs.tile([P, 2, C], F32, name="o_slots")
+            copy(both[:], sums[:])
+            o_slots[f], o_slots[f + 1] = both[:, 0, :], both[:, 1, :]
 
-        def finish(f, o_slots):
-            nc.vector.tensor_copy(out_sb[f][:].indirect(entries(LAST)), o_slots[:])
+        def finish(f):
+            window = out_sb[f][:].indirect(entries(LAST))
+            if f % 2 == 0:
+                on_vector(window, o_slots[f])
+            else:
+                nc.scalar.activation(window, o_slots[f], COPY)
             nc.sync.dma_start(out[f * P : (f + 1) * P, :], out_sb[f][:])
 
-        quantize_tokens(1, "last_upper")
-        turned = gate_and_turn(LAST)
-        c_grouped = held.tile([P, C, PACK], BF16, name="c_grouped", align_bytes=64)
         c_codes = held.tile([P, C], U32, name="c_codes", align_bytes=64)
         c_scales = held.tile([P, C], U8, name="c_scales", align_bytes=64)
 
-        interleave_wp(0, "scalar", "pass3")
-        interleave_wp(1, "scalar", "before_scatters")
-        interleave_wp(2, "gpsimd", "last_lower")
-        nc.scalar.copy(
-            c_grouped[:].rearrange("p s j -> p (s j)").bitcast(F32).rearrange("p (s u) -> p s u", u=2),
-            turned[:].rearrange("p u s -> p s u"),
-        )
+        interleave_wp(0, "scalar", "wp_first")
+        interleave_wp(2, "scalar", "before_scatters")
+        interleave_wp(1, "vector", "bias_sb3")
         quantize_wp(0)
-        quantize_tokens(0, f"gated_bias{LAST}")
+        c_grouped = turns.tile([P, C, PACK], BF16, name="wp_first", align_bytes=64)
+        on_vector(c_grouped[:], c_planes[:].rearrange("p t s -> p s t"))
+        quantize_wp(2)
         quantize(c_codes[:], c_scales[:], c_grouped[:])
         quantize_wp(1)
-        quantize_wp(2)
-        interleave_wp(3, "gpsimd", "last_lower")
-
-        project_tokens(0, 1, "scalar")
-        project_tokens(0, 0, "scalar")
-        first = project_slots(0)
-        project_tokens(1, 1, "vector")
-        project_tokens(2, 1, "vector")
-        finish(0, first)
+        interleave_wp(3, "gpsimd", "bias_sb3")
+        project_tokens(0, 0, on_scalar)
+        project_tokens(0, 1, on_vector)
+        project_slots(0, on_vector)
+        finish(0)
+        project_tokens(1, 0, on_scalar)
+        project_tokens(1, 1, on_scalar)
+        finish(1)
         quantize_wp(3)
-        for f in range(1, OUT_TILES):
-            project_tokens(f, 0, "scalar")
-            if f == OUT_TILES - 1:
-                project_tokens(f, 1, "scalar")
-            finish(f, project_slots(f))
+        project_tokens(2, 0, on_vector)
+        project_tokens(2, 1, on_vector)
+        project_slots(2, on_vector)
+        finish(2)
+        project_tokens(3, 0, on_scalar)
+        project_tokens(3, 1, on_scalar)
+        finish(3)

@@ -26,17 +26,20 @@ PASSES = K // K_PASS
 SLOTS = E * C
 OUT_TILES = M // P
 RUN = 4
-JOIN = 2 * RUN
+JOIN = T // PACK
+WP_COLS = M // 2
 LAST = E - 1
 LAST_OPENS_WITH = 2
 
+W_ON_SCALAR = 384
+CLOSING_ON_SCALAR = 192
+LAST_ON_SCALAR = (384, 256, 384, 288)
 LOAD_BUFS = 7
 GROUPED_BUFS = 4
 CODE_BUFS = 7
 TOKEN_CUTS = ((0, 512), (512, T))
 
-TOKEN_BANKS = ((0, 1), (2, 3), (4, 1), (5, 6))
-SLOT_BANKS = (4, 0)
+TOKEN_BANKS = ((0, 1), (2, 3), (6, 7), (0, 1))
 
 
 def tile_moe_nxt_lin_bias_kernel(tc, xT, w, b, wp, gate, offs, out):
@@ -57,8 +60,8 @@ def tile_moe_nxt_lin_bias_kernel(tc, xT, w, b, wp, gate, offs, out):
         ident = held.tile([P, P], F32, name="ident")
         gate_rows = held.tile([P, C], F32, name="gate_rows")
         gate_col = held.tile([P, E], F32, name="gate_col")
-        gate_all = held.tile([P, E, C], F32, name="gate_all")
-        bias_sb = [turns.tile([P, E], F32, name=f"bias_sb{t}", align_bytes=64) for t in range(PACK)]
+        gates = held.tile([P, E, C], F32, name="gates")
+        bias_sb = held.tile([P, PACK, E], F32, name="bias_sb")
         x_planes = [held.tile([P, T], U8, name=f"x_planes{i}", align_bytes=64) for i in range(2)]
         s_codes = [held.tile([P, SLOTS], U32, name=f"s_codes{a}", align_bytes=64) for a in range(PASSES)]
         s_planes = [held.tile([P, SLOTS], U8, name=f"s_planes{i}", align_bytes=64) for i in range(2)]
@@ -68,7 +71,7 @@ def tile_moe_nxt_lin_bias_kernel(tc, xT, w, b, wp, gate, offs, out):
 
         X, W, WP = "x", "w", "wp"
         early = [(X, 0), (W, 0), (W, 1), (X, 1), (X, 2), (X, 3), (W, 2), (W, 3), (X, 4)]
-        units = early + [(W, u) for u in range(PASSES - 1, E * PASSES)] + [(WP, 0)]
+        units = early + [(W, u) for u in range(PASSES - 1, E * PASSES)] + [(WP, 0), (WP, 1)]
         paired = range(0, PASSES - 1, 2)
         firsts = [n for n, (kind, i) in enumerate(units) if kind != W or i - 1 not in paired]
         ends = firsts[1:] + [len(units)]
@@ -79,14 +82,12 @@ def tile_moe_nxt_lin_bias_kernel(tc, xT, w, b, wp, gate, offs, out):
             g = count["loaded"]
             size = ends[g] - firsts[g]
             kind, i = units[firsts[g]]
-            tile = loads.tile([P, size, PACK, T if kind == X else N], F32, name="raw")
+            tile = loads.tile([P, size, PACK, {X: T, W: N, WP: WP_COLS}[kind]], F32, name="raw", align_bytes=64)
             if kind == WP:
-                rows = wp.rearrange("(c t i) f -> t c i f", t=PACK, i=RUN)
-                for t in range(PACK):
-                    nc.sync.dma_start(tile[:, 0, t, :], rows[t])
+                rows = wp[:, i * WP_COLS : (i + 1) * WP_COLS]
             else:
                 rows = {X: xT, W: w_rows}[kind][i * K_PASS : (i + size) * K_PASS, :]
-                nc.sync.dma_start(tile[:], rows.rearrange("(a p j) c -> p a j c", a=size, j=PACK))
+            nc.sync.dma_start(tile[:], rows.rearrange("(a p j) c -> p a j c", a=size, j=PACK))
             for a in range(size):
                 raw[kind, i + a] = tile[:, a]
             count["loaded"] += 1
@@ -106,23 +107,13 @@ def tile_moe_nxt_lin_bias_kernel(tc, xT, w, b, wp, gate, offs, out):
             return (lo, hi, grouped_pool.tile([P, hi - lo, PACK], BF16, name="grouped", align_bytes=64))
 
         def interleave(unit, into, lo, hi, engine):
-            dst = into[2][:, lo - into[0] : hi - into[0], :]
             if unit[0] == W:
-                src = raw[unit].rearrange("p j (c t i) -> p t c j i", t=PACK, i=RUN)[:, lo // P : hi // P]
-                dst = dst.rearrange("p (t c i) j -> p t c j i", c=P // RUN, i=RUN)
+                src = raw[unit][:, :, lo:hi].rearrange("p j (m t) -> p m j t", t=PACK)
+                dst = into[2][:].rearrange("p (t m) j -> p m j t", t=PACK)[:, lo // PACK : hi // PACK]
             else:
-                src = raw[unit][:, :, lo:hi].rearrange("p j (t c i) -> p t c j i", c=P // RUN, i=RUN)
-                dst = dst.rearrange("p (t c i) j -> p t c j i", c=P // RUN, i=RUN)
-            if engine == "gpsimd":
-                for t in range((hi - lo) // P):
-                    nc.gpsimd.tensor_scalar(
-                        dst[:, t].rearrange("p c j i -> p c i j"), src[:, t].rearrange("p c j i -> p c i j"),
-                        1.0, 0.0, MULT, ADD,
-                    )
-            elif engine == "vector":
-                on_vector(dst, src)
-            else:
-                on_scalar(dst, src)
+                src = raw[unit][:, :, lo:hi].rearrange("p j (c i) -> p c j i", i=RUN)
+                dst = into[2][:, lo - into[0] : hi - into[0], :].rearrange("p (c i) j -> p c j i", i=RUN)
+            (on_vector if engine == "vector" else on_scalar)(dst, src)
 
         def quantize(codes, scales, grouped):
             nc.vector.quantize_mx(out=codes.bitcast(FP8X4), scales=scales, in_=grouped.rearrange("p c j -> p (c j)"))
@@ -168,10 +159,10 @@ def tile_moe_nxt_lin_bias_kernel(tc, xT, w, b, wp, gate, offs, out):
             quantize_w(u, source)
             multiply(u)
 
-        def take(u, quarters, turn=None, other="vector"):
-            whole = piece(0, N, turn)
-            interleave((W, u), whole, 0, quarters * P, "scalar")
-            interleave((W, u), whole, quarters * P, N, other)
+        def take(u, cut):
+            whole = piece(0, N)
+            interleave((W, u), whole, 0, cut, "scalar")
+            interleave((W, u), whole, cut, N, "vector")
             freed()
             return whole
 
@@ -181,6 +172,7 @@ def tile_moe_nxt_lin_bias_kernel(tc, xT, w, b, wp, gate, offs, out):
         load_next()
         nc.vector.memset(gate_rows[:], 0.0)
         nc.sync.dma_start(gate_rows[0:E, :], gate[0:1, :].rearrange("o (e c) -> (o e) c", c=C))
+        nc.sync.dma_start(bias_sb[:], b.rearrange("(p t) e -> p t e", t=PACK))
         nc.sync.dma_start(offsets[:], offs)
         make_identity(nc, ident[:])
         for plane in x_planes:
@@ -188,9 +180,6 @@ def tile_moe_nxt_lin_bias_kernel(tc, xT, w, b, wp, gate, offs, out):
         for u in range(2):
             nc.vector.memset(c_tokens[u][:], 0.0)
         refill()
-        b_rows = b.rearrange("(c t i) e -> t c i e", t=PACK, i=RUN)
-        for t in range(PACK):
-            nc.sync.dma_start(bias_sb[t][:], b_rows[t])
 
         gate_turned = banks.tile([P, P], F32, name="bank0")
         nc.tensor.transpose(gate_turned[:], gate_rows[:], ident[:])
@@ -198,13 +187,13 @@ def tile_moe_nxt_lin_bias_kernel(tc, xT, w, b, wp, gate, offs, out):
         spread = banks.tile([P, E, C], F32, name="bank1")
         for e in range(E):
             nc.tensor.transpose(spread[:, e, :], gate_col[:, e : e + 1].to_broadcast([P, P]), ident[:])
-        on_scalar(gate_all[:], spread[:])
+        on_scalar(gates[:], spread[:])
 
         def scalar_share(unit):
             kind, i = unit
             if kind == X:
                 return T // 3 if i == 0 else 2 * T // 3
-            return 3 * P
+            return W_ON_SCALAR
 
         pieces, x_codes = {}, {}
         for s in range(len(early) + 2):
@@ -236,7 +225,7 @@ def tile_moe_nxt_lin_bias_kernel(tc, xT, w, b, wp, gate, offs, out):
             multiply(u)
 
         def gated(e, t, dst):
-            nc.vector.scalar_tensor_tensor(dst, acc[e, t][:], bias_sb[t][:, e : e + 1], gate_all[:, e, :], ADD, MULT)
+            nc.vector.scalar_tensor_tensor(dst, acc[e, t][:], bias_sb[:, t, e : e + 1], gates[:, e, :], ADD, MULT)
 
         def gate_into_pairs(e):
             c_pairs = [turns.tile([P, C, 2], BF16, name=f"c_pairs{u}", align_bytes=64) for u in range(2)]
@@ -250,62 +239,41 @@ def tile_moe_nxt_lin_bias_kernel(tc, xT, w, b, wp, gate, offs, out):
 
         for e in range(LAST - 1):
             closing = e * PASSES + PASSES - 1
-            use(closing, take(closing, 3))
+            use(closing, take(closing, W_ON_SCALAR))
             c_pairs = gate_into_pairs(e)
-            use(closing + 1, take(closing + 1, 3))
+            use(closing + 1, take(closing + 1, W_ON_SCALAR))
             scatter_pairs(e, c_pairs)
             for u in range(closing + 2, closing + PASSES):
-                use(u, take(u, 3))
+                use(u, take(u, W_ON_SCALAR))
 
-        def split(u, quarters, scalar_turn, other_turn):
-            lower = piece(0, quarters * P, scalar_turn)
-            upper = piece(quarters * P, N, other_turn)
-            interleave((W, u), lower, 0, quarters * P, "scalar")
-            interleave((W, u), upper, quarters * P, N, "vector")
-            freed()
-            return lower, upper
-
-        def quantize_both(u, parts, turn=None):
-            for part in reversed(parts):
-                quantize_w(u, part, part[0], part[1], turn)
-
-        def close_by_quarters(u, lower_turn, upper_turn):
-            lower = piece(0, N // 2, lower_turn)
-            upper = piece(N // 2, N, upper_turn)
+        def close_by_tiles(u):
+            whole = take(u, CLOSING_ON_SCALAR)
             for t in range(PACK):
-                interleave((W, u), upper if t >= 2 else lower, t * P, (t + 1) * P, "scalar" if t >= 2 else "vector")
-            freed()
-            for t in range(PACK):
-                quantize_w(u, upper if t >= 2 else lower, t * P, (t + 1) * P)
+                quantize_w(u, whole, t * P, (t + 1) * P)
                 multiply(u, [t])
 
         u0, u1, u2, u3, u4 = range(LAST * PASSES, E * PASSES)
-        close_by_quarters(u0 - 1, None, "before_scatters")
+        close_by_tiles(u0 - 1)
         scatter_pairs(LAST - 1, gate_into_pairs(LAST - 1))
-        pass0 = (piece(0, N // 2, "before_scatters"), piece(N // 2, N))
-        interleave((W, u0), pass0[0], 0, N // 2, "gpsimd")
-        interleave((W, u0), pass0[1], N // 2, N, "scalar")
-        freed()
-        c_joined = raw[W, u0].rearrange("p j (c u i) -> p (j c) u i", u=2, i=JOIN)[:, 0 : T // JOIN]
+        pass0 = take(u0, LAST_ON_SCALAR[0])
+        c_joined = raw[W, u0][:, :, 0 : 2 * JOIN]
         for u in range(2):
-            on_scalar(c_joined[:, :, u, :], c_tokens[u][:].rearrange("p (r i) -> p r i", i=JOIN))
-        quantize_both(u0, pass0)
-        pass1 = split(u1, 2, "scalar_a", "vector_a")
-        t_grouped = turns.tile([P, T, PACK], BF16, name="t_grouped", align_bytes=64)
+            on_scalar(c_joined[:, :, u * JOIN : (u + 1) * JOIN], c_tokens[u][:].rearrange("p (r i) -> p r i", i=JOIN))
+        quantize_w(u0, pass0)
+        pass1 = take(u1, LAST_ON_SCALAR[1])
+        t_grouped = pairs.tile([P, T, PACK], BF16, name="x_grouped", align_bytes=64)
         t_words = t_grouped[:].rearrange("p t j -> p (t j)").bitcast(F32)
-        on_vector(t_words.rearrange("p (r i u) -> p r i u", i=JOIN, u=2), c_joined.rearrange("p r u i -> p r i u"))
-        quantize_both(u1, pass1)
+        on_vector(t_words.rearrange("p (r i u) -> p r i u", i=JOIN, u=2), c_joined.rearrange("p r (u i) -> p r i u", u=2))
+        quantize_w(u1, pass1)
         t_codes = pairs.tile([P, T], U32, name="x_codes", align_bytes=64)
         for lo, hi in TOKEN_CUTS:
             quantize(t_codes[:, lo:hi], t_scales[:, lo:hi], t_grouped[:, lo:hi, :])
 
-        quantize_both(u2, split(u2, 3, None, None))
-        multiply(u2)
+        use(u2, take(u2, LAST_ON_SCALAR[2]))
         multiply(u0)
-        quantize_both(u3, split(u3, 2, None, None))
-        multiply(u3)
+        use(u3, take(u3, LAST_ON_SCALAR[3]))
         multiply(u1)
-        close_by_quarters(u4, "vector_a", "scalar_a")
+        close_by_tiles(u4)
         c_planes = turns.tile([P, PACK, C], BF16, name="c_planes", align_bytes=64)
         for t in range(PACK):
             gated(LAST, t, c_planes[:, t, :])
@@ -313,11 +281,12 @@ def tile_moe_nxt_lin_bias_kernel(tc, xT, w, b, wp, gate, offs, out):
         wp_pieces, wp_coded, o_slots = {}, {}, {}
 
         def interleave_wp(f, engine, turn):
-            wp_pieces[f] = piece(f * P, (f + 1) * P, turn)
-            interleave((WP, 0), wp_pieces[f], f * P, (f + 1) * P, engine)
+            i, lo = divmod(f * P, WP_COLS)
+            wp_pieces[f] = piece(lo, lo + P, turn)
+            interleave((WP, i), wp_pieces[f], lo, lo + P, engine)
 
         def quantize_wp(f):
-            codes = turns.tile([P, P], U32, name=("bias_sb2", "c_planes", "wp_codes2", "c_planes")[f], align_bytes=64)
+            codes = held.tile([P, P], U32, name=f"wp_codes{f}", align_bytes=64)
             plane = held.tile([P, P], U8, name=f"wp_plane{f}", align_bytes=64)
             wp_coded[f] = (codes[:], plane[:])
             quantize(codes[:], plane[:], wp_pieces[f][2][:])
@@ -328,17 +297,18 @@ def tile_moe_nxt_lin_bias_kernel(tc, xT, w, b, wp, gate, offs, out):
             mx(sums[:], *wp_coded[f], t_codes[:, lo:hi], t_scales[:, lo:hi])
             copy(out_sb[f][:, lo:hi], sums[:])
 
-        def project_slots(f, copy):
-            sums = banks.tile([P, 2, C], F32, name=f"bank{SLOT_BANKS[f // 2]}")
-            for i in range(2):
-                mx(sums[:, i, :], *wp_coded[f + i], c_codes[:], c_scales[:])
-            both = pairs.tile([P, 2, C], F32, name="o_slots")
-            copy(both[:], sums[:])
-            o_slots[f], o_slots[f + 1] = both[:, 0, :], both[:, 1, :]
+        def project_slots(tiles, bank, copy):
+            sums = banks.tile([P, len(tiles), C], F32, name=f"bank{bank}")
+            for i, f in enumerate(tiles):
+                mx(sums[:, i, :], *wp_coded[f], c_codes[:], c_scales[:])
+            copied = held.tile([P, len(tiles), C], F32, name=f"o_slots{tiles[0]}")
+            copy(copied[:], sums[:])
+            for i, f in enumerate(tiles):
+                o_slots[f] = copied[:, i, :]
 
-        def finish(f):
+        def finish(f, engine):
             window = out_sb[f][:].indirect(entries(LAST))
-            if f % 2 == 0:
+            if engine == "vector":
                 on_vector(window, o_slots[f])
             else:
                 nc.scalar.activation(window, o_slots[f], COPY)
@@ -347,28 +317,22 @@ def tile_moe_nxt_lin_bias_kernel(tc, xT, w, b, wp, gate, offs, out):
         c_codes = held.tile([P, C], U32, name="c_codes", align_bytes=64)
         c_scales = held.tile([P, C], U8, name="c_scales", align_bytes=64)
 
-        interleave_wp(0, "scalar", "wp_first")
-        interleave_wp(2, "scalar", "before_scatters")
-        interleave_wp(1, "vector", "bias_sb3")
-        quantize_wp(0)
-        c_grouped = turns.tile([P, C, PACK], BF16, name="wp_first", align_bytes=64)
+        c_grouped = held.tile([P, C, PACK], BF16, name="c_grouped", align_bytes=64)
+        for f in range(OUT_TILES):
+            interleave_wp(f, "scalar", f"wp_grouped{f}")
         on_vector(c_grouped[:], c_planes[:].rearrange("p t s -> p s t"))
-        quantize_wp(2)
         quantize(c_codes[:], c_scales[:], c_grouped[:])
-        quantize_wp(1)
-        interleave_wp(3, "gpsimd", "bias_sb3")
+        for f in range(OUT_TILES):
+            quantize_wp(f)
         project_tokens(0, 0, on_scalar)
         project_tokens(0, 1, on_vector)
-        project_slots(0, on_vector)
-        finish(0)
+        project_slots([0], 4, on_vector)
+        finish(0, "vector")
         project_tokens(1, 0, on_scalar)
         project_tokens(1, 1, on_scalar)
-        finish(1)
-        quantize_wp(3)
-        project_tokens(2, 0, on_vector)
-        project_tokens(2, 1, on_vector)
-        project_slots(2, on_vector)
-        finish(2)
-        project_tokens(3, 0, on_scalar)
-        project_tokens(3, 1, on_scalar)
-        finish(3)
+        project_slots([1, 2, 3], 5, on_scalar)
+        for f in range(1, OUT_TILES):
+            if f > 1:
+                project_tokens(f, 0, on_scalar)
+                project_tokens(f, 1, on_scalar)
+            finish(f, "vector")

@@ -33,7 +33,8 @@ LAST_OPENS_WITH = 2
 
 W_ON_SCALAR = 384
 CLOSING_ON_SCALAR = 192
-LAST_ON_SCALAR = (384, 256, 384, 288)
+LAST_ON_SCALAR = (384, 256, 448, 272)
+BEFORE_CLOSING_ON_SCALAR = 272
 LOAD_BUFS = 7
 GROUPED_BUFS = 4
 CODE_BUFS = 7
@@ -60,7 +61,7 @@ def tile_moe_nxt_lin_bias_kernel(tc, xT, w, b, wp, gate, offs, out):
         ident = held.tile([P, P], F32, name="ident")
         gate_rows = held.tile([P, C], F32, name="gate_rows")
         gate_col = held.tile([P, E], F32, name="gate_col")
-        gates = held.tile([P, E, C], F32, name="gates")
+        gates = turns.tile([P, E, C], F32, name="gates", align_bytes=64)
         bias_sb = held.tile([P, PACK, E], F32, name="bias_sb")
         x_planes = [held.tile([P, T], U8, name=f"x_planes{i}", align_bytes=64) for i in range(2)]
         s_codes = [held.tile([P, SLOTS], U32, name=f"s_codes{a}", align_bytes=64) for a in range(PASSES)]
@@ -244,7 +245,7 @@ def tile_moe_nxt_lin_bias_kernel(tc, xT, w, b, wp, gate, offs, out):
             use(closing + 1, take(closing + 1, W_ON_SCALAR))
             scatter_pairs(e, c_pairs)
             for u in range(closing + 2, closing + PASSES):
-                use(u, take(u, W_ON_SCALAR))
+                use(u, take(u, BEFORE_CLOSING_ON_SCALAR if u == LAST * PASSES - 2 else W_ON_SCALAR))
 
         def close_by_tiles(u):
             whole = take(u, CLOSING_ON_SCALAR)
@@ -318,9 +319,10 @@ def tile_moe_nxt_lin_bias_kernel(tc, xT, w, b, wp, gate, offs, out):
         c_scales = held.tile([P, C], U8, name="c_scales", align_bytes=64)
 
         c_grouped = held.tile([P, C, PACK], BF16, name="c_grouped", align_bytes=64)
-        for f in range(OUT_TILES):
+        for f in range(OUT_TILES - 1):
             interleave_wp(f, "scalar", f"wp_grouped{f}")
         on_vector(c_grouped[:], c_planes[:].rearrange("p t s -> p s t"))
+        interleave_wp(3, "vector", "gates")
         quantize(c_codes[:], c_scales[:], c_grouped[:])
         for f in range(OUT_TILES):
             quantize_wp(f)
@@ -329,7 +331,7 @@ def tile_moe_nxt_lin_bias_kernel(tc, xT, w, b, wp, gate, offs, out):
         project_slots([0], 4, on_vector)
         finish(0, "vector")
         project_tokens(1, 0, on_scalar)
-        project_tokens(1, 1, on_scalar)
+        project_tokens(1, 1, on_vector)
         project_slots([1, 2, 3], 5, on_scalar)
         for f in range(1, OUT_TILES):
             if f > 1:

@@ -17,7 +17,6 @@ FP8X4 = mybir.dt.float8_e4m3fn_x4
 
 MULT = mybir.AluOpType.mult
 ADD = mybir.AluOpType.add
-COPY = mybir.ActivationFunctionType.Copy
 
 P = 128
 PACK = 4
@@ -26,21 +25,24 @@ PASSES = K // K_PASS
 SLOTS = E * C
 OUT_TILES = M // P
 RUN = 4
-JOIN = T // PACK
-WP_COLS = M // 2
 LAST = E - 1
 LAST_OPENS_WITH = 2
+WP_COLS = M // 2
+JOIN = T // PACK
+TOKEN_CUTS = ((0, 512), (512, T))
 
-W_ON_SCALAR = 384
-CLOSING_ON_SCALAR = 192
-LAST_ON_SCALAR = (384, 256, 448, 272)
-BEFORE_CLOSING_ON_SCALAR = 272
 LOAD_BUFS = 7
 GROUPED_BUFS = 4
 CODE_BUFS = 7
-TOKEN_CUTS = ((0, 512), (512, T))
+
+W_ON_SCALAR = 384
+CLOSING_ON_SCALAR = 192
+BEFORE_CLOSING_ON_SCALAR = 272
+LAST_ON_SCALAR = (384, 256, 384)
 
 TOKEN_BANKS = ((0, 1), (2, 3), (6, 7), (0, 1))
+FIRST_SLOTS_BANK = 4
+OTHER_SLOTS_BANK = 5
 
 
 def tile_moe_nxt_lin_bias_kernel(tc, xT, w, b, wp, gate, offs, out):
@@ -66,7 +68,7 @@ def tile_moe_nxt_lin_bias_kernel(tc, xT, w, b, wp, gate, offs, out):
         x_planes = [held.tile([P, T], U8, name=f"x_planes{i}", align_bytes=64) for i in range(2)]
         s_codes = [held.tile([P, SLOTS], U32, name=f"s_codes{a}", align_bytes=64) for a in range(PASSES)]
         s_planes = [held.tile([P, SLOTS], U8, name=f"s_planes{i}", align_bytes=64) for i in range(2)]
-        c_tokens = [turns.tile([P, T], F32, name=f"c_tokens{u}", align_bytes=64) for u in range(2)]
+        c_tokens = [held.tile([P, T], F32, name=f"c_tokens{u}", align_bytes=64) for u in range(2)]
         t_scales = held.tile([P, T], U8, name="t_scales", align_bytes=64)
         out_sb = [held.tile([P, T], F32, name=f"out_sb{f}") for f in range(OUT_TILES)]
 
@@ -102,29 +104,26 @@ def tile_moe_nxt_lin_bias_kernel(tc, xT, w, b, wp, gate, offs, out):
             count["freed"] += 1
             refill()
 
-        def piece(lo, hi, turn=None):
-            if turn:
-                return (lo, hi, turns.tile([P, hi - lo, PACK], BF16, name=turn, align_bytes=64))
-            return (lo, hi, grouped_pool.tile([P, hi - lo, PACK], BF16, name="grouped", align_bytes=64))
+        def interleave(copy, grouped, rows):
+            copy(grouped.rearrange("p (c i) j -> p c j i", i=RUN), rows.rearrange("p j (c i) -> p c j i", i=RUN))
 
-        def interleave(unit, into, lo, hi, engine):
-            if unit[0] == W:
-                src = raw[unit][:, :, lo:hi].rearrange("p j (m t) -> p m j t", t=PACK)
-                dst = into[2][:].rearrange("p (t m) j -> p m j t", t=PACK)[:, lo // PACK : hi // PACK]
+        def interleave_share(unit, grouped, lo, hi, copy):
+            rows = raw[unit][:, :, lo:hi]
+            if unit[0] == X:
+                interleave(copy, grouped[:, lo:hi, :], rows)
             else:
-                src = raw[unit][:, :, lo:hi].rearrange("p j (c i) -> p c j i", i=RUN)
-                dst = into[2][:, lo - into[0] : hi - into[0], :].rearrange("p (c i) j -> p c j i", i=RUN)
-            (on_vector if engine == "vector" else on_scalar)(dst, src)
+                dealt = grouped[:].rearrange("p (t m) j -> p m j t", t=PACK)[:, lo // PACK : hi // PACK]
+                copy(dealt, rows.rearrange("p j (m t) -> p m j t", t=PACK))
 
         def quantize(codes, scales, grouped):
             nc.vector.quantize_mx(out=codes.bitcast(FP8X4), scales=scales, in_=grouped.rearrange("p c j -> p (c j)"))
 
-        def quantize_w(u, source, lo=0, hi=N, turn=None):
+        def quantize_w(u, grouped, lo=0, hi=N):
             if u not in coded:
-                codes = (turns if turn else code_pool).tile([P, N], U32, name=turn or "w_codes", align_bytes=64)
+                codes = code_pool.tile([P, N], U32, name="w_codes", align_bytes=64)
                 plane = code_pool.tile([P, N], U8, name="w_plane", align_bytes=64)
                 coded[u] = (codes, plane)
-            quantize(coded[u][0][:, lo:hi], coded[u][1][:, lo:hi], source[2][:, lo - source[0] : hi - source[0], :])
+            quantize(coded[u][0][:, lo:hi], coded[u][1][:, lo:hi], grouped[:, lo:hi, :])
 
         def mx(dst, lhs, lhs_scale, rhs, rhs_scale, start=True, stop=True):
             nc.tensor.matmul_mx(
@@ -156,16 +155,16 @@ def tile_moe_nxt_lin_bias_kernel(tc, xT, w, b, wp, gate, offs, out):
                     a == PASSES - 1,
                 )
 
-        def use(u, source):
-            quantize_w(u, source)
+        def use(u, grouped):
+            quantize_w(u, grouped)
             multiply(u)
 
         def take(u, cut):
-            whole = piece(0, N)
-            interleave((W, u), whole, 0, cut, "scalar")
-            interleave((W, u), whole, cut, N, "vector")
+            grouped = grouped_pool.tile([P, N, PACK], BF16, name="w_grouped", align_bytes=64)
+            interleave_share((W, u), grouped, 0, cut, on_scalar)
+            interleave_share((W, u), grouped, cut, N, on_vector)
             freed()
-            return whole
+            return grouped
 
         def entries(e):
             return offsets[:, e * C // 16 : (e + 1) * C // 16]
@@ -200,11 +199,11 @@ def tile_moe_nxt_lin_bias_kernel(tc, xT, w, b, wp, gate, offs, out):
         for s in range(len(early) + 2):
             if s < len(early):
                 if early[s][0] == X:
-                    pieces[s] = (0, T, pairs.tile([P, T, PACK], BF16, name="x_grouped", align_bytes=64))
+                    pieces[s] = pairs.tile([P, T, PACK], BF16, name="x_grouped", align_bytes=64)
                 else:
-                    pieces[s] = piece(0, N)
+                    pieces[s] = grouped_pool.tile([P, N, PACK], BF16, name="w_grouped", align_bytes=64)
                 cut = scalar_share(early[s])
-                interleave(early[s], pieces[s], 0, cut, "scalar")
+                interleave_share(early[s], pieces[s], 0, cut, on_scalar)
             if s >= 2 and early[s - 2][0] == X:
                 a = early[s - 2][1]
                 on_vector(s_codes[a][:], x_codes[a][:].indirect(offsets[:]))
@@ -212,15 +211,15 @@ def tile_moe_nxt_lin_bias_kernel(tc, xT, w, b, wp, gate, offs, out):
                     on_vector(s_planes[a // 4][:], x_planes[a // 4][:].indirect(offsets[:]))
             if 1 <= s <= len(early):
                 kind, i = early[s - 1]
-                grouped = pieces[s - 1][2]
+                grouped = pieces[s - 1]
                 if kind == X:
                     x_codes[i] = pairs.tile([P, T], U32, name="x_codes", align_bytes=64)
                     for lo, hi in TOKEN_CUTS:
                         quantize(x_codes[i][:, lo:hi], x_planes[i // 4][4 * (i % 4) : P, lo:hi], grouped[:, lo:hi, :])
                 else:
-                    quantize_w(i, pieces[s - 1])
+                    quantize_w(i, grouped)
             if s < len(early):
-                interleave(early[s], pieces[s], cut, pieces[s][1], "vector")
+                interleave_share(early[s], pieces[s], cut, T if early[s][0] == X else N, on_vector)
                 freed()
         for u in range(PASSES - 1):
             multiply(u)
@@ -236,7 +235,8 @@ def tile_moe_nxt_lin_bias_kernel(tc, xT, w, b, wp, gate, offs, out):
 
         def scatter_pairs(e, c_pairs):
             for u in range(2):
-                on_vector(c_tokens[u][:].indirect(entries(e)), c_pairs[u][:].rearrange("p s h -> p (s h)").bitcast(F32))
+                words = c_pairs[u][:].rearrange("p s h -> p (s h)").bitcast(F32)
+                on_vector(c_tokens[u][:].indirect(entries(e)), words)
 
         for e in range(LAST - 1):
             closing = e * PASSES + PASSES - 1
@@ -247,16 +247,17 @@ def tile_moe_nxt_lin_bias_kernel(tc, xT, w, b, wp, gate, offs, out):
             for u in range(closing + 2, closing + PASSES):
                 use(u, take(u, BEFORE_CLOSING_ON_SCALAR if u == LAST * PASSES - 2 else W_ON_SCALAR))
 
-        def close_by_tiles(u):
-            whole = take(u, CLOSING_ON_SCALAR)
+        def close_by_quarters(u):
+            grouped = take(u, CLOSING_ON_SCALAR)
             for t in range(PACK):
-                quantize_w(u, whole, t * P, (t + 1) * P)
+                quantize_w(u, grouped, t * P, (t + 1) * P)
                 multiply(u, [t])
 
         u0, u1, u2, u3, u4 = range(LAST * PASSES, E * PASSES)
-        close_by_tiles(u0 - 1)
+        close_by_quarters(u0 - 1)
         scatter_pairs(LAST - 1, gate_into_pairs(LAST - 1))
         pass0 = take(u0, LAST_ON_SCALAR[0])
+
         c_joined = raw[W, u0][:, :, 0 : 2 * JOIN]
         for u in range(2):
             on_scalar(c_joined[:, :, u * JOIN : (u + 1) * JOIN], c_tokens[u][:].rearrange("p (r i) -> p r i", i=JOIN))
@@ -264,33 +265,40 @@ def tile_moe_nxt_lin_bias_kernel(tc, xT, w, b, wp, gate, offs, out):
         pass1 = take(u1, LAST_ON_SCALAR[1])
         t_grouped = pairs.tile([P, T, PACK], BF16, name="x_grouped", align_bytes=64)
         t_words = t_grouped[:].rearrange("p t j -> p (t j)").bitcast(F32)
-        on_vector(t_words.rearrange("p (r i u) -> p r i u", i=JOIN, u=2), c_joined.rearrange("p r (u i) -> p r i u", u=2))
+        on_vector(
+            t_words.rearrange("p (r i u) -> p r i u", i=JOIN, u=2), c_joined.rearrange("p r (u i) -> p r i u", u=2)
+        )
         quantize_w(u1, pass1)
         t_codes = pairs.tile([P, T], U32, name="x_codes", align_bytes=64)
-        for lo, hi in TOKEN_CUTS:
+
+        def quantize_tokens(part):
+            lo, hi = TOKEN_CUTS[part]
             quantize(t_codes[:, lo:hi], t_scales[:, lo:hi], t_grouped[:, lo:hi, :])
 
-        use(u2, take(u2, LAST_ON_SCALAR[2]))
+        quantize_tokens(0)
+        pass2 = take(u2, LAST_ON_SCALAR[2])
+        quantize_tokens(1)
+        use(u2, pass2)
         multiply(u0)
-        use(u3, take(u3, LAST_ON_SCALAR[3]))
+        use(u3, take(u3, BEFORE_CLOSING_ON_SCALAR))
         multiply(u1)
-        close_by_tiles(u4)
-        c_planes = turns.tile([P, PACK, C], BF16, name="c_planes", align_bytes=64)
+        close_by_quarters(u4)
+        c_planes = held.tile([P, PACK, C], BF16, name="c_planes", align_bytes=64)
         for t in range(PACK):
             gated(LAST, t, c_planes[:, t, :])
 
-        wp_pieces, wp_coded, o_slots = {}, {}, {}
+        wp_grouped, wp_coded, o_slots = {}, {}, {}
 
-        def interleave_wp(f, engine, turn):
+        def interleave_wp(f, copy, buffer):
             i, lo = divmod(f * P, WP_COLS)
-            wp_pieces[f] = piece(lo, lo + P, turn)
-            interleave((WP, i), wp_pieces[f], lo, lo + P, engine)
+            wp_grouped[f] = turns.tile([P, P, PACK], BF16, name=buffer, align_bytes=64)
+            interleave(copy, wp_grouped[f][:], raw[WP, i][:, :, lo : lo + P])
 
         def quantize_wp(f):
             codes = held.tile([P, P], U32, name=f"wp_codes{f}", align_bytes=64)
             plane = held.tile([P, P], U8, name=f"wp_plane{f}", align_bytes=64)
             wp_coded[f] = (codes[:], plane[:])
-            quantize(codes[:], plane[:], wp_pieces[f][2][:])
+            quantize(codes[:], plane[:], wp_grouped[f][:])
 
         def project_tokens(f, part, copy):
             lo, hi = TOKEN_CUTS[part]
@@ -307,34 +315,27 @@ def tile_moe_nxt_lin_bias_kernel(tc, xT, w, b, wp, gate, offs, out):
             for i, f in enumerate(tiles):
                 o_slots[f] = copied[:, i, :]
 
-        def finish(f, engine):
-            window = out_sb[f][:].indirect(entries(LAST))
-            if engine == "vector":
-                on_vector(window, o_slots[f])
-            else:
-                nc.scalar.activation(window, o_slots[f], COPY)
+        def finish(f):
+            on_vector(out_sb[f][:].indirect(entries(LAST)), o_slots[f])
             nc.sync.dma_start(out[f * P : (f + 1) * P, :], out_sb[f][:])
 
+        c_grouped = held.tile([P, C, PACK], BF16, name="c_grouped", align_bytes=64)
         c_codes = held.tile([P, C], U32, name="c_codes", align_bytes=64)
         c_scales = held.tile([P, C], U8, name="c_scales", align_bytes=64)
 
-        c_grouped = held.tile([P, C, PACK], BF16, name="c_grouped", align_bytes=64)
         for f in range(OUT_TILES - 1):
-            interleave_wp(f, "scalar", f"wp_grouped{f}")
-        on_vector(c_grouped[:], c_planes[:].rearrange("p t s -> p s t"))
-        interleave_wp(3, "vector", "gates")
+            interleave_wp(f, on_scalar, f"wp_grouped{f}")
+        interleave(on_vector, c_grouped[:], c_planes[:])
+        interleave_wp(OUT_TILES - 1, on_vector, "gates")
         quantize(c_codes[:], c_scales[:], c_grouped[:])
         for f in range(OUT_TILES):
             quantize_wp(f)
-        project_tokens(0, 0, on_scalar)
-        project_tokens(0, 1, on_vector)
-        project_slots([0], 4, on_vector)
-        finish(0, "vector")
-        project_tokens(1, 0, on_scalar)
-        project_tokens(1, 1, on_vector)
-        project_slots([1, 2, 3], 5, on_scalar)
-        for f in range(1, OUT_TILES):
-            if f > 1:
-                project_tokens(f, 0, on_scalar)
-                project_tokens(f, 1, on_scalar)
-            finish(f, "vector")
+
+        for f in range(OUT_TILES):
+            project_tokens(f, 0, on_scalar)
+            project_tokens(f, 1, on_vector if f < 2 else on_scalar)
+            if f == 0:
+                project_slots([0], FIRST_SLOTS_BANK, on_vector)
+            if f == 1:
+                project_slots(range(1, OUT_TILES), OTHER_SLOTS_BANK, on_scalar)
+            finish(f)

@@ -36,7 +36,7 @@ GROUPED_BUFS = 4
 CODE_BUFS = 7
 
 W_ON_SCALAR = 384
-CLOSING_ON_SCALAR = 192
+CLOSING_ON_SCALAR = 96
 BEFORE_CLOSING_ON_SCALAR = 272
 LAST_ON_SCALAR = (384, 256, 384)
 
@@ -63,7 +63,7 @@ def tile_moe_nxt_lin_bias_kernel(tc, xT, w, b, wp, gate, offs, out):
         ident = held.tile([P, P], F32, name="ident")
         gate_rows = held.tile([P, C], F32, name="gate_rows")
         gate_col = held.tile([P, E], F32, name="gate_col")
-        gates = turns.tile([P, E, C], F32, name="gates", align_bytes=64)
+        gates = held.tile([P, E, C], F32, name="gates", align_bytes=64)
         bias_sb = held.tile([P, PACK, E], F32, name="bias_sb")
         x_planes = [held.tile([P, T], U8, name=f"x_planes{i}", align_bytes=64) for i in range(2)]
         s_codes = [held.tile([P, SLOTS], U32, name=f"s_codes{a}", align_bytes=64) for a in range(PASSES)]
@@ -248,7 +248,14 @@ def tile_moe_nxt_lin_bias_kernel(tc, xT, w, b, wp, gate, offs, out):
                 use(u, take(u, BEFORE_CLOSING_ON_SCALAR if u == LAST * PASSES - 2 else W_ON_SCALAR))
 
         def close_by_quarters(u):
-            grouped = take(u, CLOSING_ON_SCALAR)
+            grouped = grouped_pool.tile([P, N, PACK], BF16, name="w_grouped", align_bytes=64)
+            dealt = grouped[:].rearrange("p (t m) j -> p m j t", t=PACK)
+            rows = raw[W, u].rearrange("p j (m t) -> p m j t", t=PACK)
+            lower, upper = slice(0, PACK // 2), slice(PACK // 2, PACK)
+            on_vector(dealt[:, :, :, lower], rows[:, :, :, lower])
+            on_scalar(dealt[:, :CLOSING_ON_SCALAR, :, upper], rows[:, :CLOSING_ON_SCALAR, :, upper])
+            on_vector(dealt[:, CLOSING_ON_SCALAR:, :, upper], rows[:, CLOSING_ON_SCALAR:, :, upper])
+            freed()
             for t in range(PACK):
                 quantize_w(u, grouped, t * P, (t + 1) * P)
                 multiply(u, [t])
@@ -319,21 +326,23 @@ def tile_moe_nxt_lin_bias_kernel(tc, xT, w, b, wp, gate, offs, out):
             on_vector(out_sb[f][:].indirect(entries(LAST)), o_slots[f])
             nc.sync.dma_start(out[f * P : (f + 1) * P, :], out_sb[f][:])
 
-        c_grouped = held.tile([P, C, PACK], BF16, name="c_grouped", align_bytes=64)
+        c_grouped = raw[WP, 0][:, 0, :].bitcast(BF16).rearrange("p (s t) -> p s t", t=PACK)
         c_codes = held.tile([P, C], U32, name="c_codes", align_bytes=64)
         c_scales = held.tile([P, C], U8, name="c_scales", align_bytes=64)
 
         for f in range(OUT_TILES - 1):
             interleave_wp(f, on_scalar, f"wp_grouped{f}")
-        interleave(on_vector, c_grouped[:], c_planes[:])
-        interleave_wp(OUT_TILES - 1, on_vector, "gates")
-        quantize(c_codes[:], c_scales[:], c_grouped[:])
-        for f in range(OUT_TILES):
-            quantize_wp(f)
+        quantize_wp(0)
+        quantize_wp(1)
+        interleave(on_vector, c_grouped, c_planes[:])
+        interleave_wp(OUT_TILES - 1, on_vector, "wp_grouped1")
+        quantize(c_codes[:], c_scales[:], c_grouped)
+        quantize_wp(2)
+        quantize_wp(3)
 
         for f in range(OUT_TILES):
+            project_tokens(f, 1, on_vector if f == 1 else on_scalar)
             project_tokens(f, 0, on_scalar)
-            project_tokens(f, 1, on_vector if f < 2 else on_scalar)
             if f == 0:
                 project_slots([0], FIRST_SLOTS_BANK, on_vector)
             if f == 1:

@@ -37,8 +37,8 @@ CODE_BUFS = 7
 
 W_ON_SCALAR = 384
 CLOSING_ON_SCALAR = 96
-BEFORE_CLOSING_ON_SCALAR = 272
-LAST_ON_SCALAR = (384, 256, 384)
+BEFORE_CLOSING_ON_SCALAR = 256
+LAST_ON_SCALAR = (384, 192, 384)
 
 TOKEN_BANKS = ((0, 1), (2, 3), (6, 7), (0, 1))
 FIRST_SLOTS_BANK = 4
@@ -263,7 +263,18 @@ def tile_moe_nxt_lin_bias_kernel(tc, xT, w, b, wp, gate, offs, out):
         u0, u1, u2, u3, u4 = range(LAST * PASSES, E * PASSES)
         close_by_quarters(u0 - 1)
         scatter_pairs(LAST - 1, gate_into_pairs(LAST - 1))
-        pass0 = take(u0, LAST_ON_SCALAR[0])
+        pass0 = grouped_pool.tile([P, N, PACK], BF16, name="w_grouped", align_bytes=64)
+        cut = LAST_ON_SCALAR[0]
+        interleave_share((W, u0), pass0, 0, cut, on_scalar)
+        nc.gpsimd.tensor_scalar(
+            pass0[:].rearrange("p (t m) j -> p t m j", t=PACK)[:, :, cut // PACK :],
+            raw[W, u0][:, :, cut:].rearrange("p j (m t) -> p t m j", t=PACK),
+            1.0,
+            0.0,
+            MULT,
+            ADD,
+        )
+        freed()
 
         c_joined = raw[W, u0][:, :, 0 : 2 * JOIN]
         for u in range(2):

@@ -38,7 +38,8 @@ CODE_BUFS = 7
 W_ON_SCALAR = 384
 CLOSING_ON_SCALAR = 96
 BEFORE_CLOSING_ON_SCALAR = 256
-LAST_ON_SCALAR = (384, 192, 384)
+LAST_ON_SCALAR = (304, 224, 384)
+ON_GPSIMD = 128
 
 TOKEN_BANKS = ((0, 1), (2, 3), (6, 7), (0, 1))
 FIRST_SLOTS_BANK = 4
@@ -238,6 +239,7 @@ def tile_moe_nxt_lin_bias_kernel(tc, xT, w, b, wp, gate, offs, out):
                 words = c_pairs[u][:].rearrange("p s h -> p (s h)").bitcast(F32)
                 on_vector(c_tokens[u][:].indirect(entries(e)), words)
 
+        before_expert2_closes = LAST * PASSES - 2
         for e in range(LAST - 1):
             closing = e * PASSES + PASSES - 1
             use(closing, take(closing, W_ON_SCALAR))
@@ -245,7 +247,7 @@ def tile_moe_nxt_lin_bias_kernel(tc, xT, w, b, wp, gate, offs, out):
             use(closing + 1, take(closing + 1, W_ON_SCALAR))
             scatter_pairs(e, c_pairs)
             for u in range(closing + 2, closing + PASSES):
-                use(u, take(u, BEFORE_CLOSING_ON_SCALAR if u == LAST * PASSES - 2 else W_ON_SCALAR))
+                use(u, take(u, BEFORE_CLOSING_ON_SCALAR if u == before_expert2_closes else W_ON_SCALAR))
 
         def close_by_quarters(u):
             grouped = grouped_pool.tile([P, N, PACK], BF16, name="w_grouped", align_bytes=64)
@@ -263,12 +265,14 @@ def tile_moe_nxt_lin_bias_kernel(tc, xT, w, b, wp, gate, offs, out):
         u0, u1, u2, u3, u4 = range(LAST * PASSES, E * PASSES)
         close_by_quarters(u0 - 1)
         scatter_pairs(LAST - 1, gate_into_pairs(LAST - 1))
+
         pass0 = grouped_pool.tile([P, N, PACK], BF16, name="w_grouped", align_bytes=64)
-        cut = LAST_ON_SCALAR[0]
-        interleave_share((W, u0), pass0, 0, cut, on_scalar)
+        lo, hi = LAST_ON_SCALAR[0], LAST_ON_SCALAR[0] + ON_GPSIMD
+        interleave_share((W, u0), pass0, 0, lo, on_scalar)
+        interleave_share((W, u0), pass0, hi, N, on_vector)
         nc.gpsimd.tensor_scalar(
-            pass0[:].rearrange("p (t m) j -> p t m j", t=PACK)[:, :, cut // PACK :],
-            raw[W, u0][:, :, cut:].rearrange("p j (m t) -> p t m j", t=PACK),
+            pass0[:].rearrange("p (t m) j -> p t m j", t=PACK)[:, :, lo // PACK : hi // PACK],
+            raw[W, u0][:, :, lo:hi].rearrange("p j (m t) -> p t m j", t=PACK),
             1.0,
             0.0,
             MULT,

from contextlib import ExitStack

import concourse.mybir as mybir
from concourse.masks import make_identity

K, T, E, C, N, M = 2560, 768, 4, 128, 512, 512

FLOPS = 2 * E * C * K * N + 2 * T * N * M

F32 = mybir.dt.float32
BF16 = mybir.dt.bfloat16
U32 = mybir.dt.uint32
I32 = mybir.dt.int32
U16 = mybir.dt.uint16
U8 = mybir.dt.uint8
FP8X4 = mybir.dt.float8_e4m3fn_x4

MULT = mybir.AluOpType.mult
ADD = mybir.AluOpType.add

P = 128
PACK = 4
K_PASS = P * PACK
PASSES = K // K_PASS
SLOTS = E * C
OUT_TILES = M // P
RUN = 4
LAST = E - 1
LAST_OPENS_WITH = 2
WP_COLS = M // 2
JOIN = T // PACK
TOKEN_CUTS = ((0, 512), (512, T))

LOAD_BUFS = 7
GROUPED_BUFS = 4
CODE_BUFS = 7

W_ON_SCALAR = 384
CLOSING_ON_SCALAR = 96
BEFORE_CLOSING_ON_SCALAR = 256
LAST_ON_SCALAR = (304, 224, 384)
ON_GPSIMD = 128

TOKEN_BANKS = ((0, 1), (2, 3), (6, 7), (0, 1))
FIRST_SLOTS_BANK = 4
OTHER_SLOTS_BANK = 5


def tile_moe_nxt_lin_bias_kernel(tc, xT, w, b, wp, gate, offs, out):
    nc = tc.nc
    w_rows = w.rearrange("e k n -> (e k) n")
    on_vector, on_scalar = nc.vector.tensor_copy, nc.scalar.copy

    with ExitStack() as ctx:
        held = ctx.enter_context(tc.tile_pool(name="held", bufs=1))
        loads = ctx.enter_context(tc.tile_pool(name="loads", bufs=LOAD_BUFS))
        pairs = ctx.enter_context(tc.tile_pool(name="pairs", bufs=2))
        grouped_pool = ctx.enter_context(tc.tile_pool(name="grouped_pool", bufs=GROUPED_BUFS))
        code_pool = ctx.enter_context(tc.tile_pool(name="code_pool", bufs=CODE_BUFS))
        turns = ctx.enter_context(tc.tile_pool(name="turns", bufs=1))
        banks = ctx.enter_context(tc.psum_pool(name="banks", bufs=1))

        offsets = held.tile([P, SLOTS // 16], U16, name="offsets")
        ident = held.tile([P, P], F32, name="ident")
        gate_rows = held.tile([P, C], F32, name="gate_rows")
        gate_col = held.tile([P, E], F32, name="gate_col")
        gates = held.tile([P, E, C], F32, name="gates", align_bytes=64)
        bias_sb = held.tile([P, PACK, E], F32, name="bias_sb")
        x_planes = [held.tile([P, T], U8, name=f"x_planes{i}", align_bytes=64) for i in range(2)]
        s_codes = [held.tile([P, SLOTS], U32, name=f"s_codes{a}", align_bytes=64) for a in range(PASSES)]
        s_planes = [held.tile([P, SLOTS], U8, name=f"s_planes{i}", align_bytes=64) for i in range(2)]
        c_tokens = [held.tile([P, T], F32, name=f"c_tokens{u}", align_bytes=64) for u in range(2)]
        t_scales = held.tile([P, T], U8, name="t_scales", align_bytes=64)
        out_sb = [held.tile([P, T], F32, name=f"out_sb{f}") for f in range(OUT_TILES)]

        X, W, WP = "x", "w", "wp"
        early = [(X, 0), (W, 0), (W, 1), (X, 1), (X, 2), (X, 3), (W, 2), (W, 3), (X, 4)]
        units = early + [(W, u) for u in range(PASSES - 1, E * PASSES)] + [(WP, 0), (WP, 1)]
        paired = range(0, PASSES - 1, 2)
        firsts = [n for n, (kind, i) in enumerate(units) if kind != W or i - 1 not in paired]
        ends = firsts[1:] + [len(units)]
        raw, coded, acc = {}, {}, {}
        count = {"loaded": 0, "freed": 0}

        def load_next():
            g = count["loaded"]
            size = ends[g] - firsts[g]
            kind, i = units[firsts[g]]
            tile = loads.tile([P, size, PACK, {X: T, W: N, WP: WP_COLS}[kind]], F32, name="raw", align_bytes=64)
            if kind == WP:
                rows = wp[:, i * WP_COLS : (i + 1) * WP_COLS]
            else:
                rows = {X: xT, W: w_rows}[kind][i * K_PASS : (i + size) * K_PASS, :]
            nc.sync.dma_start(tile[:], rows.rearrange("(a p j) c -> p a j c", a=size, j=PACK))
            for a in range(size):
                raw[kind, i + a] = tile[:, a]
            count["loaded"] += 1

        def refill():
            done = len([n for n in ends if n <= count["freed"]])
            while count["loaded"] < len(ends) and count["loaded"] - done < LOAD_BUFS:
                load_next()

        def freed():
            count["freed"] += 1
            refill()

        def interleave(copy, grouped, rows):
            copy(grouped.rearrange("p (c i) j -> p c j i", i=RUN), rows.rearrange("p j (c i) -> p c j i", i=RUN))

        def interleave_share(unit, grouped, lo, hi, copy):
            rows = raw[unit][:, :, lo:hi]
            if unit[0] == X:
                interleave(copy, grouped[:, lo:hi, :], rows)
            else:
                dealt = grouped[:].rearrange("p (t m) j -> p m j t", t=PACK)[:, lo // PACK : hi // PACK]
                copy(dealt, rows.rearrange("p j (m t) -> p m j t", t=PACK))

        def quantize(codes, scales, grouped):
            nc.vector.quantize_mx(out=codes.bitcast(FP8X4), scales=scales, in_=grouped.rearrange("p c j -> p (c j)"))

        def quantize_w(u, grouped, lo=0, hi=N):
            if u not in coded:
                codes = code_pool.tile([P, N], U32, name="w_codes", align_bytes=64)
                plane = code_pool.tile([P, N], U8, name="w_plane", align_bytes=64)
                coded[u] = (codes, plane)
            quantize(coded[u][0][:, lo:hi], coded[u][1][:, lo:hi], grouped[:, lo:hi, :])

        def mx(dst, lhs, lhs_scale, rhs, rhs_scale, start=True, stop=True):
            nc.tensor.matmul_mx(
                out=dst,
                lhsT=lhs.bitcast(FP8X4),
                lhsT_scale=lhs_scale,
                rhs=rhs.bitcast(FP8X4),
                rhs_scale=rhs_scale,
                start=start,
                stop=stop,
            )

        def multiply(u, quarters=range(PACK)):
            e, a = divmod(u, PASSES)
            opening = LAST_OPENS_WITH if e == LAST else 0
            codes, plane = coded[u]
            slots = slice(e * C, (e + 1) * C)
            for t in quarters:
                if a == opening:
                    acc[e, t] = banks.tile([P, C], F32, name=f"bank{PACK * (e % 2) + t}")
                cols = slice(t * P, (t + 1) * P)
                mx(
                    acc[e, t][:],
                    codes[:, cols],
                    plane[:, cols],
                    s_codes[a][:, slots],
                    s_planes[a // 4][4 * (a % 4) : P, slots],
                    a == opening,
                    a == PASSES - 1,
                )

        def use(u, grouped):
            quantize_w(u, grouped)
            multiply(u)

        def take(u, cut):
            grouped = grouped_pool.tile([P, N, PACK], BF16, name="w_grouped", align_bytes=64)
            interleave_share((W, u), grouped, 0, cut, on_scalar)
            interleave_share((W, u), grouped, cut, N, on_vector)
            freed()
            return grouped

        def entries(e):
            return offsets[:, e * C // 16 : (e + 1) * C // 16]

        load_next()
        nc.vector.memset(gate_rows[:], 0.0)
        nc.sync.dma_start(gate_rows[0:E, :], gate[0:1, :].rearrange("o (e c) -> (o e) c", c=C))
        nc.sync.dma_start(bias_sb[:], b.rearrange("(p t) e -> p t e", t=PACK))
        nc.sync.dma_start(offsets[:], offs)
        make_identity(nc, ident[:])
        for plane in x_planes:
            nc.vector.memset(plane[:].bitcast(I32), 0)
        for u in range(2):
            nc.vector.memset(c_tokens[u][:], 0.0)
        refill()

        gate_turned = banks.tile([P, P], F32, name="bank0")
        nc.tensor.transpose(gate_turned[:], gate_rows[:], ident[:])
        on_scalar(gate_col[:], gate_turned[:, 0:E])
        spread = banks.tile([P, E, C], F32, name="bank1")
        for e in range(E):
            nc.tensor.transpose(spread[:, e, :], gate_col[:, e : e + 1].to_broadcast([P, P]), ident[:])
        on_scalar(gates[:], spread[:])

        def scalar_share(unit):
            kind, i = unit
            if kind == X:
                return T // 3 if i == 0 else 2 * T // 3
            return W_ON_SCALAR

        pieces, x_codes = {}, {}
        for s in range(len(early) + 2):
            if s < len(early):
                if early[s][0] == X:
                    pieces[s] = pairs.tile([P, T, PACK], BF16, name="x_grouped", align_bytes=64)
                else:
                    pieces[s] = grouped_pool.tile([P, N, PACK], BF16, name="w_grouped", align_bytes=64)
                cut = scalar_share(early[s])
                interleave_share(early[s], pieces[s], 0, cut, on_scalar)
            if s >= 2 and early[s - 2][0] == X:
                a = early[s - 2][1]
                on_vector(s_codes[a][:], x_codes[a][:].indirect(offsets[:]))
                if a % 4 == 3 or a == PASSES - 1:
                    on_vector(s_planes[a // 4][:], x_planes[a // 4][:].indirect(offsets[:]))
            if 1 <= s <= len(early):
                kind, i = early[s - 1]
                grouped = pieces[s - 1]
                if kind == X:
                    x_codes[i] = pairs.tile([P, T], U32, name="x_codes", align_bytes=64)
                    for lo, hi in TOKEN_CUTS:
                        quantize(x_codes[i][:, lo:hi], x_planes[i // 4][4 * (i % 4) : P, lo:hi], grouped[:, lo:hi, :])
                else:
                    quantize_w(i, grouped)
            if s < len(early):
                interleave_share(early[s], pieces[s], cut, T if early[s][0] == X else N, on_vector)
                freed()
        for u in range(PASSES - 1):
            multiply(u)

        def gated(e, t, dst):
            nc.vector.scalar_tensor_tensor(dst, acc[e, t][:], bias_sb[:, t, e : e + 1], gates[:, e, :], ADD, MULT)

        def gate_into_pairs(e):
            c_pairs = [turns.tile([P, C, 2], BF16, name=f"c_pairs{u}", align_bytes=64) for u in range(2)]
            for t in range(PACK):
                gated(e, t, c_pairs[t // 2][:, :, t % 2])
            return c_pairs

        def scatter_pairs(e, c_pairs):
            for u in range(2):
                words = c_pairs[u][:].rearrange("p s h -> p (s h)").bitcast(F32)
                on_vector(c_tokens[u][:].indirect(entries(e)), words)

        before_expert2_closes = LAST * PASSES - 2
        for e in range(LAST - 1):
            closing = e * PASSES + PASSES - 1
            use(closing, take(closing, W_ON_SCALAR))
            c_pairs = gate_into_pairs(e)
            use(closing + 1, take(closing + 1, W_ON_SCALAR))
            scatter_pairs(e, c_pairs)
            for u in range(closing + 2, closing + PASSES):
                use(u, take(u, BEFORE_CLOSING_ON_SCALAR if u == before_expert2_closes else W_ON_SCALAR))

        def close_by_quarters(u):
            grouped = grouped_pool.tile([P, N, PACK], BF16, name="w_grouped", align_bytes=64)
            dealt = grouped[:].rearrange("p (t m) j -> p m j t", t=PACK)
            rows = raw[W, u].rearrange("p j (m t) -> p m j t", t=PACK)
            lower, upper = slice(0, PACK // 2), slice(PACK // 2, PACK)
            on_vector(dealt[:, :, :, lower], rows[:, :, :, lower])
            on_scalar(dealt[:, :CLOSING_ON_SCALAR, :, upper], rows[:, :CLOSING_ON_SCALAR, :, upper])
            on_vector(dealt[:, CLOSING_ON_SCALAR:, :, upper], rows[:, CLOSING_ON_SCALAR:, :, upper])
            freed()
            for t in range(PACK):
                quantize_w(u, grouped, t * P, (t + 1) * P)
                multiply(u, [t])

        u0, u1, u2, u3, u4 = range(LAST * PASSES, E * PASSES)
        close_by_quarters(u0 - 1)
        scatter_pairs(LAST - 1, gate_into_pairs(LAST - 1))

        pass0 = grouped_pool.tile([P, N, PACK], BF16, name="w_grouped", align_bytes=64)
        lo, hi = LAST_ON_SCALAR[0], LAST_ON_SCALAR[0] + ON_GPSIMD
        interleave_share((W, u0), pass0, 0, lo, on_scalar)
        interleave_share((W, u0), pass0, hi, N, on_vector)
        nc.gpsimd.tensor_scalar(
            pass0[:].rearrange("p (t m) j -> p t m j", t=PACK)[:, :, lo // PACK : hi // PACK],
            raw[W, u0][:, :, lo:hi].rearrange("p j (m t) -> p t m j", t=PACK),
            1.0,
            0.0,
            MULT,
            ADD,
        )
        freed()

        c_joined = raw[W, u0][:, :, 0 : 2 * JOIN]
        for u in range(2):
            on_scalar(c_joined[:, :, u * JOIN : (u + 1) * JOIN], c_tokens[u][:].rearrange("p (r i) -> p r i", i=JOIN))
        quantize_w(u0, pass0)
        pass1 = take(u1, LAST_ON_SCALAR[1])
        t_grouped = pairs.tile([P, T, PACK], BF16, name="x_grouped", align_bytes=64)
        t_words = t_grouped[:].rearrange("p t j -> p (t j)").bitcast(F32)
        on_vector(
            t_words.rearrange("p (r i u) -> p r i u", i=JOIN, u=2), c_joined.rearrange("p r (u i) -> p r i u", u=2)
        )
        quantize_w(u1, pass1)
        t_codes = pairs.tile([P, T], U32, name="x_codes", align_bytes=64)

        def quantize_tokens(part):
            lo, hi = TOKEN_CUTS[part]
            quantize(t_codes[:, lo:hi], t_scales[:, lo:hi], t_grouped[:, lo:hi, :])

        quantize_tokens(0)
        pass2 = take(u2, LAST_ON_SCALAR[2])
        quantize_tokens(1)
        use(u2, pass2)
        multiply(u0)
        use(u3, take(u3, BEFORE_CLOSING_ON_SCALAR))
        multiply(u1)
        close_by_quarters(u4)
        c_planes = held.tile([P, PACK, C], BF16, name="c_planes", align_bytes=64)
        for t in range(PACK):
            gated(LAST, t, c_planes[:, t, :])

        wp_grouped, wp_coded, o_slots = {}, {}, {}

        def interleave_wp(f, copy, buffer):
            i, lo = divmod(f * P, WP_COLS)
            wp_grouped[f] = turns.tile([P, P, PACK], BF16, name=buffer, align_bytes=64)
            interleave(copy, wp_grouped[f][:], raw[WP, i][:, :, lo : lo + P])

        def quantize_wp(f):
            codes = held.tile([P, P], U32, name=f"wp_codes{f}", align_bytes=64)
            plane = held.tile([P, P], U8, name=f"wp_plane{f}", align_bytes=64)
            wp_coded[f] = (codes[:], plane[:])
            quantize(codes[:], plane[:], wp_grouped[f][:])

        def project_tokens(f, part, copy):
            lo, hi = TOKEN_CUTS[part]
            sums = banks.tile([P, hi - lo], F32, name=f"bank{TOKEN_BANKS[f][part]}")
            mx(sums[:], *wp_coded[f], t_codes[:, lo:hi], t_scales[:, lo:hi])
            copy(out_sb[f][:, lo:hi], sums[:])

        def project_slots(tiles, bank, copy):
            sums = banks.tile([P, len(tiles), C], F32, name=f"bank{bank}")
            for i, f in enumerate(tiles):
                mx(sums[:, i, :], *wp_coded[f], c_codes[:], c_scales[:])
            copied = held.tile([P, len(tiles), C], F32, name=f"o_slots{tiles[0]}")
            copy(copied[:], sums[:])
            for i, f in enumerate(tiles):
                o_slots[f] = copied[:, i, :]

        def finish(f):
            on_vector(out_sb[f][:].indirect(entries(LAST)), o_slots[f])
            nc.sync.dma_start(out[f * P : (f + 1) * P, :], out_sb[f][:])

        c_grouped = raw[WP, 0][:, 0, :].bitcast(BF16).rearrange("p (s t) -> p s t", t=PACK)
        c_codes = held.tile([P, C], U32, name="c_codes", align_bytes=64)
        c_scales = held.tile([P, C], U8, name="c_scales", align_bytes=64)

        for f in range(OUT_TILES - 1):
            interleave_wp(f, on_scalar, f"wp_grouped{f}")
        quantize_wp(0)
        quantize_wp(1)
        interleave(on_vector, c_grouped, c_planes[:])
        interleave_wp(OUT_TILES - 1, on_vector, "wp_grouped1")
        quantize(c_codes[:], c_scales[:], c_grouped)
        quantize_wp(2)
        quantize_wp(3)

        for f in range(OUT_TILES):
            project_tokens(f, 1, on_vector if f == 1 else on_scalar)
            project_tokens(f, 0, on_scalar)
            if f == 0:
                project_slots([0], FIRST_SLOTS_BANK, on_vector)
            if f == 1:
                project_slots(range(1, OUT_TILES), OTHER_SLOTS_BANK, on_scalar)
            finish(f)
